import numpy as np
import ml_dtypes


def mxq(x, axis, fmt="e4m3"):
    dtype, down = {"e4m3": (ml_dtypes.float8_e4m3fn, 7), "e5m2": (ml_dtypes.float8_e5m2, 14)}[fmt]
    v = np.moveaxis(np.asarray(x, np.float32).astype(ml_dtypes.bfloat16).astype(np.float64), axis, -1)
    blocks = v.reshape(v.shape[:-1] + (-1, 32))
    amax = np.abs(blocks).max(-1, keepdims=True)
    byte = np.maximum(np.where(amax > 0, np.frexp(amax)[1] - 1 + 127, 0) - down, 1)
    scale = np.exp2(byte - 127.0)
    codes = (blocks / scale).astype(np.float32).astype(dtype).astype(np.float64)
    return np.moveaxis((codes * scale).reshape(v.shape), -1, axis)


WIDE = False


def mx_kscale(k):
    if not WIDE:
        return np.ones(k)
    levels = np.array([10, -10, 5, -5, 0])
    if k % 512:
        return np.exp2(np.random.permutation(np.resize(levels, k // 32))).repeat(32)
    a = np.empty((k // 512, 16))
    for p in range(k // 512):
        a[p, :8] = np.random.permutation(np.resize(levels, 8))
        for g in range(8):
            far = levels[np.abs(levels - a[p, g]) >= 10]
            a[p, g + 8] = far[np.random.randint(len(far))]
    return np.exp2(a.ravel()).repeat(32)


BF16 = ml_dtypes.bfloat16


def bf(x):
    return np.asarray(x, np.float32).astype(BF16)


def f64(x):
    return np.asarray(x).astype(np.float64)


M, G, P, L, H = 1024, 2048, 1024, 256, 512


def silu(v):
    return v / (1.0 + np.exp(-v))


def draw0():
    s = mx_kscale(G)
    t = mx_kscale(P)
    return {"x": bf(np.random.standard_normal((M, G)) * s),
            "w": bf(np.random.standard_normal((G, P)) / np.sqrt(G) / s[:, None]),
            "e": bf(np.random.standard_normal((G, H)) * s[:, None]),
            "cell_factor": bf(np.exp(0.3 * np.random.standard_normal(M))),
            "pathway_bias": bf(0.4 * np.random.standard_normal(P)),
            "activity_gain": bf((1.0 + 0.1 * np.random.standard_normal(P)) * t),
            "loading_gain": bf((1.0 + 0.1 * np.random.standard_normal(P)) / np.sqrt(P) / t),
            "latent_bias": bf(0.3 * np.random.standard_normal(H)),
            "noise": bf(np.random.standard_normal((M, L)))}


def core(x, w, e, cell_factor, pathway_bias, activity_gain, loading_gain, latent_bias, noise):
    wq = mxq(f64(w), 0, "e4m3")
    u = mxq(f64(x), 1, "e4m3") @ wq
    a = silu(f64(cell_factor)[:, None] * u + f64(pathway_bias)) * f64(activity_gain)
    v = wq.T @ mxq(f64(e), 0, "e4m3")
    v = v * f64(loading_gain)[:, None]
    q = (mxq(a, 1, "e4m3") @ mxq(v, 0, "e4m3")) + f64(latent_bias)
    mu = q[:, :L]
    sd = np.exp(0.5 * np.tanh(q[:, L:]))
    z = mu + sd * f64(noise)
    return mu, sd, z


def e4m3fn_bytes(y):
    return np.clip(np.asarray(y, np.float64), -448.0, 448.0).astype(np.float32).astype(ml_dtypes.float8_e4m3fn).view(np.uint8)


def e4m3fn_values(b):
    return np.asarray(b, np.uint8).view(ml_dtypes.float8_e4m3fn).astype(np.float64)


def setup_inputs():
    d = draw0()
    x0 = np.asarray(d['x']).astype(np.float64)
    s = (np.max(np.abs(x0), axis=(0,), keepdims=True) / 448.0).astype(np.float32)
    out = {}
    for k, v in d.items():
        if k == 'x':
            out['x_bytes'] = e4m3fn_bytes(x0 / s.astype(np.float64))
            out['x_scale'] = s
        else:
            out[k] = v
    return out


def reference(x_bytes, x_scale, w, e, cell_factor, pathway_bias, activity_gain, loading_gain, latent_bias, noise):
    return core(e4m3fn_values(x_bytes) * x_scale.astype(np.float64), w, e, cell_factor, pathway_bias, activity_gain, loading_gain, latent_bias, noise)

@@ -1,0 +1,519 @@
+from contextlib import ExitStack
+
+import concourse.mybir as mybir
+from concourse.masks import make_identity
+
+F32 = mybir.dt.float32
+BF16 = mybir.dt.bfloat16
+U32 = mybir.dt.uint32
+U8 = mybir.dt.uint8
+F8 = mybir.dt.float8_e4m3fn
+FP8X4 = mybir.dt.float8_e4m3fn_x4
+ACT = mybir.ActivationFunctionType
+ALU = mybir.AluOpType
+
+CELLS, GENES, PATHWAYS, LATENT = 1024, 2048, 1024, 256
+H = 2 * LATENT
+P = 128
+PASSES = GENES // 512
+GROUPS = PATHWAYS // 512
+HALVES = CELLS // 512
+TILES = CELLS // P
+TR = 4
+TURNED = {(0, 0), (0, 1)}
+Z_ON_GPSIMD = (0, 1,)
+D_ENGINE = {("w", 0, 0): "V", ("w", 1, 0): "V", ("w", 2, 0): "V", ("w", 3, 0): "S", ("w", 0, 1): "S", ("w", 1, 1): "S", ("w", 2, 1): "S", ("w", 3, 1): "S", ("e", 0, 0): "S", ("e", 1, 0): "S", ("e", 2, 0): "S", ("e", 3, 0): "S"}
+FIRST_LOADS = ("x0", "w00", "w10", "x1", "w20", "w30", "w01", "x2", "w11", "w21",)
+LOADS_AFTER = {0: ("x3", "w31",), 3: ("e2", "e0",), 4: ("e3", "noise",), 5: ("e1",)}
+FLOPS = 2 * CELLS * GENES * PATHWAYS + 2 * GENES * PATHWAYS * H + 2 * CELLS * PATHWAYS * H
+
+ORDER = [
+    ("K", 1),
+    ("D", "w", 0, 0),
+    ("K", 0),
+    ("CF", 0),
+    ("Tp", 0, 1),
+    ("D", "w", 1, 0),
+    ("Tp", 0, 0),
+    ("Tp", 0, 3),
+    ("PP", 0, 1),
+    ("K", 3),
+    ("Tp", 0, 2),
+    ("WQ", "w", 0, 0),
+    ("K", 2),
+    ("PP", 0, 0),
+    ("D", "w", 3, 0),
+    ("Tp", 1, 1),
+    ("PP", 0, 3),
+    ("Tp", 1, 2),
+    ("PP", 1, 2),
+    ("Tp", 1, 0),
+    ("K", 5),
+    ("PP", 1, 0),
+    ("Tp", 1, 3),
+    ("D", "w", 0, 1),
+    ("PP", 1, 3),
+    ("D", "w", 2, 0),
+    ("K", 7),
+    ("PP", 1, 1),
+    ("K", 6),
+    ("WQ", "w", 2, 0),
+    ("K", 4),
+    ("Tp", 3, 1),
+    ("Tp", 3, 2),
+    ("XQ", 1),
+    ("D", "w", 2, 1),
+    ("Tp", 2, 0),
+    ("PP", 3, 1),
+    ("U", 0, 0, 2, 3),
+    ("PP", 0, 2),
+    ("U", 0, 0, 3, 3),
+    ("D", "w", 3, 1),
+    ("PP", 3, 2),
+    ("Tp", 2, 3),
+    ("Tp", 3, 3),
+    ("XQ", 0),
+    ("Tp", 2, 1),
+    ("CS", 0, 0, 3),
+    ("CS", 0, 0, 2),
+    ("PP", 3, 3),
+    ("U", 0, 0, 1, 3),
+    ("D", "w", 1, 1),
+    ("WQ", "w", 2, 1),
+    ("Tp", 3, 0),
+    ("U", 0, 0, 0, 3),
+    ("PP", 2, 0),
+    ("CS", 0, 0, 1),
+    ("WQ", "w", 0, 1),
+    ("Tp", 2, 2),
+    ("D", "e", 2, 0),
+    ("PP", 2, 2),
+    ("U", 1, 0, 0, 0),
+    ("U", 1, 0, 1, 0),
+    ("PP", 2, 1),
+    ("U", 1, 0, 0, 1),
+    ("CS", 0, 0, 0),
+    ("U", 1, 0, 3, 0),
+    ("D", "e", 1, 0),
+    ("C", 1, 0, 0),
+    ("U", 1, 0, 2, 0),
+    ("PP", 2, 3),
+    ("U", 1, 0, 2, 1),
+    ("UT", 0, 0, 2),
+    ("C", 1, 0, 2),
+    ("UT", 0, 0, 0),
+    ("UT", 0, 0, 1),
+    ("SI", 1, 0, 0),
+    ("XQ", 2),
+    ("U", 1, 0, 1, 1),
+    ("SI", 1, 0, 2),
+    ("U", 1, 0, 3, 1),
+    ("D", "e", 0, 0),
+    ("C", 1, 0, 1),
+    ("U", 1, 1, 1, 0),
+    ("PP", 3, 0),
+    ("U", 1, 1, 3, 0),
+    ("U", 1, 1, 2, 0),
+    ("C", 1, 0, 3),
+    ("UT", 0, 0, 3),
+    ("XQ", 3),
+    ("U", 0, 1, 1, 3),
+    ("D", "e", 3, 0),
+    ("WQ", "e", 0, 0),
+    ("U", 1, 1, 1, 1),
+    ("U", 1, 1, 3, 1),
+    ("C", 1, 1, 1),
+    ("U", 1, 1, 2, 1),
+    ("CS", 0, 1, 1),
+    ("C", 1, 1, 3),
+    ("U", 0, 1, 3, 3),
+    ("SI", 1, 0, 3),
+    ("WQ", "e", 2, 0),
+    ("SI", 1, 1, 1),
+    ("U", 1, 1, 0, 0),
+    ("CS", 0, 1, 3),
+    ("U", 1, 1, 0, 1),
+    ("C", 1, 1, 2),
+    ("SI", 1, 1, 3),
+    ("VM", 1, 2),
+    ("C", 1, 1, 0),
+    ("SI", 1, 0, 1),
+    ("VM", 1, 3),
+    ("SI", 1, 1, 2),
+    ("G", 1, 0),
+    ("VS", 1, 2),
+    ("VM", 1, 0),
+    ("SI", 1, 1, 0),
+    ("VS", 1, 3),
+    ("VM", 1, 1),
+    ("G", 1, 1),
+    ("SI", 0, 0, 3),
+    ("VS", 1, 0),
+    ("VM", 0, 1),
+    ("VS", 1, 1),
+    ("VM", 0, 2),
+    ("SI", 0, 0, 2),
+    ("AQ", 1, 0),
+    ("SI", 0, 0, 0),
+    ("VI", 1),
+    ("VM", 0, 0),
+    ("SI", 0, 0, 1),
+    ("VM", 0, 3),
+    ("G", 0, 0),
+    ("VS", 0, 2),
+    ("VS", 0, 0),
+    ("U", 0, 1, 2, 3),
+    ("VS", 0, 1),
+    ("VS", 0, 3),
+    ("U", 0, 1, 0, 3),
+    ("VQ", 1),
+    ("CS", 0, 1, 2),
+    ("VI", 0),
+    ("CS", 0, 1, 0),
+    ("UT", 0, 1, 2),
+    ("AQ", 0, 0),
+    ("UT", 0, 1, 0),
+    ("SI", 0, 1, 2),
+    ("VQ", 0),
+    ("UT", 0, 1, 3),
+    ("UT", 0, 1, 1),
+    ("SI", 0, 1, 0),
+    ("AQ", 1, 1),
+    ("Q", 0),
+    ("SI", 0, 1, 1),
+    ("Q", 1),
+    ("SI", 0, 1, 3),
+    ("QB", 0),
+    ("Q", 2),
+    ("QB", 1),
+    ("Q", 3),
+    ("G", 0, 1),
+    ("TH", 0),
+    ("QB", 2),
+    ("AQ", 0, 1),
+    ("QB", 3),
+    ("Z", 0),
+    ("Q", 4),
+    ("Q", 6),
+    ("TH", 1),
+    ("QB", 4),
+    ("Q", 5),
+    ("QB", 6),
+    ("Q", 7),
+    ("QB", 5),
+    ("Z", 1),
+    ("QB", 7),
+    ("TH", 2),
+    ("TH", 3),
+    ("Z", 2),
+    ("Z", 3),
+]
+
+
+def tile_pathway_latent_encoder_f5_kernel(
+    tc, x_bytes, x_scale, w, e, cell_factor, pathway_bias, activity_gain, loading_gain, latent_bias, noise, mu_out, sd_out, z_out
+):
+    nc = tc.nc
+    with ExitStack() as ctx:
+        keep = ctx.enter_context(tc.tile_pool(name="keep", bufs=1))
+        xin = ctx.enter_context(tc.tile_pool(name="xin", bufs=3))
+        xwp = ctx.enter_context(tc.tile_pool(name="xwp", bufs=2))
+        xgp = ctx.enter_context(tc.tile_pool(name="xgp", bufs=2))
+        yp = ctx.enter_context(tc.tile_pool(name="yp", bufs=2))
+        uyp = ctx.enter_context(tc.tile_pool(name="uyp", bufs=1))
+        pairs = ctx.enter_context(tc.tile_pool(name="pairs", bufs=2))
+        grp = ctx.enter_context(tc.tile_pool(name="grp", bufs=3))
+        vlp = ctx.enter_context(tc.tile_pool(name="vlp", bufs=1))
+        outs = ctx.enter_context(tc.tile_pool(name="outs", bufs=3))
+        qbp = ctx.enter_context(tc.tile_pool(name="qbp", bufs=4))
+        rawp = ctx.enter_context(tc.tile_pool(name="rawp", bufs=8))
+        ps_tr = ctx.enter_context(tc.psum_pool(name="ps_tr", bufs=TR))
+        ps_mx = ctx.enter_context(tc.psum_pool(name="ps_mx", bufs=8 - TR))
+        ctx.enter_context(tc.manual_schedule())
+
+        x_raw = {}
+        raws = {}
+        x_rows = x_bytes.rearrange("(p i) k -> p i k", i=TILES)
+
+        def load(what):
+            kind = what[0]
+            if kind == "x":
+                pr = int(what[1])
+                x_raw[pr] = xin.tile([P, 2, GENES], U8, name="x_raw")
+                nc.sync.dma_start(out=x_raw[pr][:], in_=x_rows[:, 2 * pr : 2 * pr + 2, :])
+            elif kind == "w":
+                g, jg = int(what[1]), int(what[2])
+                raws["w", g, jg] = rawp.tile([P, 4, 512], BF16, name="raw")
+                nc.sync.dma_start(
+                    out=raws["w", g, jg][:], in_=w[g * 512 : (g + 1) * 512, jg * 512 : (jg + 1) * 512].rearrange("(p j) n -> p j n", j=4)
+                )
+            elif kind == "e":
+                g = int(what[1])
+                raws["e", g, 0] = rawp.tile([P, 4, H], BF16, name="raw")
+                nc.sync.dma_start(out=raws["e", g, 0][:], in_=e[g * 512 : (g + 1) * 512, :].rearrange("(p j) n -> p j n", j=4))
+            else:
+                nc.sync.dma_start(out=noise_t[:], in_=noise.rearrange("(p i) l -> p i l", i=TILES))
+
+        warm = keep.tile([P, 1], F32, name="warm")
+        nc.gpsimd.memset(warm[:], 0.0)
+        ident_bf = keep.tile([P, P], BF16, name="ident_bf")
+        make_identity(nc, ident_bf[:])
+        ident = keep.tile([P, P], F32, name="ident")
+        make_identity(nc, ident[:])
+
+        xs_t = keep.tile([P, PASSES, 4], F32, name="xs_t")
+        cf_c = keep.tile([P, TILES], BF16, name="cf_c")
+        lb_c = keep.tile([P, 4], BF16, name="lb_c")
+        pb_t = keep.tile([P, GROUPS, 4], BF16, name="pb_t")
+        ag_t = keep.tile([P, GROUPS, 4], BF16, name="ag_t")
+        lg_t = keep.tile([P, GROUPS, 4], BF16, name="lg_t")
+        cf_f = keep.tile([P, TILES], F32, name="cf_f")
+        lg_f = keep.tile([P, GROUPS, 4], F32, name="lg_f")
+        lb_b = keep.tile([P, H], F32, name="lb_b")
+        cf_b = keep.tile([P, CELLS], F32, name="cf_b")
+        noise_t = keep.tile([P, TILES, LATENT], BF16, name="noise_t")
+        nc.scalar.dma_start(out=xs_t[:], in_=x_scale.rearrange("o (g p t) -> p (o g) t", p=P, t=4))
+        nc.scalar.dma_start(out=cf_c[:], in_=cell_factor.rearrange("(p i) -> p i", i=TILES))
+        nc.scalar.dma_start(out=lb_c[:], in_=latent_bias.rearrange("(n c) -> n c", c=4))
+        nc.scalar.dma_start(out=pb_t[:], in_=pathway_bias.rearrange("(g p t) -> p g t", p=P, t=4))
+        nc.scalar.dma_start(out=ag_t[:], in_=activity_gain.rearrange("(g p t) -> p g t", p=P, t=4))
+        nc.scalar.dma_start(out=lg_t[:], in_=loading_gain.rearrange("(g p t) -> p g t", p=P, t=4))
+        nc.scalar.activation(out=warm[:], in_=warm[:], func=ACT.Silu)
+        for what in FIRST_LOADS:
+            load(what)
+        nc.gpsimd.tensor_copy(out=cf_f[:], in_=cf_c[:])
+        nc.gpsimd.tensor_copy(out=lg_f[:], in_=lg_t[:])
+
+        xc = [keep.tile([P, PASSES, 256], U32, name=f"xc{pr}", align_bytes=64) for pr in range(4)]
+        xs = [keep.tile([P, PASSES, 256], U8, name=f"xs{pr}", align_bytes=64) for pr in range(4)]
+        wc = {}
+        ws = {}
+        for gp in range(2):
+            for k, jg in (("w", 0), ("w", 1), ("e", 0)):
+                wc[k, gp, jg] = keep.tile([P, 2, 512], U32, name=f"{k}c{gp}{jg}", align_bytes=64)
+                ws[k, gp, jg] = keep.tile([P, 2, 512], U8, name=f"{k}s{gp}{jg}", align_bytes=64)
+
+        def codes(k, g, jg, cols):
+            return wc[k, g // 2, jg][:, g % 2, cols].bitcast(FP8X4)
+
+        def plane(k, g, jg, cols):
+            return ws[k, g // 2, jg][:, g % 2, cols]
+
+        ac = [[keep.tile([P, 512], U32, name=f"ac{jg}{h}", align_bytes=64) for h in range(HALVES)] for jg in range(GROUPS)]
+        asc = [[keep.tile([P, 512], U8, name=f"asc{jg}{h}", align_bytes=64) for h in range(HALVES)] for jg in range(GROUPS)]
+        vc = [keep.tile([P, H], U32, name=f"vc{jg}", align_bytes=64) for jg in range(GROUPS)]
+        vsc = [keep.tile([P, H], U8, name=f"vsc{jg}", align_bytes=64) for jg in range(GROUPS)]
+
+        T = {}
+
+        def get(pool, tag, key, shape, dt, **kw):
+            if key not in T:
+                T[key] = pool.tile(shape, dt, name=tag, **kw)
+            return T[key]
+
+        def CF(_):
+            for h in range(HALVES):
+                bank = get(ps_tr, "tr", ("cf", h), [P, 512], F32)
+                for i in range(4):
+                    nc.tensor.matmul(
+                        bank[:, i * P : (i + 1) * P],
+                        lhsT=cf_c[:, 4 * h + i : 4 * h + i + 1].to_broadcast([P, P]),
+                        rhs=ident_bf[:],
+                        start=True,
+                        stop=True,
+                    )
+                nc.scalar.copy(out=cf_b[:, h * 512 : (h + 1) * 512], in_=bank[:])
+            bank = get(ps_tr, "tr", ("lb",), [P, 512], F32)
+            for c in range(4):
+                nc.tensor.matmul(
+                    bank[:, c * P : (c + 1) * P], lhsT=lb_c[:, c : c + 1].to_broadcast([P, P]), rhs=ident_bf[:], start=True, stop=True
+                )
+            nc.scalar.copy(out=lb_b[:].rearrange("p (n c) -> p n c", c=4), in_=bank[:].rearrange("p (c n) -> p n c", c=4))
+
+        def K(i):
+            pr, i2 = divmod(i, 2)
+            xw = get(xwp, "xw", ("xw", pr), [P, 2, GENES], BF16)
+            nc.scalar.copy(out=xw[:, i2, :], in_=x_raw[pr][:, i2, :].bitcast(F8))
+            for what in LOADS_AFTER.get(i, ()):
+                load(what)
+
+        def Tp(pr, g):
+            bank = get(ps_tr, "tr", ("x", pr, g), [P, 512], F32)
+            for i2 in range(2):
+                words = T["xw", pr][:, i2, :].bitcast(F32)
+                for u in range(2):
+                    nc.tensor.transpose(
+                        bank[:, u * 256 + i2 * P : u * 256 + (i2 + 1) * P], words[:, 256 * g + u : 256 * (g + 1) : 2], ident[:]
+                    )
+
+        def PP(pr, g):
+            xg = get(xgp, "xg", ("xg", pr), [P, PASSES, 1024], BF16, align_bytes=64)
+            nc.vector.tensor_tensor(
+                out=xg[:, g, :].rearrange("p (m u e) -> p m u e", u=2, e=2),
+                in0=T["x", pr, g][:].bitcast(BF16).rearrange("p (u m e) -> p m u e", u=2, e=2),
+                in1=xs_t[:, g, :].rearrange("p (u e) -> p u e", e=2).unsqueeze(1).to_broadcast([P, 256, 2, 2]),
+                op=ALU.mult,
+            )
+
+        def XQ(pr):
+            nc.vector.quantize_mx(
+                out=xc[pr][:].rearrange("p g m -> p (g m)").bitcast(FP8X4),
+                scales=xs[pr][:].rearrange("p g m -> p (g m)"),
+                in_=T["xg", pr][:].rearrange("p g c -> p (g c)"),
+            )
+
+        def D(k, g, jg):
+            u = (k, g, jg)
+            both = get(pairs, "pair", ("pair", k, g // 2, jg), [P, 2, 2048], BF16, align_bytes=64)
+            dst = both[:, g % 2, :]
+            if k == "w":
+                o = dst.rearrange("p (t m j) -> p m j t", t=4, j=4)
+                i = raws[u][:].rearrange("p j (m t) -> p m j t", t=4)
+            else:
+                o = dst.rearrange("p (c i j) -> p c j i", i=4, j=4)
+                i = raws[u][:].rearrange("p j (c i) -> p c j i", i=4)
+            if D_ENGINE[u] == "V":
+                nc.vector.tensor_copy(out=o, in_=i)
+            else:
+                nc.scalar.copy(out=o, in_=i)
+
+        def WQ(k, g, jg):
+            u = (k, g // 2, jg)
+            nc.vector.quantize_mx(
+                out=wc[u][:].rearrange("p g c -> p (g c)").bitcast(FP8X4),
+                scales=ws[u][:].rearrange("p g c -> p (g c)"),
+                in_=T["pair", k, g // 2, jg][:].rearrange("p g c -> p (g c)"),
+            )
+
+        def U(jg, h, t, k):
+            if (jg, h) in TURNED:
+                turned_u(jg, h, t)
+                return
+            col = slice(t * P, (t + 1) * P)
+            bank = get(ps_mx, "mx", ("u", jg, h, t), [P, 512], F32)
+            for g in range(PASSES):
+                nc.tensor.matmul_mx(
+                    out=bank[:, k * 256 : (k + 1) * 256],
+                    lhsT=codes("w", g, jg, col),
+                    lhsT_scale=plane("w", g, jg, col),
+                    rhs=xc[2 * h + k][:, g, :].bitcast(FP8X4),
+                    rhs_scale=xs[2 * h + k][:, g, :],
+                    start=(g == 0),
+                    stop=(g == PASSES - 1),
+                )
+
+        def turned_u(jg, h, k):
+            pr, i2 = divmod(4 * h + k, 2)
+            cells = slice(i2 * P, (i2 + 1) * P)
+            bank = get(ps_mx, "mx", ("u", jg, h, k), [P, 512], F32)
+            for g in range(PASSES):
+                nc.tensor.matmul_mx(
+                    out=bank[:],
+                    lhsT=xc[pr][:, g, cells].bitcast(FP8X4),
+                    lhsT_scale=xs[pr][:, g, cells],
+                    rhs=codes("w", g, jg, slice(0, 512)),
+                    rhs_scale=plane("w", g, jg, slice(0, 512)),
+                    start=(g == 0),
+                    stop=(g == PASSES - 1),
+                )
+
+        def CS(jg, h, k):
+            uy = get(uyp, "uy", ("uy", jg, h), [P, 4, 512], F32)
+            i = 4 * h + k
+            nc.scalar.activation(out=uy[:, k, :], in_=T["u", jg, h, k][:], func=ACT.Copy, scale=cf_f[:, i : i + 1])
+
+        def UT(jg, h, t):
+            bank = get(ps_tr, "tr", ("y", jg, h, t), [P, 512], F32)
+            for k in range(4):
+                nc.tensor.transpose(bank[:, k * P : (k + 1) * P], T["uy", jg, h][:, k, t * P : (t + 1) * P], ident[:])
+            T["ut", jg, h, t] = bank
+
+        def C(jg, h, t):
+            y = get(yp, "y", ("y", jg, h), [P, 4, 512], F32)
+            nc.vector.tensor_tensor(out=y[:, t, :], in0=T["u", jg, h, t][:], in1=cf_b[:, h * 512 : (h + 1) * 512], op=ALU.mult)
+
+        def SI(jg, h, t):
+            y = get(yp, "y", ("y", jg, h), [P, 4, 512], F32)
+            nc.scalar.activation(out=y[:, t, :], in_=T["ut", jg, h, t][:] if (jg, h) in TURNED else y[:, t, :], func=ACT.Silu, bias=pb_t[:, jg, t : t + 1])
+
+        def G(jg, h):
+            dst = get(grp, "gr", ("gr", ("a", jg, h)), [P, 2048], BF16, align_bytes=64)
+            nc.vector.tensor_tensor(
+                out=dst[:].rearrange("p (c i t) -> p c t i", i=4, t=4),
+                in0=T["y", jg, h][:].rearrange("p t (c i) -> p c t i", i=4),
+                in1=ag_t[:, jg, :].unsqueeze(1).unsqueeze(3).to_broadcast([P, P, 4, 4]),
+                op=ALU.mult,
+            )
+
+        def AQ(jg, h):
+            nc.vector.quantize_mx(out=ac[jg][h][:].bitcast(FP8X4), scales=asc[jg][h][:], in_=T["gr", ("a", jg, h)][:])
+
+        def VM(jg, t):
+            col = slice(t * P, (t + 1) * P)
+            bank = get(ps_mx, "mx", ("v", jg, t), [P, 512], F32)
+            for g in range(PASSES):
+                nc.tensor.matmul_mx(
+                    out=bank[:],
+                    lhsT=codes("w", g, jg, col),
+                    lhsT_scale=plane("w", g, jg, col),
+                    rhs=codes("e", g, 0, slice(0, 512)),
+                    rhs_scale=plane("e", g, 0, slice(0, 512)),
+                    start=(g == 0),
+                    stop=(g == PASSES - 1),
+                )
+
+        def VS(jg, t):
+            vl = get(vlp, "vl", ("vl", jg), [P, 4, 512], BF16)
+            nc.scalar.activation(out=vl[:, t, :], in_=T["v", jg, t][:], func=ACT.Copy, scale=lg_f[:, jg, t : t + 1])
+
+        def VI(jg):
+            dst = get(grp, "gr", ("gr", ("v", jg)), [P, 2048], BF16, align_bytes=64)
+            nc.vector.tensor_copy(out=dst[:].rearrange("p (c i t) -> p c t i", i=4, t=4), in_=T["vl", jg][:].rearrange("p t (c i) -> p c t i", i=4))
+
+        def VQ(jg):
+            nc.vector.quantize_mx(out=vc[jg][:].bitcast(FP8X4), scales=vsc[jg][:], in_=T["gr", ("v", jg)][:])
+
+        def Q(i):
+            h, k = divmod(i, 4)
+            cells = slice(k * P, (k + 1) * P)
+            bank = get(ps_mx, "mx", ("q", i), [P, 512], F32)
+            for jg in range(GROUPS):
+                nc.tensor.matmul_mx(
+                    out=bank[:],
+                    lhsT=ac[jg][h][:, cells].bitcast(FP8X4),
+                    lhsT_scale=asc[jg][h][:, cells],
+                    rhs=vc[jg][:].bitcast(FP8X4),
+                    rhs_scale=vsc[jg][:],
+                    start=(jg == 0),
+                    stop=(jg == GROUPS - 1),
+                )
+
+        mu_rows = mu_out.rearrange("(p i) l -> p i l", i=TILES)
+        sd_rows = sd_out.rearrange("(p i) l -> p i l", i=TILES)
+        z_rows = z_out.rearrange("(p i) l -> p i l", i=TILES)
+
+        def QB(i):
+            pr, i2 = divmod(i, 2)
+            qb = get(qbp, "qb", ("qb", pr), [P, 2, H], F32)
+            nc.vector.tensor_tensor(out=qb[:, i2, :], in0=T["q", i][:], in1=lb_b[:], op=ALU.add)
+
+        def TH(pr):
+            qb = T["qb", pr]
+            rows = slice(2 * pr, 2 * pr + 2)
+            nc.sync.dma_start(out=mu_rows[:, rows, :], in_=qb[:, :, 0:LATENT])
+            sd = get(outs, "sd", ("sd", pr), [P, 2, LATENT], F32)
+            nc.scalar.activation(out=sd[:], in_=qb[:, :, LATENT:H], func=ACT.Tanh)
+            nc.scalar.activation(out=sd[:], in_=sd[:], func=ACT.Exp, scale=0.5)
+            nc.sync.dma_start(out=sd_rows[:, rows, :], in_=sd[:])
+
+        def Z(pr):
+            rows = slice(2 * pr, 2 * pr + 2)
+            z = get(outs, "z", ("z", pr), [P, 2, LATENT], F32)
+            eng = nc.gpsimd if pr in Z_ON_GPSIMD else nc.vector
+            eng.tensor_tensor(out=z[:], in0=T["sd", pr][:], in1=noise_t[:, rows, :], op=ALU.mult)
+            eng.tensor_tensor(out=z[:], in0=z[:], in1=T["qb", pr][:, :, 0:LATENT], op=ALU.add)
+            nc.sync.dma_start(out=z_rows[:, rows, :], in_=z[:])
+
+        steps = dict(C=C, CF=CF, K=K, Tp=Tp, PP=PP, XQ=XQ, D=D, WQ=WQ, U=U, SI=SI, G=G, AQ=AQ, CS=CS, UT=UT, VM=VM, VS=VS, VI=VI, VQ=VQ, Q=Q, QB=QB, TH=TH, Z=Z)
+        for step in ORDER:
+            steps[step[0]](*step[1:])

@@ -17,197 +17,12 @@ H = 2 * LATENT
 P = 128
 PASSES = GENES // 512
 GROUPS = PATHWAYS // 512
-HALVES = CELLS // 512
 TILES = CELLS // P
-TR = 4
-TURNED = {(0, 0), (0, 1)}
-Z_ON_GPSIMD = (0, 1,)
-D_ENGINE = {("w", 0, 0): "V", ("w", 1, 0): "V", ("w", 2, 0): "V", ("w", 3, 0): "S", ("w", 0, 1): "S", ("w", 1, 1): "S", ("w", 2, 1): "S", ("w", 3, 1): "S", ("e", 0, 0): "S", ("e", 1, 0): "S", ("e", 2, 0): "S", ("e", 3, 0): "S"}
-FIRST_LOADS = ("x0", "w00", "w10", "x1", "w20", "w30", "w01", "x2", "w11", "w21",)
-LOADS_AFTER = {0: ("x3", "w31",), 3: ("e2", "e0",), 4: ("e3", "noise",), 5: ("e1",)}
+PAIRS = TILES // 2
 FLOPS = 2 * CELLS * GENES * PATHWAYS + 2 * GENES * PATHWAYS * H + 2 * CELLS * PATHWAYS * H
-
-ORDER = [
-    ("K", 1),
-    ("D", "w", 0, 0),
-    ("K", 0),
-    ("CF", 0),
-    ("Tp", 0, 1),
-    ("D", "w", 1, 0),
-    ("Tp", 0, 0),
-    ("Tp", 0, 3),
-    ("PP", 0, 1),
-    ("K", 3),
-    ("Tp", 0, 2),
-    ("WQ", "w", 0, 0),
-    ("K", 2),
-    ("PP", 0, 0),
-    ("D", "w", 3, 0),
-    ("Tp", 1, 1),
-    ("PP", 0, 3),
-    ("Tp", 1, 2),
-    ("PP", 1, 2),
-    ("Tp", 1, 0),
-    ("K", 5),
-    ("PP", 1, 0),
-    ("Tp", 1, 3),
-    ("D", "w", 0, 1),
-    ("PP", 1, 3),
-    ("D", "w", 2, 0),
-    ("K", 7),
-    ("PP", 1, 1),
-    ("K", 6),
-    ("WQ", "w", 2, 0),
-    ("K", 4),
-    ("Tp", 3, 1),
-    ("Tp", 3, 2),
-    ("XQ", 1),
-    ("D", "w", 2, 1),
-    ("Tp", 2, 0),
-    ("PP", 3, 1),
-    ("U", 0, 0, 2, 3),
-    ("PP", 0, 2),
-    ("U", 0, 0, 3, 3),
-    ("D", "w", 3, 1),
-    ("PP", 3, 2),
-    ("Tp", 2, 3),
-    ("Tp", 3, 3),
-    ("XQ", 0),
-    ("Tp", 2, 1),
-    ("CS", 0, 0, 3),
-    ("CS", 0, 0, 2),
-    ("PP", 3, 3),
-    ("U", 0, 0, 1, 3),
-    ("D", "w", 1, 1),
-    ("WQ", "w", 2, 1),
-    ("Tp", 3, 0),
-    ("U", 0, 0, 0, 3),
-    ("PP", 2, 0),
-    ("CS", 0, 0, 1),
-    ("WQ", "w", 0, 1),
-    ("Tp", 2, 2),
-    ("D", "e", 2, 0),
-    ("PP", 2, 2),
-    ("U", 1, 0, 0, 0),
-    ("U", 1, 0, 1, 0),
-    ("PP", 2, 1),
-    ("U", 1, 0, 0, 1),
-    ("CS", 0, 0, 0),
-    ("U", 1, 0, 3, 0),
-    ("D", "e", 1, 0),
-    ("C", 1, 0, 0),
-    ("U", 1, 0, 2, 0),
-    ("PP", 2, 3),
-    ("U", 1, 0, 2, 1),
-    ("UT", 0, 0, 2),
-    ("C", 1, 0, 2),
-    ("UT", 0, 0, 0),
-    ("UT", 0, 0, 1),
-    ("SI", 1, 0, 0),
-    ("XQ", 2),
-    ("U", 1, 0, 1, 1),
-    ("SI", 1, 0, 2),
-    ("U", 1, 0, 3, 1),
-    ("D", "e", 0, 0),
-    ("C", 1, 0, 1),
-    ("U", 1, 1, 1, 0),
-    ("PP", 3, 0),
-    ("U", 1, 1, 3, 0),
-    ("U", 1, 1, 2, 0),
-    ("C", 1, 0, 3),
-    ("UT", 0, 0, 3),
-    ("XQ", 3),
-    ("U", 0, 1, 1, 3),
-    ("D", "e", 3, 0),
-    ("WQ", "e", 0, 0),
-    ("U", 1, 1, 1, 1),
-    ("U", 1, 1, 3, 1),
-    ("C", 1, 1, 1),
-    ("U", 1, 1, 2, 1),
-    ("CS", 0, 1, 1),
-    ("C", 1, 1, 3),
-    ("U", 0, 1, 3, 3),
-    ("SI", 1, 0, 3),
-    ("WQ", "e", 2, 0),
-    ("SI", 1, 1, 1),
-    ("U", 1, 1, 0, 0),
-    ("CS", 0, 1, 3),
-    ("U", 1, 1, 0, 1),
-    ("C", 1, 1, 2),
-    ("SI", 1, 1, 3),
-    ("VM", 1, 2),
-    ("C", 1, 1, 0),
-    ("SI", 1, 0, 1),
-    ("VM", 1, 3),
-    ("SI", 1, 1, 2),
-    ("G", 1, 0),
-    ("VS", 1, 2),
-    ("VM", 1, 0),
-    ("SI", 1, 1, 0),
-    ("VS", 1, 3),
-    ("VM", 1, 1),
-    ("G", 1, 1),
-    ("SI", 0, 0, 3),
-    ("VS", 1, 0),
-    ("VM", 0, 1),
-    ("VS", 1, 1),
-    ("VM", 0, 2),
-    ("SI", 0, 0, 2),
-    ("AQ", 1, 0),
-    ("SI", 0, 0, 0),
-    ("VI", 1),
-    ("VM", 0, 0),
-    ("SI", 0, 0, 1),
-    ("VM", 0, 3),
-    ("G", 0, 0),
-    ("VS", 0, 2),
-    ("VS", 0, 0),
-    ("U", 0, 1, 2, 3),
-    ("VS", 0, 1),
-    ("VS", 0, 3),
-    ("U", 0, 1, 0, 3),
-    ("VQ", 1),
-    ("CS", 0, 1, 2),
-    ("VI", 0),
-    ("CS", 0, 1, 0),
-    ("UT", 0, 1, 2),
-    ("AQ", 0, 0),
-    ("UT", 0, 1, 0),
-    ("SI", 0, 1, 2),
-    ("VQ", 0),
-    ("UT", 0, 1, 3),
-    ("UT", 0, 1, 1),
-    ("SI", 0, 1, 0),
-    ("AQ", 1, 1),
-    ("Q", 0),
-    ("SI", 0, 1, 1),
-    ("Q", 1),
-    ("SI", 0, 1, 3),
-    ("QB", 0),
-    ("Q", 2),
-    ("QB", 1),
-    ("Q", 3),
-    ("G", 0, 1),
-    ("TH", 0),
-    ("QB", 2),
-    ("AQ", 0, 1),
-    ("QB", 3),
-    ("Z", 0),
-    ("Q", 4),
-    ("Q", 6),
-    ("TH", 1),
-    ("QB", 4),
-    ("Q", 5),
-    ("QB", 6),
-    ("Q", 7),
-    ("QB", 5),
-    ("Z", 1),
-    ("QB", 7),
-    ("TH", 2),
-    ("TH", 3),
-    ("Z", 2),
-    ("Z", 3),
-]
+RAW_BUFS = 6
+TR_BANKS = 4
+TURNED = {(pr, 1) for pr in range(PAIRS)}
 
 
 def tile_pathway_latent_encoder_f5_kernel(
@@ -216,304 +31,326 @@ def tile_pathway_latent_encoder_f5_kernel(
     nc = tc.nc
     with ExitStack() as ctx:
         keep = ctx.enter_context(tc.tile_pool(name="keep", bufs=1))
-        xin = ctx.enter_context(tc.tile_pool(name="xin", bufs=3))
-        xwp = ctx.enter_context(tc.tile_pool(name="xwp", bufs=2))
-        xgp = ctx.enter_context(tc.tile_pool(name="xgp", bufs=2))
-        yp = ctx.enter_context(tc.tile_pool(name="yp", bufs=2))
-        uyp = ctx.enter_context(tc.tile_pool(name="uyp", bufs=1))
-        pairs = ctx.enter_context(tc.tile_pool(name="pairs", bufs=2))
-        grp = ctx.enter_context(tc.tile_pool(name="grp", bufs=3))
-        vlp = ctx.enter_context(tc.tile_pool(name="vlp", bufs=1))
-        outs = ctx.enter_context(tc.tile_pool(name="outs", bufs=3))
-        qbp = ctx.enter_context(tc.tile_pool(name="qbp", bufs=4))
-        rawp = ctx.enter_context(tc.tile_pool(name="rawp", bufs=8))
-        ps_tr = ctx.enter_context(tc.psum_pool(name="ps_tr", bufs=TR))
-        ps_mx = ctx.enter_context(tc.psum_pool(name="ps_mx", bufs=8 - TR))
+        pools = {1: keep}
+        for n in (2, 3, 4, RAW_BUFS):
+            pools[n] = ctx.enter_context(tc.tile_pool(name=f"ring{n}", bufs=n))
+        ps_tr = ctx.enter_context(tc.psum_pool(name="ps_tr", bufs=TR_BANKS))
+        ps_mx = ctx.enter_context(tc.psum_pool(name="ps_mx", bufs=8 - TR_BANKS))
         ctx.enter_context(tc.manual_schedule())
 
-        x_raw = {}
-        raws = {}
-        x_rows = x_bytes.rearrange("(p i) k -> p i k", i=TILES)
+        GROUPED = {"S": 4, "V": 2, "G": 1, "H": 1}
+        T = {}
+        taken = {}
 
-        def load(what):
-            kind = what[0]
-            if kind == "x":
-                pr = int(what[1])
-                x_raw[pr] = xin.tile([P, 2, GENES], U8, name="x_raw")
-                nc.sync.dma_start(out=x_raw[pr][:], in_=x_rows[:, 2 * pr : 2 * pr + 2, :])
-            elif kind == "w":
-                g, jg = int(what[1]), int(what[2])
-                raws["w", g, jg] = rawp.tile([P, 4, 512], BF16, name="raw")
-                nc.sync.dma_start(
-                    out=raws["w", g, jg][:], in_=w[g * 512 : (g + 1) * 512, jg * 512 : (jg + 1) * 512].rearrange("(p j) n -> p j n", j=4)
-                )
-            elif kind == "e":
-                g = int(what[1])
-                raws["e", g, 0] = rawp.tile([P, 4, H], BF16, name="raw")
-                nc.sync.dma_start(out=raws["e", g, 0][:], in_=e[g * 512 : (g + 1) * 512, :].rearrange("(p j) n -> p j n", j=4))
-            else:
-                nc.sync.dma_start(out=noise_t[:], in_=noise.rearrange("(p i) l -> p i l", i=TILES))
+        def get(bufs, tag, key, shape, dt, **kw):
+            if key not in T:
+                pool = ps_tr if tag == "tr" else ps_mx if tag == "mx" else pools[bufs]
+                earlier = taken.setdefault(tag, [])
+                if len(earlier) >= bufs:
+                    for step in users(earlier[-bufs]):
+                        emit(step)
+                earlier.append(key)
+                T[key] = pool.tile(shape, dt, name=tag, **kw)
+            return T[key]
 
-        warm = keep.tile([P, 1], F32, name="warm")
-        nc.gpsimd.memset(warm[:], 0.0)
-        ident_bf = keep.tile([P, P], BF16, name="ident_bf")
-        make_identity(nc, ident_bf[:])
+        def rows(ap):
+            return ap.rearrange("(p i) c -> p i c", i=TILES)
+
         ident = keep.tile([P, P], F32, name="ident")
         make_identity(nc, ident[:])
+        ident_bf = keep.tile([P, P], BF16, name="ident_bf")
+        make_identity(nc, ident_bf[:])
 
         xs_t = keep.tile([P, PASSES, 4], F32, name="xs_t")
         cf_c = keep.tile([P, TILES], BF16, name="cf_c")
-        lb_c = keep.tile([P, 4], BF16, name="lb_c")
         pb_t = keep.tile([P, GROUPS, 4], BF16, name="pb_t")
         ag_t = keep.tile([P, GROUPS, 4], BF16, name="ag_t")
         lg_t = keep.tile([P, GROUPS, 4], BF16, name="lg_t")
         cf_f = keep.tile([P, TILES], F32, name="cf_f")
         lg_f = keep.tile([P, GROUPS, 4], F32, name="lg_f")
-        lb_b = keep.tile([P, H], F32, name="lb_b")
-        cf_b = keep.tile([P, CELLS], F32, name="cf_b")
+        lb_b = keep.tile([P, H], BF16, name="lb_b")
+        cf_b = keep.tile([P, CELLS], BF16, name="cf_b")
         noise_t = keep.tile([P, TILES, LATENT], BF16, name="noise_t")
-        nc.scalar.dma_start(out=xs_t[:], in_=x_scale.rearrange("o (g p t) -> p (o g) t", p=P, t=4))
-        nc.scalar.dma_start(out=cf_c[:], in_=cell_factor.rearrange("(p i) -> p i", i=TILES))
-        nc.scalar.dma_start(out=lb_c[:], in_=latent_bias.rearrange("(n c) -> n c", c=4))
-        nc.scalar.dma_start(out=pb_t[:], in_=pathway_bias.rearrange("(g p t) -> p g t", p=P, t=4))
-        nc.scalar.dma_start(out=ag_t[:], in_=activity_gain.rearrange("(g p t) -> p g t", p=P, t=4))
-        nc.scalar.dma_start(out=lg_t[:], in_=loading_gain.rearrange("(g p t) -> p g t", p=P, t=4))
-        nc.scalar.activation(out=warm[:], in_=warm[:], func=ACT.Silu)
-        for what in FIRST_LOADS:
-            load(what)
-        nc.gpsimd.tensor_copy(out=cf_f[:], in_=cf_c[:])
-        nc.gpsimd.tensor_copy(out=lg_f[:], in_=lg_t[:])
 
-        xc = [keep.tile([P, PASSES, 256], U32, name=f"xc{pr}", align_bytes=64) for pr in range(4)]
-        xs = [keep.tile([P, PASSES, 256], U8, name=f"xs{pr}", align_bytes=64) for pr in range(4)]
-        wc = {}
-        ws = {}
-        for gp in range(2):
-            for k, jg in (("w", 0), ("w", 1), ("e", 0)):
-                wc[k, gp, jg] = keep.tile([P, 2, 512], U32, name=f"{k}c{gp}{jg}", align_bytes=64)
-                ws[k, gp, jg] = keep.tile([P, 2, 512], U8, name=f"{k}s{gp}{jg}", align_bytes=64)
+        def by_slot(vec):
+            return vec.rearrange("(g p t) -> p g t", p=P, t=4)
 
-        def codes(k, g, jg, cols):
-            return wc[k, g // 2, jg][:, g % 2, cols].bitcast(FP8X4)
+        def load_x(i):
+            raw = get(4, "x_raw", ("x_raw", i), [P, GENES], U8)
+            nc.sync.dma_start(out=raw[:], in_=rows(x_bytes)[:, i, :])
 
-        def plane(k, g, jg, cols):
-            return ws[k, g // 2, jg][:, g % 2, cols]
+        def load_unit(k, g):
+            src = e if k == "e" else w[:, k * 512 : (k + 1) * 512]
+            raw = get(RAW_BUFS, "raw", ("raw", k, g), [P, 4, 512], BF16)
+            nc.sync.dma_start(out=raw[:], in_=src[g * 512 : (g + 1) * 512, :].rearrange("(p j) n -> p j n", j=4))
 
-        ac = [[keep.tile([P, 512], U32, name=f"ac{jg}{h}", align_bytes=64) for h in range(HALVES)] for jg in range(GROUPS)]
-        asc = [[keep.tile([P, 512], U8, name=f"asc{jg}{h}", align_bytes=64) for h in range(HALVES)] for jg in range(GROUPS)]
-        vc = [keep.tile([P, H], U32, name=f"vc{jg}", align_bytes=64) for jg in range(GROUPS)]
-        vsc = [keep.tile([P, H], U8, name=f"vsc{jg}", align_bytes=64) for jg in range(GROUPS)]
+        def load_xs():
+            nc.sync.dma_start(out=xs_t[:], in_=by_slot(x_scale.rearrange("o k -> (o k)")))
 
-        T = {}
+        def load_cf():
+            nc.sync.dma_start(out=cf_c[:], in_=cell_factor.rearrange("(p i) -> p i", i=TILES))
 
-        def get(pool, tag, key, shape, dt, **kw):
-            if key not in T:
-                T[key] = pool.tile(shape, dt, name=tag, **kw)
-            return T[key]
+        def load_small():
+            nc.sync.dma_start(out=pb_t[:], in_=by_slot(pathway_bias))
+            nc.sync.dma_start(out=ag_t[:], in_=by_slot(activity_gain))
+            nc.sync.dma_start(out=lg_t[:], in_=by_slot(loading_gain))
 
-        def CF(_):
-            for h in range(HALVES):
-                bank = get(ps_tr, "tr", ("cf", h), [P, 512], F32)
-                for i in range(4):
-                    nc.tensor.matmul(
-                        bank[:, i * P : (i + 1) * P],
-                        lhsT=cf_c[:, 4 * h + i : 4 * h + i + 1].to_broadcast([P, P]),
-                        rhs=ident_bf[:],
-                        start=True,
-                        stop=True,
-                    )
-                nc.scalar.copy(out=cf_b[:, h * 512 : (h + 1) * 512], in_=bank[:])
-            bank = get(ps_tr, "tr", ("lb",), [P, 512], F32)
-            for c in range(4):
-                nc.tensor.matmul(
-                    bank[:, c * P : (c + 1) * P], lhsT=lb_c[:, c : c + 1].to_broadcast([P, P]), rhs=ident_bf[:], start=True, stop=True
-                )
-            nc.scalar.copy(out=lb_b[:].rearrange("p (n c) -> p n c", c=4), in_=bank[:].rearrange("p (c n) -> p n c", c=4))
+        def load_late():
+            nc.sync.dma_start(out=lb_b[:], in_=latent_bias.partition_broadcast(P))
+            nc.sync.dma_start(out=noise_t[:], in_=rows(noise))
+
+        def CF():
+            bank = get(TR_BANKS, "tr", ("cf",), [P, CELLS], BF16)
+            for i in range(TILES):
+                nc.tensor.transpose(bank[:, i * P : (i + 1) * P], cf_c[:, i : i + 1].to_broadcast([P, P]), ident_bf[:])
+
+        def CC():
+            nc.scalar.copy(out=cf_b[:], in_=T["cf",][:])
+            nc.scalar.copy(out=cf_f[:], in_=cf_c[:])
+
+        def LC():
+            nc.scalar.copy(out=lg_f[:], in_=lg_t[:])
 
         def K(i):
-            pr, i2 = divmod(i, 2)
-            xw = get(xwp, "xw", ("xw", pr), [P, 2, GENES], BF16)
-            nc.scalar.copy(out=xw[:, i2, :], in_=x_raw[pr][:, i2, :].bitcast(F8))
-            for what in LOADS_AFTER.get(i, ()):
-                load(what)
+            xw = get(3, "xw", ("xw", i), [P, GENES], BF16)
+            nc.scalar.copy(out=xw[:], in_=T["x_raw", i][:].bitcast(F8))
 
-        def Tp(pr, g):
-            bank = get(ps_tr, "tr", ("x", pr, g), [P, 512], F32)
+        def XT(pr, g):
+            bank = get(TR_BANKS, "tr", ("xt", pr, g), [P, 512], F32)
             for i2 in range(2):
-                words = T["xw", pr][:, i2, :].bitcast(F32)
+                words = T["xw", 2 * pr + i2][:].bitcast(F32)
                 for u in range(2):
                     nc.tensor.transpose(
                         bank[:, u * 256 + i2 * P : u * 256 + (i2 + 1) * P], words[:, 256 * g + u : 256 * (g + 1) : 2], ident[:]
                     )
 
         def PP(pr, g):
-            xg = get(xgp, "xg", ("xg", pr), [P, PASSES, 1024], BF16, align_bytes=64)
+            xg = get(3, "xg", ("xg", pr, g // 2), [P, 2, 1024], BF16, align_bytes=64)
             nc.vector.tensor_tensor(
-                out=xg[:, g, :].rearrange("p (m u e) -> p m u e", u=2, e=2),
-                in0=T["x", pr, g][:].bitcast(BF16).rearrange("p (u m e) -> p m u e", u=2, e=2),
+                out=xg[:, g % 2, :].rearrange("p (m u e) -> p m u e", u=2, e=2),
+                in0=T["xt", pr, g][:].bitcast(BF16).rearrange("p (u m e) -> p m u e", u=2, e=2),
                 in1=xs_t[:, g, :].rearrange("p (u e) -> p u e", e=2).unsqueeze(1).to_broadcast([P, 256, 2, 2]),
                 op=ALU.mult,
             )
 
-        def XQ(pr):
-            nc.vector.quantize_mx(
-                out=xc[pr][:].rearrange("p g m -> p (g m)").bitcast(FP8X4),
-                scales=xs[pr][:].rearrange("p g m -> p (g m)"),
-                in_=T["xg", pr][:].rearrange("p g c -> p (g c)"),
+        def quantize(name, key, src, width):
+            c = get(1, name + "_c", ("codes",) + key, [P, width], U32, align_bytes=64)
+            s = get(1, name + "_s", ("scales",) + key, [P, width], U8, align_bytes=64)
+            nc.vector.quantize_mx(out=c[:].bitcast(FP8X4), scales=s[:], in_=src)
+
+        def mx(out, left, left_cols, right, right_cols, start, stop):
+            nc.tensor.matmul_mx(
+                out=out,
+                lhsT=T[("codes",) + left][:, left_cols].bitcast(FP8X4),
+                lhsT_scale=T[("scales",) + left][:, left_cols],
+                rhs=T[("codes",) + right][:, right_cols].bitcast(FP8X4),
+                rhs_scale=T[("scales",) + right][:, right_cols],
+                start=start,
+                stop=stop,
             )
 
-        def D(k, g, jg):
-            u = (k, g, jg)
-            both = get(pairs, "pair", ("pair", k, g // 2, jg), [P, 2, 2048], BF16, align_bytes=64)
-            dst = both[:, g % 2, :]
-            if k == "w":
-                o = dst.rearrange("p (t m j) -> p m j t", t=4, j=4)
-                i = raws[u][:].rearrange("p j (m t) -> p m j t", t=4)
+        def XQ(pr, a):
+            quantize(f"x{pr}{a}", ("x", pr, a), T["xg", pr, a][:].rearrange("p g c -> p (g c)"), 512)
+
+        def D(k, g, eng):
+            dst = get(GROUPED[eng], "grouped_" + eng, ("grouped", k, g), [P, 2048], BF16, align_bytes=64)
+            raw = T["raw", k, g]
+            if k == "e":
+                o = dst[:].rearrange("p (c i j) -> p c j i", i=4, j=4)
+                i = raw[:].rearrange("p j (c i) -> p c j i", i=4)
             else:
-                o = dst.rearrange("p (c i j) -> p c j i", i=4, j=4)
-                i = raws[u][:].rearrange("p j (c i) -> p c j i", i=4)
-            if D_ENGINE[u] == "V":
+                o = dst[:].rearrange("p (t m j) -> p m j t", t=4, j=4)
+                i = raw[:].rearrange("p j (m t) -> p m j t", t=4)
+            if eng == "V":
                 nc.vector.tensor_copy(out=o, in_=i)
-            else:
+            elif eng == "S":
                 nc.scalar.copy(out=o, in_=i)
+            else:
+                if k == "e":
+                    o = dst[:].rearrange("p (c j) -> p c j", j=4)
+                    i = raw[:].rearrange("p j c -> p c j")
+                else:
+                    o = dst[:].rearrange("p (t m j) -> p m t j", t=4, j=4)
+                    i = raw[:].rearrange("p j (m t) -> p m t j", t=4)
+                nc.gpsimd.tensor_scalar(out=o, in0=i, scalar1=1.0, scalar2=0.0, op0=ALU.mult, op1=ALU.add)
 
-        def WQ(k, g, jg):
-            u = (k, g // 2, jg)
-            nc.vector.quantize_mx(
-                out=wc[u][:].rearrange("p g c -> p (g c)").bitcast(FP8X4),
-                scales=ws[u][:].rearrange("p g c -> p (g c)"),
-                in_=T["pair", k, g // 2, jg][:].rearrange("p g c -> p (g c)"),
-            )
+        def WQ(k, g):
+            quantize(f"w{k}{g}", ("w", k, g), T["grouped", k, g][:], 512)
 
-        def U(jg, h, t, k):
-            if (jg, h) in TURNED:
-                turned_u(jg, h, t)
-                return
-            col = slice(t * P, (t + 1) * P)
-            bank = get(ps_mx, "mx", ("u", jg, h, t), [P, 512], F32)
-            for g in range(PASSES):
-                nc.tensor.matmul_mx(
-                    out=bank[:, k * 256 : (k + 1) * 256],
-                    lhsT=codes("w", g, jg, col),
-                    lhsT_scale=plane("w", g, jg, col),
-                    rhs=xc[2 * h + k][:, g, :].bitcast(FP8X4),
-                    rhs_scale=xs[2 * h + k][:, g, :],
-                    start=(g == 0),
-                    stop=(g == PASSES - 1),
-                )
+        def x_cols(g, first, count):
+            return slice((g % 2) * 256 + first, (g % 2) * 256 + first + count)
 
-        def turned_u(jg, h, k):
-            pr, i2 = divmod(4 * h + k, 2)
-            cells = slice(i2 * P, (i2 + 1) * P)
-            bank = get(ps_mx, "mx", ("u", jg, h, k), [P, 512], F32)
-            for g in range(PASSES):
-                nc.tensor.matmul_mx(
-                    out=bank[:],
-                    lhsT=xc[pr][:, g, cells].bitcast(FP8X4),
-                    lhsT_scale=xs[pr][:, g, cells],
-                    rhs=codes("w", g, jg, slice(0, 512)),
-                    rhs_scale=plane("w", g, jg, slice(0, 512)),
-                    start=(g == 0),
-                    stop=(g == PASSES - 1),
-                )
+        def US(pr, jg, b):
+            bank = get(8 - TR_BANKS, "mx", ("us", pr, jg, b), [P, 512], F32)
+            for tt in range(2):
+                t = 2 * b + tt
+                for g in range(PASSES):
+                    mx(bank[:, tt * 256 : (tt + 1) * 256], ("w", jg, g), slice(t * P, (t + 1) * P), ("x", pr, g // 2), x_cols(g, 0, 256), g == 0, g == PASSES - 1)
 
-        def CS(jg, h, k):
-            uy = get(uyp, "uy", ("uy", jg, h), [P, 4, 512], F32)
-            i = 4 * h + k
-            nc.scalar.activation(out=uy[:, k, :], in_=T["u", jg, h, k][:], func=ACT.Copy, scale=cf_f[:, i : i + 1])
-
-        def UT(jg, h, t):
-            bank = get(ps_tr, "tr", ("y", jg, h, t), [P, 512], F32)
-            for k in range(4):
-                nc.tensor.transpose(bank[:, k * P : (k + 1) * P], T["uy", jg, h][:, k, t * P : (t + 1) * P], ident[:])
-            T["ut", jg, h, t] = bank
-
-        def C(jg, h, t):
-            y = get(yp, "y", ("y", jg, h), [P, 4, 512], F32)
-            nc.vector.tensor_tensor(out=y[:, t, :], in0=T["u", jg, h, t][:], in1=cf_b[:, h * 512 : (h + 1) * 512], op=ALU.mult)
-
-        def SI(jg, h, t):
-            y = get(yp, "y", ("y", jg, h), [P, 4, 512], F32)
-            nc.scalar.activation(out=y[:, t, :], in_=T["ut", jg, h, t][:] if (jg, h) in TURNED else y[:, t, :], func=ACT.Silu, bias=pb_t[:, jg, t : t + 1])
-
-        def G(jg, h):
-            dst = get(grp, "gr", ("gr", ("a", jg, h)), [P, 2048], BF16, align_bytes=64)
+        def C(pr, jg, b):
+            y = get(RAW_BUFS, "y", ("y", pr, jg), [P, 4, 256], F32)
             nc.vector.tensor_tensor(
-                out=dst[:].rearrange("p (c i t) -> p c t i", i=4, t=4),
-                in0=T["y", jg, h][:].rearrange("p t (c i) -> p c t i", i=4),
-                in1=ag_t[:, jg, :].unsqueeze(1).unsqueeze(3).to_broadcast([P, P, 4, 4]),
+                out=y[:, 2 * b : 2 * b + 2, :],
+                in0=T["us", pr, jg, b][:].rearrange("p (t m) -> p t m", t=2),
+                in1=cf_b[:, pr * 256 : (pr + 1) * 256].unsqueeze(1).to_broadcast([P, 2, 256]),
                 op=ALU.mult,
             )
 
-        def AQ(jg, h):
-            nc.vector.quantize_mx(out=ac[jg][h][:].bitcast(FP8X4), scales=asc[jg][h][:], in_=T["gr", ("a", jg, h)][:])
+        def UC(pr, jg, i2):
+            bank = get(8 - TR_BANKS, "mx", ("uc", pr, jg, i2), [P, 512], F32)
+            for g in range(PASSES):
+                mx(bank[:], ("x", pr, g // 2), x_cols(g, i2 * P, P), ("w", jg, g), slice(0, 512), g == 0, g == PASSES - 1)
+
+        def CS(pr, jg, i2):
+            uy = get(4, "uy", ("uy", pr, jg), [P, 2, 512], F32)
+            i = 2 * pr + i2
+            nc.scalar.activation(out=uy[:, i2, :], in_=T["uc", pr, jg, i2][:], func=ACT.Copy, scale=cf_f[:, i : i + 1])
+
+        def UT(pr, jg, b):
+            bank = get(TR_BANKS, "tr", ("ut", pr, jg, b), [P, 512], F32)
+            for tt in range(2):
+                t = 2 * b + tt
+                for i2 in range(2):
+                    nc.tensor.transpose(bank[:, tt * 256 + i2 * P : tt * 256 + (i2 + 1) * P], T["uy", pr, jg][:, i2, t * P : (t + 1) * P], ident[:])
+
+        def SI(pr, jg, b):
+            y = get(RAW_BUFS, "y", ("y", pr, jg), [P, 4, 256], F32)
+            for tt in range(2):
+                t = 2 * b + tt
+                src = T["ut", pr, jg, b][:, tt * 256 : (tt + 1) * 256] if ("ut", pr, jg, b) in T else y[:, t, :]
+                nc.scalar.activation(out=y[:, t, :], in_=src, func=ACT.Silu, bias=pb_t[:, jg, t : t + 1])
+
+        def G(pr, jg):
+            dst = get(3, "ag", ("ag", pr, jg), [P, 1024], BF16, align_bytes=64)
+            nc.vector.tensor_tensor(
+                out=dst[:].rearrange("p (c i t) -> p c t i", i=4, t=4),
+                in0=T["y", pr, jg][:].rearrange("p t (c i) -> p c t i", i=4),
+                in1=ag_t[:, jg, :].unsqueeze(1).unsqueeze(3).to_broadcast([P, 64, 4, 4]),
+                op=ALU.mult,
+            )
+
+        def AQ(pr, jg):
+            quantize(f"a{pr}{jg}", ("a", pr, jg), T["ag", pr, jg][:], 256)
 
         def VM(jg, t):
-            col = slice(t * P, (t + 1) * P)
-            bank = get(ps_mx, "mx", ("v", jg, t), [P, 512], F32)
+            bank = get(8 - TR_BANKS, "mx", ("v", jg, t), [P, 512], F32)
             for g in range(PASSES):
-                nc.tensor.matmul_mx(
-                    out=bank[:],
-                    lhsT=codes("w", g, jg, col),
-                    lhsT_scale=plane("w", g, jg, col),
-                    rhs=codes("e", g, 0, slice(0, 512)),
-                    rhs_scale=plane("e", g, 0, slice(0, 512)),
-                    start=(g == 0),
-                    stop=(g == PASSES - 1),
-                )
+                mx(bank[:], ("w", jg, g), slice(t * P, (t + 1) * P), ("w", "e", g), slice(0, 512), g == 0, g == PASSES - 1)
 
         def VS(jg, t):
-            vl = get(vlp, "vl", ("vl", jg), [P, 4, 512], BF16)
+            vl = get(2, "vl", ("vl", jg), [P, 4, H], BF16)
             nc.scalar.activation(out=vl[:, t, :], in_=T["v", jg, t][:], func=ACT.Copy, scale=lg_f[:, jg, t : t + 1])
 
-        def VI(jg):
-            dst = get(grp, "gr", ("gr", ("v", jg)), [P, 2048], BF16, align_bytes=64)
-            nc.vector.tensor_copy(out=dst[:].rearrange("p (c i t) -> p c t i", i=4, t=4), in_=T["vl", jg][:].rearrange("p t (c i) -> p c t i", i=4))
+        def VI(jg, on):
+            dst = get(GROUPED[on], "grouped_" + on, ("grouped", "v", jg), [P, 2048], BF16, align_bytes=64)
+            copy = nc.vector.tensor_copy if on == "V" else nc.scalar.copy
+            copy(out=dst[:].rearrange("p (c i t) -> p c t i", i=4, t=4), in_=T["vl", jg][:].rearrange("p t (c i) -> p c t i", i=4))
 
         def VQ(jg):
-            nc.vector.quantize_mx(out=vc[jg][:].bitcast(FP8X4), scales=vsc[jg][:], in_=T["gr", ("v", jg)][:])
+            quantize(f"v{jg}", ("v", jg), T["grouped", "v", jg][:], H)
 
         def Q(i):
-            h, k = divmod(i, 4)
-            cells = slice(k * P, (k + 1) * P)
-            bank = get(ps_mx, "mx", ("q", i), [P, 512], F32)
+            pr, i2 = divmod(i, 2)
+            bank = get(8 - TR_BANKS, "mx", ("q", i), [P, 512], F32)
             for jg in range(GROUPS):
-                nc.tensor.matmul_mx(
-                    out=bank[:],
-                    lhsT=ac[jg][h][:, cells].bitcast(FP8X4),
-                    lhsT_scale=asc[jg][h][:, cells],
-                    rhs=vc[jg][:].bitcast(FP8X4),
-                    rhs_scale=vsc[jg][:],
-                    start=(jg == 0),
-                    stop=(jg == GROUPS - 1),
-                )
-
-        mu_rows = mu_out.rearrange("(p i) l -> p i l", i=TILES)
-        sd_rows = sd_out.rearrange("(p i) l -> p i l", i=TILES)
-        z_rows = z_out.rearrange("(p i) l -> p i l", i=TILES)
+                mx(bank[:], ("a", pr, jg), slice(i2 * P, (i2 + 1) * P), ("v", jg), slice(0, H), jg == 0, jg == GROUPS - 1)
 
         def QB(i):
             pr, i2 = divmod(i, 2)
-            qb = get(qbp, "qb", ("qb", pr), [P, 2, H], F32)
+            qb = get(RAW_BUFS, "raw", ("qb", pr), [P, 2, H], F32)
             nc.vector.tensor_tensor(out=qb[:, i2, :], in0=T["q", i][:], in1=lb_b[:], op=ALU.add)
+
+        def store(out, key, pr):
+            nc.sync.dma_start(out=rows(out)[:, 2 * pr : 2 * pr + 2, :], in_=T[key, pr][:, :, 0:LATENT])
+
+        def SMU(pr):
+            store(mu_out, "qb", pr)
+
+        def SSD(pr):
+            store(sd_out, "sd", pr)
+
+        def SZ(pr):
+            store(z_out, "z", pr)
 
         def TH(pr):
             qb = T["qb", pr]
-            rows = slice(2 * pr, 2 * pr + 2)
-            nc.sync.dma_start(out=mu_rows[:, rows, :], in_=qb[:, :, 0:LATENT])
-            sd = get(outs, "sd", ("sd", pr), [P, 2, LATENT], F32)
-            nc.scalar.activation(out=sd[:], in_=qb[:, :, LATENT:H], func=ACT.Tanh)
+            th = get(4, "sd", ("sd", pr), [P, 2, LATENT], F32)
+            nc.scalar.activation(out=th[:], in_=qb[:, :, LATENT:H], func=ACT.Tanh)
+
+        def EX(pr):
+            sd = T["sd", pr]
             nc.scalar.activation(out=sd[:], in_=sd[:], func=ACT.Exp, scale=0.5)
-            nc.sync.dma_start(out=sd_rows[:, rows, :], in_=sd[:])
 
-        def Z(pr):
-            rows = slice(2 * pr, 2 * pr + 2)
-            z = get(outs, "z", ("z", pr), [P, 2, LATENT], F32)
-            eng = nc.gpsimd if pr in Z_ON_GPSIMD else nc.vector
-            eng.tensor_tensor(out=z[:], in0=T["sd", pr][:], in1=noise_t[:, rows, :], op=ALU.mult)
+        def ZM(pr, on):
+            eng = nc.vector if on == "V" else nc.gpsimd
+            z = get(4, "z", ("z", pr), [P, 2, LATENT], F32)
+            eng.tensor_tensor(out=z[:], in0=T["sd", pr][:], in1=noise_t[:, 2 * pr : 2 * pr + 2, :], op=ALU.mult)
+
+        def ZA(pr, on):
+            eng = nc.vector if on == "V" else nc.gpsimd
+            z = T["z", pr]
             eng.tensor_tensor(out=z[:], in0=z[:], in1=T["qb", pr][:, :, 0:LATENT], op=ALU.add)
-            nc.sync.dma_start(out=z_rows[:, rows, :], in_=z[:])
 
-        steps = dict(C=C, CF=CF, K=K, Tp=Tp, PP=PP, XQ=XQ, D=D, WQ=WQ, U=U, SI=SI, G=G, AQ=AQ, CS=CS, UT=UT, VM=VM, VS=VS, VI=VI, VQ=VQ, Q=Q, QB=QB, TH=TH, Z=Z)
-        for step in ORDER:
-            steps[step[0]](*step[1:])
+        def touches(name, *a):
+            pr, jg = a[0] if a else None, a[1] if len(a) > 1 else None
+            x_done = [("XQ", pr, 0), ("XQ", pr, 1)]
+            w_done = [("WQ", jg, g) for g in range(PASSES)]
+            turned = (pr, jg) in TURNED
+            return {
+                "K": lambda: ([("x_raw", pr), ("xw", pr)], [("load_x", pr)]),
+                "XT": lambda: ([("xw", 2 * pr), ("xw", 2 * pr + 1)], [("K", 2 * pr), ("K", 2 * pr + 1)]),
+                "PP": lambda: ([("xt", pr, jg), ("xg", pr, jg // 2)], [("XT", pr, jg), ("load_xs",)]),
+                "XQ": lambda: ([("xg", pr, jg)], [("PP", pr, 2 * jg), ("PP", pr, 2 * jg + 1)]),
+                "D": lambda: ([("raw", pr, jg)], [("load_unit", pr, jg)]),
+                "WQ": lambda: ([("grouped", pr, jg)], [s for s in steps if s[:3] == ("D", pr, jg)]),
+                "CF": lambda: ([], [("load_cf",)]),
+                "LC": lambda: ([], [("load_small",)]),
+                "CC": lambda: ([("cf",)], [("CF",)]),
+                "US": lambda: ([], x_done + w_done),
+                "UC": lambda: ([], x_done + w_done),
+                "C": lambda: ([("us",) + a, ("y", pr, jg)], [("US",) + a, ("CC",)]),
+                "CS": lambda: ([("uc",) + a, ("uy", pr, jg)], [("UC",) + a, ("CC",)]),
+                "UT": lambda: ([("uy", pr, jg)], [("CS", pr, jg, 0), ("CS", pr, jg, 1)]),
+                "SI": lambda: ([("ut",) + a, ("y", pr, jg)], [("UT" if turned else "C",) + a, ("load_small",)]),
+                "G": lambda: ([("y", pr, jg)], [("SI", pr, jg, 0), ("SI", pr, jg, 1)]),
+                "AQ": lambda: ([("ag", pr, jg)], [("G", pr, jg)]),
+                "VM": lambda: ([], [("WQ", k, g) for k in (pr, "e") for g in range(PASSES)]),
+                "VS": lambda: ([("v",) + a, ("vl", pr)], [("VM",) + a, ("LC",)]),
+                "VI": lambda: ([("vl", pr)], [("VS", pr, t) for t in range(4)]),
+                "VQ": lambda: ([("grouped", "v", pr)], [s for s in steps if s[:2] == ("VI", pr)]),
+                "Q": lambda: ([], [("AQ", pr // 2, g) for g in range(GROUPS)] + [("VQ", g) for g in range(GROUPS)]),
+                "QB": lambda: ([("q", pr), ("qb", pr // 2)], [("Q", pr), ("load_late",)]),
+                "TH": lambda: ([("qb", pr)], [("QB", 2 * pr), ("QB", 2 * pr + 1)]),
+                "SMU": lambda: ([("qb", pr)], [("QB", 2 * pr), ("QB", 2 * pr + 1)]),
+                "EX": lambda: ([("sd", pr)], [("TH", pr)]),
+                "SSD": lambda: ([("sd", pr)], [("EX", pr)]),
+                "ZM": lambda: ([("sd", pr)], [("EX", pr)]),
+                "ZA": lambda: ([("z", pr), ("qb", pr)], [s for s in steps if s[:2] == ("ZM", pr)]),
+                "SZ": lambda: ([("z", pr)], [s for s in steps if s[:2] == ("ZA", pr)]),
+            }.get(name, lambda: ([], []))()
+
+        calls = dict(load_cf=load_cf, LC=LC, load_x=load_x, load_unit=load_unit, load_xs=load_xs, load_small=load_small, load_late=load_late, K=K, XT=XT, PP=PP, XQ=XQ, D=D, WQ=WQ, CF=CF, CC=CC, US=US, UC=UC, C=C, CS=CS, UT=UT, SI=SI, G=G, AQ=AQ, VM=VM, VS=VS, VI=VI, VQ=VQ, Q=Q, QB=QB, TH=TH, EX=EX, ZM=ZM, ZA=ZA, SMU=SMU, SSD=SSD, SZ=SZ)
+        queues = [
+            [("load_x", 0), ("load_cf",), ("load_unit", 0,0), ("load_x", 1), ("load_xs",), ("load_unit", 0,1), ("load_unit", 0,2), ("load_unit", 0,3), ("load_x", 2), ("load_x", 3), ("load_unit", "e",0), ("load_small",), ("load_unit", "e",3), ("load_unit", "e",1), ("load_x", 4), ("load_x", 5), ("load_unit", "e",2), ("load_x", 6), ("load_unit", 1,0), ("load_unit", 1,2), ("load_x", 7), ("load_unit", 1,3), ("load_unit", 1,1), ("load_late",), ("SMU", 0), ("SSD", 0), ("SMU", 1), ("SSD", 1), ("SMU", 2), ("SSD", 2), ("SZ", 0), ("SMU", 3), ("SSD", 3), ("SZ", 1), ("SZ", 2), ("SZ", 3)],
+            [("D", 0,3,"G"), ("D", "e",3,"G"), ("D", 1,2,"G"), ("D", 1,3,"H")],
+            [("CF",), ("XT", 0,0), ("XT", 0,1), ("XT", 0,2), ("XT", 0,3), ("XT", 1,0), ("XT", 1,1), ("XT", 1,2), ("XT", 1,3), ("US", 0,0,0), ("US", 0,0,1), ("XT", 2,0), ("XT", 2,1), ("XT", 2,2), ("XT", 2,3), ("US", 1,0,0), ("US", 1,0,1), ("VM", 0,0), ("VM", 0,1), ("VM", 0,2), ("VM", 0,3), ("XT", 3,0), ("XT", 3,1), ("XT", 3,2), ("XT", 3,3), ("US", 2,0,0), ("US", 2,0,1), ("UC", 0,1,0), ("UC", 0,1,1), ("UC", 1,1,0), ("UC", 1,1,1), ("VM", 1,0), ("VM", 1,1), ("VM", 1,2), ("VM", 1,3), ("UT", 0,1,0), ("UT", 0,1,1), ("UT", 1,1,0), ("UT", 1,1,1), ("UC", 2,1,0), ("UC", 2,1,1), ("US", 3,0,0), ("US", 3,0,1), ("UT", 2,1,0), ("UT", 2,1,1), ("UC", 3,1,0), ("UC", 3,1,1), ("Q", 0), ("Q", 1), ("UT", 3,1,0), ("UT", 3,1,1), ("Q", 2), ("Q", 3), ("Q", 4), ("Q", 5), ("Q", 6), ("Q", 7)],
+            [("K", 0), ("CC",), ("K", 1), ("D", 0,2,"S"), ("K", 2), ("K", 3), ("D", "e",0,"S"), ("D", "e",1,"S"), ("K", 4), ("K", 5), ("D", "e",2,"S"), ("K", 6), ("D", 1,0,"S"), ("K", 7), ("D", 1,1,"S"), ("LC",), ("SI", 0,0,0), ("SI", 0,0,1), ("VS", 0,0), ("VS", 0,1), ("VS", 0,2), ("VS", 0,3), ("SI", 1,0,0), ("SI", 1,0,1), ("SI", 2,0,0), ("SI", 2,0,1), ("CS", 0,1,0), ("CS", 0,1,1), ("CS", 1,1,0), ("CS", 1,1,1), ("VS", 1,0), ("VS", 1,1), ("VS", 1,2), ("VS", 1,3), ("SI", 0,1,0), ("SI", 0,1,1), ("SI", 1,1,0), ("SI", 1,1,1), ("CS", 2,1,0), ("CS", 2,1,1), ("VI", 1,"S"), ("SI", 2,1,0), ("SI", 2,1,1), ("CS", 3,1,0), ("CS", 3,1,1), ("SI", 3,0,0), ("SI", 3,0,1), ("SI", 3,1,0), ("SI", 3,1,1), ("TH", 0), ("EX", 0), ("TH", 1), ("EX", 1), ("TH", 2), ("EX", 2), ("TH", 3), ("EX", 3)],
+            [("D", 0,0,"V"), ("WQ", 0,0), ("D", 0,1,"V"), ("PP", 0,0), ("PP", 0,1), ("PP", 0,2), ("PP", 0,3), ("WQ", 0,1), ("XQ", 0,0), ("WQ", 0,2), ("XQ", 0,1), ("WQ", 0,3), ("PP", 1,0), ("PP", 1,1), ("PP", 1,2), ("PP", 1,3), ("WQ", "e",0), ("XQ", 1,0), ("WQ", "e",1), ("XQ", 1,1), ("WQ", "e",2), ("WQ", "e",3), ("C", 0,0,0), ("C", 0,0,1), ("PP", 2,0), ("C", 1,0,0), ("C", 1,0,1), ("PP", 2,1), ("PP", 2,2), ("PP", 2,3), ("XQ", 2,0), ("XQ", 2,1), ("WQ", 1,0), ("WQ", 1,2), ("WQ", 1,1), ("WQ", 1,3), ("PP", 3,0), ("C", 2,0,0), ("C", 2,0,1), ("PP", 3,1), ("PP", 3,2), ("PP", 3,3), ("G", 0,0), ("XQ", 3,0), ("XQ", 3,1), ("VI", 0,"V"), ("AQ", 0,0), ("G", 1,0), ("VQ", 0), ("G", 2,0), ("AQ", 1,0), ("AQ", 2,0), ("G", 0,1), ("G", 1,1), ("AQ", 0,1), ("C", 3,0,0), ("C", 3,0,1), ("AQ", 1,1), ("VQ", 1), ("G", 2,1), ("QB", 0), ("QB", 1), ("AQ", 2,1), ("G", 3,0), ("QB", 2), ("QB", 3), ("G", 3,1), ("AQ", 3,0), ("QB", 4), ("AQ", 3,1), ("QB", 5), ("ZM", 0,"V"), ("ZM", 1,"V"), ("QB", 6), ("QB", 7), ("ZA", 0,"V"), ("ZA", 1,"V"), ("ZM", 2,"V"), ("ZM", 3,"V"), ("ZA", 2,"V"), ("ZA", 3,"V")],
+        ]
+        steps = [s for queue in queues for s in queue]
+        done = set()
+
+        def users(key):
+            return [s for s in steps if key in touches(*s)[0]]
+
+        def emit(step):
+            queue = [qu for qu in queues if step in qu][0]
+            for s in queue[: queue.index(step) + 1]:
+                if s not in done:
+                    done.add(s)
+                    for need in touches(*s)[1]:
+                        emit(need)
+                    calls[s[0]](*s[1:])
+
+        for step in steps:
+            emit(step)

@@ -22,7 +22,8 @@ PAIRS = TILES // 2
 FLOPS = 2 * CELLS * GENES * PATHWAYS + 2 * GENES * PATHWAYS * H + 2 * CELLS * PATHWAYS * H
 RAW_BUFS = 6
 TR_BANKS = 4
-TURNED = {(pr, 1) for pr in range(PAIRS)}
+TURNED = {(1, 1), (2, 1)}
+SPANS = [(0, 2), (2, 2), (4, 2), (6, 1), (7, 1)]
 
 
 def tile_pathway_latent_encoder_f5_kernel(
@@ -68,6 +69,7 @@ def tile_pathway_latent_encoder_f5_kernel(
         lg_t = keep.tile([P, GROUPS, 4], BF16, name="lg_t")
         cf_f = keep.tile([P, TILES], F32, name="cf_f")
         lg_f = keep.tile([P, GROUPS, 4], F32, name="lg_f")
+        ag_f = keep.tile([P, GROUPS, 4], F32, name="ag_f")
         lb_b = keep.tile([P, H], BF16, name="lb_b")
         cf_b = keep.tile([P, CELLS], BF16, name="cf_b")
         noise_t = keep.tile([P, TILES, LATENT], BF16, name="noise_t")
@@ -110,6 +112,7 @@ def tile_pathway_latent_encoder_f5_kernel(
 
         def LC():
             nc.scalar.copy(out=lg_f[:], in_=lg_t[:])
+            nc.scalar.copy(out=ag_f[:], in_=ag_t[:])
 
         def K(i):
             xw = get(3, "xw", ("xw", i), [P, GENES], BF16)
@@ -152,27 +155,30 @@ def tile_pathway_latent_encoder_f5_kernel(
         def XQ(pr, a):
             quantize(f"x{pr}{a}", ("x", pr, a), T["xg", pr, a][:].rearrange("p g c -> p (g c)"), 512)
 
-        def D(k, g, eng):
-            dst = get(GROUPED[eng], "grouped_" + eng, ("grouped", k, g), [P, 2048], BF16, align_bytes=64)
+        def D(k, g, eng, lo=0, hi=4):
+            ring = "S" if (lo, hi) != (0, 4) else "G" if (k, g) == (0, 0) else eng
+            dst = get(GROUPED[ring], "grouped_" + ring, ("grouped", k, g), [P, 2048], BF16, align_bytes=64)
             raw = T["raw", k, g]
+            out = dst[:, lo * 512 : hi * 512]
+            if eng in ("G", "H"):
+                if k == "e":
+                    o = out.rearrange("p (c j) -> p c j", j=4)
+                    i = raw[:, :, lo * P : hi * P].rearrange("p j c -> p c j")
+                else:
+                    o = out.rearrange("p (t m j) -> p m t j", m=P, j=4)
+                    i = raw[:].rearrange("p j (m t) -> p m t j", t=4)[:, :, lo:hi, :]
+                nc.gpsimd.tensor_scalar(out=o, in0=i, scalar1=1.0, scalar2=0.0, op0=ALU.mult, op1=ALU.add)
+                return
             if k == "e":
-                o = dst[:].rearrange("p (c i j) -> p c j i", i=4, j=4)
-                i = raw[:].rearrange("p j (c i) -> p c j i", i=4)
+                o = out.rearrange("p (c i j) -> p c j i", i=4, j=4)
+                i = raw[:, :, lo * P : hi * P].rearrange("p j (c i) -> p c j i", i=4)
             else:
-                o = dst[:].rearrange("p (t m j) -> p m j t", t=4, j=4)
-                i = raw[:].rearrange("p j (m t) -> p m j t", t=4)
+                o = out.rearrange("p (t m j) -> p m j t", m=P, j=4)
+                i = raw[:].rearrange("p j (m t) -> p m j t", t=4)[:, :, :, lo:hi]
             if eng == "V":
                 nc.vector.tensor_copy(out=o, in_=i)
-            elif eng == "S":
-                nc.scalar.copy(out=o, in_=i)
             else:
-                if k == "e":
-                    o = dst[:].rearrange("p (c j) -> p c j", j=4)
-                    i = raw[:].rearrange("p j c -> p c j")
-                else:
-                    o = dst[:].rearrange("p (t m j) -> p m t j", t=4, j=4)
-                    i = raw[:].rearrange("p j (m t) -> p m t j", t=4)
-                nc.gpsimd.tensor_scalar(out=o, in0=i, scalar1=1.0, scalar2=0.0, op0=ALU.mult, op1=ALU.add)
+                nc.scalar.copy(out=o, in_=i)
 
         def WQ(k, g):
             quantize(f"w{k}{g}", ("w", k, g), T["grouped", k, g][:], 512)
@@ -180,57 +186,89 @@ def tile_pathway_latent_encoder_f5_kernel(
         def x_cols(g, first, count):
             return slice((g % 2) * 256 + first, (g % 2) * 256 + first + count)
 
-        def US(pr, jg, b):
-            bank = get(8 - TR_BANKS, "mx", ("us", pr, jg, b), [P, 512], F32)
-            for tt in range(2):
-                t = 2 * b + tt
-                for g in range(PASSES):
-                    mx(bank[:, tt * 256 : (tt + 1) * 256], ("w", jg, g), slice(t * P, (t + 1) * P), ("x", pr, g // 2), x_cols(g, 0, 256), g == 0, g == PASSES - 1)
+        def span(s):
+            first, count = SPANS[s]
+            return first, count, count * P, 4 // count
 
-        def C(pr, jg, b):
-            y = get(RAW_BUFS, "y", ("y", pr, jg), [P, 4, 256], F32)
+        def US(s, jg, b):
+            first, count, width, per = span(s)
+            bank = get(8 - TR_BANKS, "mx", ("us", s, jg, b), [P, 512], F32)
+            for tt in range(per):
+                t = per * b + tt
+                for g in range(PASSES):
+                    mx(bank[:, tt * width : (tt + 1) * width], ("w", jg, g), slice(t * P, (t + 1) * P), ("x", first // 2, g // 2), x_cols(g, first % 2 * P, width), g == 0, g == PASSES - 1)
+
+        def C(s, jg, b):
+            first, count, width, per = span(s)
+            y = get(RAW_BUFS, "y", ("y", s, jg), [P, 4, width], F32)
             nc.vector.tensor_tensor(
-                out=y[:, 2 * b : 2 * b + 2, :],
-                in0=T["us", pr, jg, b][:].rearrange("p (t m) -> p t m", t=2),
-                in1=cf_b[:, pr * 256 : (pr + 1) * 256].unsqueeze(1).to_broadcast([P, 2, 256]),
+                out=y[:, per * b : per * (b + 1), :],
+                in0=T["us", s, jg, b][:].rearrange("p (t m) -> p t m", t=per),
+                in1=cf_b[:, first * P : first * P + width].unsqueeze(1).to_broadcast([P, per, width]),
                 op=ALU.mult,
             )
 
-        def UC(pr, jg, i2):
-            bank = get(8 - TR_BANKS, "mx", ("uc", pr, jg, i2), [P, 512], F32)
+        def UC(s, jg, i2):
+            i = SPANS[s][0] + i2
+            bank = get(8 - TR_BANKS, "mx", ("uc", s, jg, i2), [P, 512], F32)
             for g in range(PASSES):
-                mx(bank[:], ("x", pr, g // 2), x_cols(g, i2 * P, P), ("w", jg, g), slice(0, 512), g == 0, g == PASSES - 1)
+                mx(bank[:], ("x", i // 2, g // 2), x_cols(g, i % 2 * P, P), ("w", jg, g), slice(0, 512), g == 0, g == PASSES - 1)
 
-        def CS(pr, jg, i2):
-            uy = get(4, "uy", ("uy", pr, jg), [P, 2, 512], F32)
-            i = 2 * pr + i2
-            nc.scalar.activation(out=uy[:, i2, :], in_=T["uc", pr, jg, i2][:], func=ACT.Copy, scale=cf_f[:, i : i + 1])
+        def CS(s, jg, i2):
+            first, count, width, per = span(s)
+            uy = get(4, "uy", ("uy", s, jg), [P, count, 512], F32)
+            i = first + i2
+            nc.scalar.activation(out=uy[:, i2, :], in_=T["uc", s, jg, i2][:], func=ACT.Copy, scale=cf_f[:, i : i + 1])
 
-        def UT(pr, jg, b):
-            bank = get(TR_BANKS, "tr", ("ut", pr, jg, b), [P, 512], F32)
-            for tt in range(2):
-                t = 2 * b + tt
-                for i2 in range(2):
-                    nc.tensor.transpose(bank[:, tt * 256 + i2 * P : tt * 256 + (i2 + 1) * P], T["uy", pr, jg][:, i2, t * P : (t + 1) * P], ident[:])
+        def UT(s, jg, b):
+            first, count, width, per = span(s)
+            bank = get(TR_BANKS, "tr", ("ut", s, jg, b), [P, 512], F32)
+            for tt in range(per):
+                t = per * b + tt
+                for i2 in range(count):
+                    nc.tensor.transpose(bank[:, tt * width + i2 * P : tt * width + (i2 + 1) * P], T["uy", s, jg][:, i2, t * P : (t + 1) * P], ident[:])
 
-        def SI(pr, jg, b):
-            y = get(RAW_BUFS, "y", ("y", pr, jg), [P, 4, 256], F32)
-            for tt in range(2):
-                t = 2 * b + tt
-                src = T["ut", pr, jg, b][:, tt * 256 : (tt + 1) * 256] if ("ut", pr, jg, b) in T else y[:, t, :]
+        def SI(s, jg, b):
+            first, count, width, per = span(s)
+            y = get(RAW_BUFS, "y", ("y", s, jg), [P, 4, width], F32)
+            for tt in range(per):
+                t = per * b + tt
+                src = T["ut", s, jg, b][:, tt * width : (tt + 1) * width] if (s, jg) in TURNED else y[:, t, :]
                 nc.scalar.activation(out=y[:, t, :], in_=src, func=ACT.Silu, bias=pb_t[:, jg, t : t + 1])
 
-        def G(pr, jg):
-            dst = get(3, "ag", ("ag", pr, jg), [P, 1024], BF16, align_bytes=64)
+        def G(s, jg):
+            first, count, width, per = span(s)
+            dst = get(3, "ag", ("ag", s, jg), [P, 4 * width], BF16, align_bytes=64)
             nc.vector.tensor_tensor(
                 out=dst[:].rearrange("p (c i t) -> p c t i", i=4, t=4),
-                in0=T["y", pr, jg][:].rearrange("p t (c i) -> p c t i", i=4),
-                in1=ag_t[:, jg, :].unsqueeze(1).unsqueeze(3).to_broadcast([P, 64, 4, 4]),
+                in0=T["y", s, jg][:].rearrange("p t (c i) -> p c t i", i=4),
+                in1=ag_t[:, jg, :].unsqueeze(1).unsqueeze(3).to_broadcast([P, width // 4, 4, 4]),
                 op=ALU.mult,
             )
 
-        def AQ(pr, jg):
-            quantize(f"a{pr}{jg}", ("a", pr, jg), T["ag", pr, jg][:], 256)
+        def GG(s, jg):
+            first, count, width, per = span(s)
+            dst = get(3, "ag", ("ag", s, jg), [P, 4 * width], BF16, align_bytes=64)
+            nc.gpsimd.tensor_tensor(
+                out=dst[:].rearrange("p (c t) -> p c t", t=4),
+                in0=T["y", s, jg][:].rearrange("p t c -> p c t"),
+                in1=ag_f[:, jg, :].unsqueeze(1).to_broadcast([P, width, 4]),
+                op=ALU.mult,
+            )
+
+        def GS(s, jg):
+            first, count, width, per = span(s)
+            planes = get(2, "planes", ("planes", s, jg), [P, 4, width], BF16)
+            for t in range(4):
+                nc.scalar.activation(out=planes[:, t, :], in_=T["y", s, jg][:, t, :], func=ACT.Copy, scale=ag_f[:, jg, t : t + 1])
+
+        def GI(s, jg):
+            first, count, width, per = span(s)
+            dst = get(3, "ag", ("ag", s, jg), [P, 4 * width], BF16, align_bytes=64)
+            nc.vector.tensor_copy(out=dst[:].rearrange("p (c i t) -> p c t i", i=4, t=4), in_=T["planes", s, jg][:].rearrange("p t (c i) -> p c t i", i=4))
+
+        def AQ(s, jg):
+            quantize(f"a{s}{jg}", ("a", s, jg), T["ag", s, jg][:], SPANS[s][1] * P)
 
         def VM(jg, t):
             bank = get(8 - TR_BANKS, "mx", ("v", jg, t), [P, 512], F32)
@@ -243,57 +281,69 @@ def tile_pathway_latent_encoder_f5_kernel(
 
         def VI(jg, on):
             dst = get(GROUPED[on], "grouped_" + on, ("grouped", "v", jg), [P, 2048], BF16, align_bytes=64)
-            copy = nc.vector.tensor_copy if on == "V" else nc.scalar.copy
-            copy(out=dst[:].rearrange("p (c i t) -> p c t i", i=4, t=4), in_=T["vl", jg][:].rearrange("p t (c i) -> p c t i", i=4))
+            if on == "G":
+                nc.gpsimd.tensor_scalar(
+                    out=dst[:].rearrange("p (c t) -> p c t", t=4), in0=T["vl", jg][:].rearrange("p t c -> p c t"), scalar1=1.0, scalar2=0.0, op0=ALU.mult, op1=ALU.add
+                )
+            else:
+                copy = nc.vector.tensor_copy if on == "V" else nc.scalar.copy
+                copy(out=dst[:].rearrange("p (c i t) -> p c t i", i=4, t=4), in_=T["vl", jg][:].rearrange("p t (c i) -> p c t i", i=4))
 
         def VQ(jg):
             quantize(f"v{jg}", ("v", jg), T["grouped", "v", jg][:], H)
 
+        def span_of(i):
+            return [s for s, (first, count) in enumerate(SPANS) if first <= i < first + count][0]
+
         def Q(i):
-            pr, i2 = divmod(i, 2)
+            s = span_of(i)
+            i2 = i - SPANS[s][0]
             bank = get(8 - TR_BANKS, "mx", ("q", i), [P, 512], F32)
             for jg in range(GROUPS):
-                mx(bank[:], ("a", pr, jg), slice(i2 * P, (i2 + 1) * P), ("v", jg), slice(0, H), jg == 0, jg == GROUPS - 1)
+                mx(bank[:], ("a", s, jg), slice(i2 * P, (i2 + 1) * P), ("v", jg), slice(0, H), jg == 0, jg == GROUPS - 1)
 
         def QB(i):
-            pr, i2 = divmod(i, 2)
-            qb = get(RAW_BUFS, "raw", ("qb", pr), [P, 2, H], F32)
-            nc.vector.tensor_tensor(out=qb[:, i2, :], in0=T["q", i][:], in1=lb_b[:], op=ALU.add)
+            s = span_of(i)
+            qb = get(RAW_BUFS, "raw", ("qb", s), [P, SPANS[s][1], H], F32)
+            nc.vector.tensor_tensor(out=qb[:, i - SPANS[s][0], :], in0=T["q", i][:], in1=lb_b[:], op=ALU.add)
 
-        def store(out, key, pr):
-            nc.sync.dma_start(out=rows(out)[:, 2 * pr : 2 * pr + 2, :], in_=T[key, pr][:, :, 0:LATENT])
+        def tiles(s):
+            return slice(SPANS[s][0], SPANS[s][0] + SPANS[s][1])
 
-        def SMU(pr):
-            store(mu_out, "qb", pr)
+        def store(out, key, s):
+            nc.sync.dma_start(out=rows(out)[:, tiles(s), :], in_=T[key, s][:, :, 0:LATENT])
 
-        def SSD(pr):
-            store(sd_out, "sd", pr)
+        def SMU(s):
+            store(mu_out, "qb", s)
 
-        def SZ(pr):
-            store(z_out, "z", pr)
+        def SSD(s):
+            store(sd_out, "sd", s)
 
-        def TH(pr):
-            qb = T["qb", pr]
-            th = get(4, "sd", ("sd", pr), [P, 2, LATENT], F32)
-            nc.scalar.activation(out=th[:], in_=qb[:, :, LATENT:H], func=ACT.Tanh)
+        def SZ(s):
+            store(z_out, "z", s)
 
-        def EX(pr):
-            sd = T["sd", pr]
+        def TH(s):
+            sd = get(1, f"sd{s}", ("sd", s), [P, SPANS[s][1], LATENT], F32)
+            nc.scalar.activation(out=sd[:], in_=T["qb", s][:, :, LATENT:H], func=ACT.Tanh)
+
+        def EX(s):
+            sd = T["sd", s]
             nc.scalar.activation(out=sd[:], in_=sd[:], func=ACT.Exp, scale=0.5)
 
-        def ZM(pr, on):
+        def ZM(s, on):
             eng = nc.vector if on == "V" else nc.gpsimd
-            z = get(4, "z", ("z", pr), [P, 2, LATENT], F32)
-            eng.tensor_tensor(out=z[:], in0=T["sd", pr][:], in1=noise_t[:, 2 * pr : 2 * pr + 2, :], op=ALU.mult)
+            z = get(1, f"z{s}", ("z", s), [P, SPANS[s][1], LATENT], F32)
+            eng.tensor_tensor(out=z[:], in0=T["sd", s][:], in1=noise_t[:, tiles(s), :], op=ALU.mult)
 
-        def ZA(pr, on):
+        def ZA(s, on):
             eng = nc.vector if on == "V" else nc.gpsimd
-            z = T["z", pr]
-            eng.tensor_tensor(out=z[:], in0=z[:], in1=T["qb", pr][:, :, 0:LATENT], op=ALU.add)
+            z = T["z", s]
+            eng.tensor_tensor(out=z[:], in0=z[:], in1=T["qb", s][:, :, 0:LATENT], op=ALU.add)
 
         def touches(name, *a):
             pr, jg = a[0] if a else None, a[1] if len(a) > 1 else None
-            x_done = [("XQ", pr, 0), ("XQ", pr, 1)]
+            banks = range(SPANS[pr][1]) if name in ("US", "UC", "UT", "G", "GG", "GS", "TH", "SMU") else ()
+            x_done = [("XQ", SPANS[pr][0] // 2, half) for half in range(2)] if banks else []
             w_done = [("WQ", jg, g) for g in range(PASSES)]
             turned = (pr, jg) in TURNED
             return {
@@ -301,7 +351,7 @@ def tile_pathway_latent_encoder_f5_kernel(
                 "XT": lambda: ([("xw", 2 * pr), ("xw", 2 * pr + 1)], [("K", 2 * pr), ("K", 2 * pr + 1)]),
                 "PP": lambda: ([("xt", pr, jg), ("xg", pr, jg // 2)], [("XT", pr, jg), ("load_xs",)]),
                 "XQ": lambda: ([("xg", pr, jg)], [("PP", pr, 2 * jg), ("PP", pr, 2 * jg + 1)]),
-                "D": lambda: ([("raw", pr, jg)], [("load_unit", pr, jg)]),
+                "D": lambda: ([("raw", pr, jg), ("grouped", pr, jg)], [("load_unit", pr, jg)]),
                 "WQ": lambda: ([("grouped", pr, jg)], [s for s in steps if s[:3] == ("D", pr, jg)]),
                 "CF": lambda: ([], [("load_cf",)]),
                 "LC": lambda: ([], [("load_small",)]),
@@ -310,18 +360,21 @@ def tile_pathway_latent_encoder_f5_kernel(
                 "UC": lambda: ([], x_done + w_done),
                 "C": lambda: ([("us",) + a, ("y", pr, jg)], [("US",) + a, ("CC",)]),
                 "CS": lambda: ([("uc",) + a, ("uy", pr, jg)], [("UC",) + a, ("CC",)]),
-                "UT": lambda: ([("uy", pr, jg)], [("CS", pr, jg, 0), ("CS", pr, jg, 1)]),
+                "UT": lambda: ([("uy", pr, jg)], [("CS", pr, jg, b) for b in banks]),
                 "SI": lambda: ([("ut",) + a, ("y", pr, jg)], [("UT" if turned else "C",) + a, ("load_small",)]),
-                "G": lambda: ([("y", pr, jg)], [("SI", pr, jg, 0), ("SI", pr, jg, 1)]),
-                "AQ": lambda: ([("ag", pr, jg)], [("G", pr, jg)]),
+                "G": lambda: ([("y", pr, jg)], [("SI", pr, jg, b) for b in banks]),
+                "GG": lambda: ([("y", pr, jg)], [("SI", pr, jg, b) for b in banks] + [("LC",)]),
+                "GS": lambda: ([("y", pr, jg)], [("SI", pr, jg, b) for b in banks]),
+                "GI": lambda: ([("planes", pr, jg)], [("GS", pr, jg)]),
+                "AQ": lambda: ([("ag", pr, jg)], [s for s in steps if s in (("G", pr, jg), ("GI", pr, jg), ("GG", pr, jg))]),
                 "VM": lambda: ([], [("WQ", k, g) for k in (pr, "e") for g in range(PASSES)]),
                 "VS": lambda: ([("v",) + a, ("vl", pr)], [("VM",) + a, ("LC",)]),
                 "VI": lambda: ([("vl", pr)], [("VS", pr, t) for t in range(4)]),
                 "VQ": lambda: ([("grouped", "v", pr)], [s for s in steps if s[:2] == ("VI", pr)]),
-                "Q": lambda: ([], [("AQ", pr // 2, g) for g in range(GROUPS)] + [("VQ", g) for g in range(GROUPS)]),
-                "QB": lambda: ([("q", pr), ("qb", pr // 2)], [("Q", pr), ("load_late",)]),
-                "TH": lambda: ([("qb", pr)], [("QB", 2 * pr), ("QB", 2 * pr + 1)]),
-                "SMU": lambda: ([("qb", pr)], [("QB", 2 * pr), ("QB", 2 * pr + 1)]),
+                "Q": lambda: ([], [("AQ", span_of(pr), g) for g in range(GROUPS)] + [("VQ", g) for g in range(GROUPS)]),
+                "QB": lambda: ([("q", pr), ("qb", span_of(pr))], [("Q", pr), ("load_late",)]),
+                "TH": lambda: ([("qb", pr)], [("QB", SPANS[pr][0] + b) for b in banks]),
+                "SMU": lambda: ([("qb", pr)], [("QB", SPANS[pr][0] + b) for b in banks]),
                 "EX": lambda: ([("sd", pr)], [("TH", pr)]),
                 "SSD": lambda: ([("sd", pr)], [("EX", pr)]),
                 "ZM": lambda: ([("sd", pr)], [("EX", pr)]),
@@ -329,13 +382,13 @@ def tile_pathway_latent_encoder_f5_kernel(
                 "SZ": lambda: ([("z", pr)], [s for s in steps if s[:2] == ("ZA", pr)]),
             }.get(name, lambda: ([], []))()
 
-        calls = dict(load_cf=load_cf, LC=LC, load_x=load_x, load_unit=load_unit, load_xs=load_xs, load_small=load_small, load_late=load_late, K=K, XT=XT, PP=PP, XQ=XQ, D=D, WQ=WQ, CF=CF, CC=CC, US=US, UC=UC, C=C, CS=CS, UT=UT, SI=SI, G=G, AQ=AQ, VM=VM, VS=VS, VI=VI, VQ=VQ, Q=Q, QB=QB, TH=TH, EX=EX, ZM=ZM, ZA=ZA, SMU=SMU, SSD=SSD, SZ=SZ)
+        calls = dict(GG=GG, GS=GS, GI=GI, load_cf=load_cf, LC=LC, load_x=load_x, load_unit=load_unit, load_xs=load_xs, load_small=load_small, load_late=load_late, K=K, XT=XT, PP=PP, XQ=XQ, D=D, WQ=WQ, CF=CF, CC=CC, US=US, UC=UC, C=C, CS=CS, UT=UT, SI=SI, G=G, AQ=AQ, VM=VM, VS=VS, VI=VI, VQ=VQ, Q=Q, QB=QB, TH=TH, EX=EX, ZM=ZM, ZA=ZA, SMU=SMU, SSD=SSD, SZ=SZ)
         queues = [
-            [("load_x", 0), ("load_cf",), ("load_unit", 0,0), ("load_x", 1), ("load_xs",), ("load_unit", 0,1), ("load_unit", 0,2), ("load_unit", 0,3), ("load_x", 2), ("load_x", 3), ("load_unit", "e",0), ("load_small",), ("load_unit", "e",3), ("load_unit", "e",1), ("load_x", 4), ("load_x", 5), ("load_unit", "e",2), ("load_x", 6), ("load_unit", 1,0), ("load_unit", 1,2), ("load_x", 7), ("load_unit", 1,3), ("load_unit", 1,1), ("load_late",), ("SMU", 0), ("SSD", 0), ("SMU", 1), ("SSD", 1), ("SMU", 2), ("SSD", 2), ("SZ", 0), ("SMU", 3), ("SSD", 3), ("SZ", 1), ("SZ", 2), ("SZ", 3)],
-            [("D", 0,3,"G"), ("D", "e",3,"G"), ("D", 1,2,"G"), ("D", 1,3,"H")],
-            [("CF",), ("XT", 0,0), ("XT", 0,1), ("XT", 0,2), ("XT", 0,3), ("XT", 1,0), ("XT", 1,1), ("XT", 1,2), ("XT", 1,3), ("US", 0,0,0), ("US", 0,0,1), ("XT", 2,0), ("XT", 2,1), ("XT", 2,2), ("XT", 2,3), ("US", 1,0,0), ("US", 1,0,1), ("VM", 0,0), ("VM", 0,1), ("VM", 0,2), ("VM", 0,3), ("XT", 3,0), ("XT", 3,1), ("XT", 3,2), ("XT", 3,3), ("US", 2,0,0), ("US", 2,0,1), ("UC", 0,1,0), ("UC", 0,1,1), ("UC", 1,1,0), ("UC", 1,1,1), ("VM", 1,0), ("VM", 1,1), ("VM", 1,2), ("VM", 1,3), ("UT", 0,1,0), ("UT", 0,1,1), ("UT", 1,1,0), ("UT", 1,1,1), ("UC", 2,1,0), ("UC", 2,1,1), ("US", 3,0,0), ("US", 3,0,1), ("UT", 2,1,0), ("UT", 2,1,1), ("UC", 3,1,0), ("UC", 3,1,1), ("Q", 0), ("Q", 1), ("UT", 3,1,0), ("UT", 3,1,1), ("Q", 2), ("Q", 3), ("Q", 4), ("Q", 5), ("Q", 6), ("Q", 7)],
-            [("K", 0), ("CC",), ("K", 1), ("D", 0,2,"S"), ("K", 2), ("K", 3), ("D", "e",0,"S"), ("D", "e",1,"S"), ("K", 4), ("K", 5), ("D", "e",2,"S"), ("K", 6), ("D", 1,0,"S"), ("K", 7), ("D", 1,1,"S"), ("LC",), ("SI", 0,0,0), ("SI", 0,0,1), ("VS", 0,0), ("VS", 0,1), ("VS", 0,2), ("VS", 0,3), ("SI", 1,0,0), ("SI", 1,0,1), ("SI", 2,0,0), ("SI", 2,0,1), ("CS", 0,1,0), ("CS", 0,1,1), ("CS", 1,1,0), ("CS", 1,1,1), ("VS", 1,0), ("VS", 1,1), ("VS", 1,2), ("VS", 1,3), ("SI", 0,1,0), ("SI", 0,1,1), ("SI", 1,1,0), ("SI", 1,1,1), ("CS", 2,1,0), ("CS", 2,1,1), ("VI", 1,"S"), ("SI", 2,1,0), ("SI", 2,1,1), ("CS", 3,1,0), ("CS", 3,1,1), ("SI", 3,0,0), ("SI", 3,0,1), ("SI", 3,1,0), ("SI", 3,1,1), ("TH", 0), ("EX", 0), ("TH", 1), ("EX", 1), ("TH", 2), ("EX", 2), ("TH", 3), ("EX", 3)],
-            [("D", 0,0,"V"), ("WQ", 0,0), ("D", 0,1,"V"), ("PP", 0,0), ("PP", 0,1), ("PP", 0,2), ("PP", 0,3), ("WQ", 0,1), ("XQ", 0,0), ("WQ", 0,2), ("XQ", 0,1), ("WQ", 0,3), ("PP", 1,0), ("PP", 1,1), ("PP", 1,2), ("PP", 1,3), ("WQ", "e",0), ("XQ", 1,0), ("WQ", "e",1), ("XQ", 1,1), ("WQ", "e",2), ("WQ", "e",3), ("C", 0,0,0), ("C", 0,0,1), ("PP", 2,0), ("C", 1,0,0), ("C", 1,0,1), ("PP", 2,1), ("PP", 2,2), ("PP", 2,3), ("XQ", 2,0), ("XQ", 2,1), ("WQ", 1,0), ("WQ", 1,2), ("WQ", 1,1), ("WQ", 1,3), ("PP", 3,0), ("C", 2,0,0), ("C", 2,0,1), ("PP", 3,1), ("PP", 3,2), ("PP", 3,3), ("G", 0,0), ("XQ", 3,0), ("XQ", 3,1), ("VI", 0,"V"), ("AQ", 0,0), ("G", 1,0), ("VQ", 0), ("G", 2,0), ("AQ", 1,0), ("AQ", 2,0), ("G", 0,1), ("G", 1,1), ("AQ", 0,1), ("C", 3,0,0), ("C", 3,0,1), ("AQ", 1,1), ("VQ", 1), ("G", 2,1), ("QB", 0), ("QB", 1), ("AQ", 2,1), ("G", 3,0), ("QB", 2), ("QB", 3), ("G", 3,1), ("AQ", 3,0), ("QB", 4), ("AQ", 3,1), ("QB", 5), ("ZM", 0,"V"), ("ZM", 1,"V"), ("QB", 6), ("QB", 7), ("ZA", 0,"V"), ("ZA", 1,"V"), ("ZM", 2,"V"), ("ZM", 3,"V"), ("ZA", 2,"V"), ("ZA", 3,"V")],
+            [("load_x", 0), ("load_cf",), ("load_unit", 0,0), ("load_x", 1), ("load_xs",), ("load_unit", 0,1), ("load_unit", 0,2), ("load_unit", 0,3), ("load_x", 2), ("load_x", 3), ("load_unit", "e",0), ("load_small",), ("load_unit", "e",3), ("load_unit", "e",1), ("load_x", 4), ("load_x", 5), ("load_unit", "e",2), ("load_x", 6), ("load_unit", 1,0), ("load_unit", 1,2), ("load_x", 7), ("load_unit", 1,3), ("load_unit", 1,1), ("load_late",), ("SMU", 0), ("SMU", 1), ("SSD", 0), ("SSD", 1), ("SMU", 2), ("SMU", 3), ("SZ", 0), ("SSD", 2), ("SMU", 4), ("SSD", 3), ("SZ", 1), ("SSD", 4), ("SZ", 2), ("SZ", 3), ("SZ", 4)],
+            [("D", 0,3,"G"), ("D", "e",3,"G"), ("D", 1,2,"G"), ("D", 1,3,"H"), ("VI", 0,"G"), ("VI", 1,"G"), ("ZM", 0,"G"), ("ZA", 0,"G")],
+            [("CF",), ("XT", 0,0), ("XT", 0,1), ("XT", 0,2), ("XT", 0,3), ("XT", 1,0), ("XT", 1,1), ("XT", 1,2), ("XT", 1,3), ("US", 0,0,0), ("XT", 2,0), ("XT", 2,1), ("US", 0,0,1), ("XT", 2,2), ("XT", 2,3), ("US", 1,0,0), ("US", 1,0,1), ("VM", 0,0), ("VM", 0,1), ("VM", 0,2), ("XT", 3,0), ("XT", 3,1), ("VM", 0,3), ("XT", 3,2), ("XT", 3,3), ("US", 2,0,0), ("US", 2,0,1), ("VM", 1,0), ("VM", 1,1), ("VM", 1,2), ("VM", 1,3), ("US", 0,1,0), ("US", 0,1,1), ("UC", 1,1,0), ("UC", 1,1,1), ("UC", 2,1,0), ("UC", 2,1,1), ("UT", 1,1,0), ("UT", 1,1,1), ("US", 3,0,0), ("US", 3,1,0), ("UT", 2,1,0), ("UT", 2,1,1), ("Q", 0), ("Q", 1), ("US", 4,0,0), ("US", 4,1,0), ("Q", 2), ("Q", 3), ("Q", 4), ("Q", 5), ("Q", 6), ("Q", 7)],
+            [("K", 0), ("CC",), ("K", 1), ("D", 0,2,"S"), ("K", 2), ("K", 3), ("D", "e",0,"S"), ("K", 4), ("K", 5), ("D", "e",1,"S"), ("D", "e",2,"S"), ("K", 6), ("D", 1,0,"S"), ("K", 7), ("D", 1,1,"S"), ("LC",), ("VS", 0,0), ("VS", 0,1), ("VS", 0,2), ("VS", 0,3), ("SI", 0,0,0), ("SI", 0,0,1), ("SI", 1,0,0), ("SI", 1,0,1), ("GS", 0,0), ("VS", 1,0), ("VS", 1,1), ("VS", 1,2), ("VS", 1,3), ("GS", 1,0), ("SI", 2,0,0), ("SI", 2,0,1), ("SI", 0,1,0), ("SI", 0,1,1), ("CS", 1,1,0), ("CS", 1,1,1), ("GS", 2,0), ("CS", 2,1,0), ("CS", 2,1,1), ("SI", 1,1,0), ("SI", 1,1,1), ("GS", 1,1), ("SI", 3,0,0), ("SI", 3,1,0), ("SI", 2,1,0), ("SI", 2,1,1), ("GS", 2,1), ("TH", 0), ("SI", 4,0,0), ("SI", 4,1,0), ("EX", 0), ("TH", 1), ("EX", 1), ("TH", 2), ("EX", 2), ("TH", 3), ("EX", 3), ("TH", 4), ("EX", 4)],
+            [("D", 0,0,"V"), ("WQ", 0,0), ("D", 0,1,"V"), ("PP", 0,0), ("PP", 0,1), ("PP", 0,2), ("PP", 0,3), ("WQ", 0,1), ("XQ", 0,0), ("WQ", 0,2), ("XQ", 0,1), ("WQ", 0,3), ("PP", 1,0), ("PP", 1,1), ("PP", 1,2), ("PP", 1,3), ("XQ", 1,0), ("XQ", 1,1), ("WQ", "e",0), ("WQ", "e",1), ("WQ", "e",2), ("WQ", "e",3), ("C", 0,0,0), ("C", 0,0,1), ("PP", 2,0), ("C", 1,0,0), ("C", 1,0,1), ("PP", 2,1), ("PP", 2,2), ("PP", 2,3), ("XQ", 2,0), ("XQ", 2,1), ("WQ", 1,0), ("WQ", 1,1), ("WQ", 1,3), ("WQ", 1,2), ("PP", 3,0), ("C", 2,0,0), ("C", 2,0,1), ("PP", 3,1), ("GI", 0,0), ("AQ", 0,0), ("VQ", 0), ("PP", 3,2), ("C", 0,1,0), ("C", 0,1,1), ("PP", 3,3), ("GI", 1,0), ("XQ", 3,0), ("XQ", 3,1), ("VQ", 1), ("AQ", 1,0), ("G", 0,1), ("GI", 2,0), ("AQ", 0,1), ("AQ", 2,0), ("C", 3,0,0), ("GI", 1,1), ("C", 3,1,0), ("AQ", 1,1), ("QB", 0), ("QB", 1), ("G", 3,0), ("G", 3,1), ("C", 4,0,0), ("AQ", 3,0), ("C", 4,1,0), ("AQ", 3,1), ("GI", 2,1), ("QB", 2), ("QB", 3), ("AQ", 2,1), ("G", 4,0), ("G", 4,1), ("AQ", 4,0), ("AQ", 4,1), ("QB", 4), ("QB", 5), ("QB", 6), ("QB", 7), ("ZM", 1,"V"), ("ZM", 2,"V"), ("ZA", 1,"V"), ("ZA", 2,"V"), ("ZM", 3,"V"), ("ZM", 4,"V"), ("ZA", 3,"V"), ("ZA", 4,"V")],
         ]
         steps = [s for queue in queues for s in queue]
         done = set()

@@ -20,10 +20,12 @@ GROUPS = PATHWAYS // 512
 TILES = CELLS // P
 PAIRS = TILES // 2
 FLOPS = 2 * CELLS * GENES * PATHWAYS + 2 * GENES * PATHWAYS * H + 2 * CELLS * PATHWAYS * H
-RAW_BUFS = 6
 TR_BANKS = 4
-TURNED = {(1, 1), (2, 1)}
-SPANS = [(0, 2), (2, 2), (4, 2), (6, 1), (7, 1)]
+LB_COLS = LATENT
+GAIN_RUN = 2
+SPANS = [(0, 4), (4, 2), (6, 1), (7, 1)]
+OUTS = [(0, 2), (2, 2), (4, 2), (6, 1), (7, 1)]
+BUFS = {"x_raw": 5, "raw": 7, "xw": 4, "xg": 4, "grouped_S": 4, "y4": 2, "y2": 2, "y1": 4, "uy": 4, "ag4": 2, "ag2": 2, "ag1": 4}
 
 
 def tile_pathway_latent_encoder_f5_kernel(
@@ -31,59 +33,53 @@ def tile_pathway_latent_encoder_f5_kernel(
 ):
     nc = tc.nc
     with ExitStack() as ctx:
-        keep = ctx.enter_context(tc.tile_pool(name="keep", bufs=1))
-        pools = {1: keep}
-        for n in (2, 3, 4, RAW_BUFS):
-            pools[n] = ctx.enter_context(tc.tile_pool(name=f"ring{n}", bufs=n))
+        sb = ctx.enter_context(tc.tile_pool(name="sb", bufs=1))
         ps_tr = ctx.enter_context(tc.psum_pool(name="ps_tr", bufs=TR_BANKS))
         ps_mx = ctx.enter_context(tc.psum_pool(name="ps_mx", bufs=8 - TR_BANKS))
         ctx.enter_context(tc.manual_schedule())
-
-        GROUPED = {"S": 4, "V": 2, "G": 1, "H": 1}
         T = {}
-        taken = {}
 
-        def get(bufs, tag, key, shape, dt, **kw):
+        def get(tag, key, shape, dt):
             if key not in T:
-                pool = ps_tr if tag == "tr" else ps_mx if tag == "mx" else pools[bufs]
-                earlier = taken.setdefault(tag, [])
-                if len(earlier) >= bufs:
-                    for step in users(earlier[-bufs]):
-                        emit(step)
-                earlier.append(key)
-                T[key] = pool.tile(shape, dt, name=tag, **kw)
+                if tag == "tr":
+                    T[key] = ps_tr.tile(shape, dt, name=tag)
+                elif tag == "mx":
+                    T[key] = ps_mx.tile(shape, dt, name=tag)
+                else:
+                    T[key] = sb.tile(shape, dt, name=tag, bufs=BUFS.get(tag, 1), align_bytes=64)
             return T[key]
 
         def rows(ap):
             return ap.rearrange("(p i) c -> p i c", i=TILES)
 
-        ident = keep.tile([P, P], F32, name="ident")
-        make_identity(nc, ident[:])
-        ident_bf = keep.tile([P, P], BF16, name="ident_bf")
-        make_identity(nc, ident_bf[:])
-
-        xs_t = keep.tile([P, PASSES, 4], F32, name="xs_t")
-        cf_c = keep.tile([P, TILES], BF16, name="cf_c")
-        pb_t = keep.tile([P, GROUPS, 4], BF16, name="pb_t")
-        ag_t = keep.tile([P, GROUPS, 4], BF16, name="ag_t")
-        lg_t = keep.tile([P, GROUPS, 4], BF16, name="lg_t")
-        cf_f = keep.tile([P, TILES], F32, name="cf_f")
-        lg_f = keep.tile([P, GROUPS, 4], F32, name="lg_f")
-        ag_f = keep.tile([P, GROUPS, 4], F32, name="ag_f")
-        lb_b = keep.tile([P, H], BF16, name="lb_b")
-        cf_b = keep.tile([P, CELLS], BF16, name="cf_b")
-        noise_t = keep.tile([P, TILES, LATENT], BF16, name="noise_t")
-
         def by_slot(vec):
             return vec.rearrange("(g p t) -> p g t", p=P, t=4)
 
+        ident = sb.tile([P, P], F32, name="ident")
+        make_identity(nc, ident[:])
+        ident_bf = sb.tile([P, P], BF16, name="ident_bf")
+        make_identity(nc, ident_bf[:])
+
+        xs_t = sb.tile([P, PASSES, 4], F32, name="xs_t")
+        cf_c = sb.tile([P, TILES], BF16, name="cf_c")
+        pb_t = sb.tile([P, GROUPS, 4], BF16, name="pb_t")
+        ag_t = sb.tile([P, GROUPS, 4], BF16, name="ag_t")
+        lg_t = sb.tile([P, GROUPS, 4], BF16, name="lg_t")
+        cf_f = sb.tile([P, TILES], F32, name="cf_f")
+        lg_f = sb.tile([P, GROUPS, 4], F32, name="lg_f")
+        ag_f = sb.tile([P, GROUPS, 4], F32, name="ag_f")
+        lb_b = sb.tile([P, LB_COLS], BF16, name="lb_b")
+        lb_c = sb.tile([P, 2, 2], BF16, name="lb_c")
+        cf_b = sb.tile([P, CELLS], BF16, name="cf_b")
+        noise_t = sb.tile([P, TILES, LATENT], BF16, name="noise_t")
+
         def load_x(i):
-            raw = get(4, "x_raw", ("x_raw", i), [P, GENES], U8)
+            raw = get("x_raw", ("x_raw", i), [P, GENES], U8)
             nc.sync.dma_start(out=raw[:], in_=rows(x_bytes)[:, i, :])
 
-        def load_unit(k, g):
+        def load_w(k, g):
             src = e if k == "e" else w[:, k * 512 : (k + 1) * 512]
-            raw = get(RAW_BUFS, "raw", ("raw", k, g), [P, 4, 512], BF16)
+            raw = get("raw", ("raw", k, g), [P, 4, 512], BF16)
             nc.sync.dma_start(out=raw[:], in_=src[g * 512 : (g + 1) * 512, :].rearrange("(p j) n -> p j n", j=4))
 
         def load_xs():
@@ -94,32 +90,39 @@ def tile_pathway_latent_encoder_f5_kernel(
 
         def load_small():
             nc.sync.dma_start(out=pb_t[:], in_=by_slot(pathway_bias))
-            nc.sync.dma_start(out=ag_t[:], in_=by_slot(activity_gain))
             nc.sync.dma_start(out=lg_t[:], in_=by_slot(loading_gain))
+            nc.sync.dma_start(out=ag_t[:], in_=by_slot(activity_gain))
 
         def load_late():
-            nc.sync.dma_start(out=lb_b[:], in_=latent_bias.partition_broadcast(P))
+            nc.sync.dma_start(out=lb_b[:], in_=latent_bias[0:LB_COLS].partition_broadcast(P))
             nc.sync.dma_start(out=noise_t[:], in_=rows(noise))
 
-        def CF():
-            bank = get(TR_BANKS, "tr", ("cf",), [P, CELLS], BF16)
-            for i in range(TILES):
-                nc.tensor.transpose(bank[:, i * P : (i + 1) * P], cf_c[:, i : i + 1].to_broadcast([P, P]), ident_bf[:])
+        def load_lbc():
+            with nc.allow_non_contiguous_dma(reason="one bias value for each partition"):
+                nc.sync.dma_start(out=lb_c[:, :, 0:1], in_=latent_bias[LATENT:H].rearrange("(h p o) -> p h o", h=2, o=1))
+
+        def CF(first, count):
+            bank = get("mx", ("cf", first), [P, count * P], BF16)
+            for i in range(count):
+                nc.tensor.transpose(bank[:, i * P : (i + 1) * P], cf_c[:, first + i : first + i + 1].to_broadcast([P, P]), ident_bf[:])
+            nc.scalar.copy(out=cf_b[:, first * P : (first + count) * P], in_=bank[:])
 
         def CC():
-            nc.scalar.copy(out=cf_b[:], in_=T["cf",][:])
             nc.scalar.copy(out=cf_f[:], in_=cf_c[:])
 
         def LC():
             nc.scalar.copy(out=lg_f[:], in_=lg_t[:])
+
+        def AC():
             nc.scalar.copy(out=ag_f[:], in_=ag_t[:])
 
-        def K(i):
-            xw = get(3, "xw", ("xw", i), [P, GENES], BF16)
-            nc.scalar.copy(out=xw[:], in_=T["x_raw", i][:].bitcast(F8))
+        def K(i, on="S"):
+            xw = get("xw", ("xw", i), [P, GENES], BF16)
+            copy = nc.scalar.copy if on == "S" else nc.vector.tensor_copy
+            copy(out=xw[:], in_=T["x_raw", i][:].bitcast(F8))
 
         def XT(pr, g):
-            bank = get(TR_BANKS, "tr", ("xt", pr, g), [P, 512], F32)
+            bank = get("tr", ("xt", pr, g), [P, 512], F32)
             for i2 in range(2):
                 words = T["xw", 2 * pr + i2][:].bitcast(F32)
                 for u in range(2):
@@ -127,18 +130,27 @@ def tile_pathway_latent_encoder_f5_kernel(
                         bank[:, u * 256 + i2 * P : u * 256 + (i2 + 1) * P], words[:, 256 * g + u : 256 * (g + 1) : 2], ident[:]
                     )
 
+        def x_part(pr, g):
+            return ((0, g), pr) if pr < 2 else ((pr, g // 2), g % 2)
+
+        def x_op(i, g, count):
+            key, half = x_part(i // 2, g)
+            first = half * 256 + i % 2 * P
+            return ("x",) + key, slice(first, first + count * P)
+
         def PP(pr, g):
-            xg = get(3, "xg", ("xg", pr, g // 2), [P, 2, 1024], BF16, align_bytes=64)
+            key, half = x_part(pr, g)
+            xg = get("xg", ("xg",) + key, [P, 2, 1024], BF16)
             nc.vector.tensor_tensor(
-                out=xg[:, g % 2, :].rearrange("p (m u e) -> p m u e", u=2, e=2),
+                out=xg[:, half, :].rearrange("p (m u e) -> p m u e", u=2, e=2),
                 in0=T["xt", pr, g][:].bitcast(BF16).rearrange("p (u m e) -> p m u e", u=2, e=2),
                 in1=xs_t[:, g, :].rearrange("p (u e) -> p u e", e=2).unsqueeze(1).to_broadcast([P, 256, 2, 2]),
                 op=ALU.mult,
             )
 
         def quantize(name, key, src, width):
-            c = get(1, name + "_c", ("codes",) + key, [P, width], U32, align_bytes=64)
-            s = get(1, name + "_s", ("scales",) + key, [P, width], U8, align_bytes=64)
+            c = get(name + "_c", ("codes",) + key, [P, width], U32)
+            s = get(name + "_s", ("scales",) + key, [P, width], U8)
             nc.vector.quantize_mx(out=c[:].bitcast(FP8X4), scales=s[:], in_=src)
 
         def mx(out, left, left_cols, right, right_cols, start, stop):
@@ -155,26 +167,25 @@ def tile_pathway_latent_encoder_f5_kernel(
         def XQ(pr, a):
             quantize(f"x{pr}{a}", ("x", pr, a), T["xg", pr, a][:].rearrange("p g c -> p (g c)"), 512)
 
-        def D(k, g, eng, lo=0, hi=4):
-            ring = "S" if (lo, hi) != (0, 4) else "G" if (k, g) == (0, 0) else eng
-            dst = get(GROUPED[ring], "grouped_" + ring, ("grouped", k, g), [P, 2048], BF16, align_bytes=64)
+        def D(k, g, eng, lo=0, hi=4, ring=None):
+            dst = get("grouped_" + (ring or eng), ("grouped", k, g), [P, 2048], BF16)
             raw = T["raw", k, g]
             out = dst[:, lo * 512 : hi * 512]
-            if eng in ("G", "H"):
+            if eng == "G":
                 if k == "e":
                     o = out.rearrange("p (c j) -> p c j", j=4)
                     i = raw[:, :, lo * P : hi * P].rearrange("p j c -> p c j")
                 else:
-                    o = out.rearrange("p (t m j) -> p m t j", m=P, j=4)
-                    i = raw[:].rearrange("p j (m t) -> p m t j", t=4)[:, :, lo:hi, :]
+                    o = out.rearrange("p (t m j) -> p t m j", m=P, j=4)
+                    i = raw[:].rearrange("p j (m t) -> p t m j", t=4)[:, lo:hi, :, :]
                 nc.gpsimd.tensor_scalar(out=o, in0=i, scalar1=1.0, scalar2=0.0, op0=ALU.mult, op1=ALU.add)
                 return
             if k == "e":
                 o = out.rearrange("p (c i j) -> p c j i", i=4, j=4)
                 i = raw[:, :, lo * P : hi * P].rearrange("p j (c i) -> p c j i", i=4)
             else:
-                o = out.rearrange("p (t m j) -> p m j t", m=P, j=4)
-                i = raw[:].rearrange("p j (m t) -> p m j t", t=4)[:, :, :, lo:hi]
+                o = out.rearrange("p (t c i j) -> p t c j i", c=P // 4, i=4, j=4)
+                i = raw[:].rearrange("p j (c i t) -> p t c j i", i=4, t=4)[:, lo:hi, :, :, :]
             if eng == "V":
                 nc.vector.tensor_copy(out=o, in_=i)
             else:
@@ -183,24 +194,27 @@ def tile_pathway_latent_encoder_f5_kernel(
         def WQ(k, g):
             quantize(f"w{k}{g}", ("w", k, g), T["grouped", k, g][:], 512)
 
-        def x_cols(g, first, count):
-            return slice((g % 2) * 256 + first, (g % 2) * 256 + first + count)
-
         def span(s):
             first, count = SPANS[s]
             return first, count, count * P, 4 // count
 
         def US(s, jg, b):
             first, count, width, per = span(s)
-            bank = get(8 - TR_BANKS, "mx", ("us", s, jg, b), [P, 512], F32)
+            bank = get("mx", ("us", s, jg, b), [P, 512], F32)
             for tt in range(per):
                 t = per * b + tt
                 for g in range(PASSES):
-                    mx(bank[:, tt * width : (tt + 1) * width], ("w", jg, g), slice(t * P, (t + 1) * P), ("x", first // 2, g // 2), x_cols(g, first % 2 * P, width), g == 0, g == PASSES - 1)
+                    mx(bank[:, tt * width : (tt + 1) * width], ("w", jg, g), slice(t * P, (t + 1) * P), *x_op(first, g, count), g == 0, g == PASSES - 1)
+
+        def UG(s, jg, g, start, stop):
+            first, count, width, per = span(s)
+            for t in range(4):
+                bank = get("mx", ("us", s, jg, t), [P, 512], F32)
+                mx(bank[:], ("w", jg, g), slice(t * P, (t + 1) * P), *x_op(first, g, count), start, stop)
 
         def C(s, jg, b):
             first, count, width, per = span(s)
-            y = get(RAW_BUFS, "y", ("y", s, jg), [P, 4, width], F32)
+            y = get(f"y{count}", ("y", s, jg), [P, 4, width], F32)
             nc.vector.tensor_tensor(
                 out=y[:, per * b : per * (b + 1), :],
                 in0=T["us", s, jg, b][:].rearrange("p (t m) -> p t m", t=per),
@@ -210,77 +224,80 @@ def tile_pathway_latent_encoder_f5_kernel(
 
         def UC(s, jg, i2):
             i = SPANS[s][0] + i2
-            bank = get(8 - TR_BANKS, "mx", ("uc", s, jg, i2), [P, 512], F32)
+            bank = get("mx", ("uc", s, jg, i2), [P, 512], F32)
             for g in range(PASSES):
-                mx(bank[:], ("x", i // 2, g // 2), x_cols(g, i % 2 * P, P), ("w", jg, g), slice(0, 512), g == 0, g == PASSES - 1)
+                mx(bank[:], *x_op(i, g, 1), ("w", jg, g), slice(0, 512), g == 0, g == PASSES - 1)
 
         def CS(s, jg, i2):
             first, count, width, per = span(s)
-            uy = get(4, "uy", ("uy", s, jg), [P, count, 512], F32)
+            uy = get("uy", ("uy", s, jg, i2), [P, 512], F32)
             i = first + i2
-            nc.scalar.activation(out=uy[:, i2, :], in_=T["uc", s, jg, i2][:], func=ACT.Copy, scale=cf_f[:, i : i + 1])
+            nc.scalar.activation(out=uy[:], in_=T["uc", s, jg, i2][:], func=ACT.Copy, scale=cf_f[:, i : i + 1])
 
-        def UT(s, jg, b):
+        def UT(s, jg):
             first, count, width, per = span(s)
-            bank = get(TR_BANKS, "tr", ("ut", s, jg, b), [P, 512], F32)
-            for tt in range(per):
-                t = per * b + tt
-                for i2 in range(count):
-                    nc.tensor.transpose(bank[:, tt * width + i2 * P : tt * width + (i2 + 1) * P], T["uy", s, jg][:, i2, t * P : (t + 1) * P], ident[:])
+            for b in range(count):
+                bank = get("tr", ("ut", s, jg, b), [P, 512], F32)
+                for tt in range(per):
+                    t = per * b + tt
+                    for i2 in range(count):
+                        nc.tensor.transpose(bank[:, tt * width + i2 * P : tt * width + (i2 + 1) * P], T["uy", s, jg, i2][:, t * P : (t + 1) * P], ident[:])
 
-        def SI(s, jg, b):
+        def SI(s, jg):
             first, count, width, per = span(s)
-            y = get(RAW_BUFS, "y", ("y", s, jg), [P, 4, width], F32)
-            for tt in range(per):
-                t = per * b + tt
-                src = T["ut", s, jg, b][:, tt * width : (tt + 1) * width] if (s, jg) in TURNED else y[:, t, :]
+            y = get(f"y{count}", ("y", s, jg), [P, 4, width], F32)
+            for t in range(4):
+                b, tt = divmod(t, per)
+                src = T["ut", s, jg, b][:, tt * width : (tt + 1) * width] if ("ut", s, jg, 0) in T else y[:, t, :]
                 nc.scalar.activation(out=y[:, t, :], in_=src, func=ACT.Silu, bias=pb_t[:, jg, t : t + 1])
 
-        def G(s, jg):
+        def G(s, jg, lo=0, hi=4):
             first, count, width, per = span(s)
-            dst = get(3, "ag", ("ag", s, jg), [P, 4 * width], BF16, align_bytes=64)
+            dst = get(f"ag{count}", ("ag", s, jg), [P, 4 * width], BF16)
+            a, b = lo * width // 4, hi * width // 4
             nc.vector.tensor_tensor(
-                out=dst[:].rearrange("p (c i t) -> p c t i", i=4, t=4),
-                in0=T["y", s, jg][:].rearrange("p t (c i) -> p c t i", i=4),
-                in1=ag_t[:, jg, :].unsqueeze(1).unsqueeze(3).to_broadcast([P, width // 4, 4, 4]),
+                out=dst[:, 4 * a : 4 * b].rearrange("p (c i t) -> p c t i", i=GAIN_RUN, t=4),
+                in0=T["y", s, jg][:, :, a:b].rearrange("p t (c i) -> p c t i", i=GAIN_RUN),
+                in1=ag_t[:, jg, :].unsqueeze(1).unsqueeze(3).to_broadcast([P, (b - a) // GAIN_RUN, 4, GAIN_RUN]),
                 op=ALU.mult,
             )
 
-        def GG(s, jg):
+        def GG(s, jg, lo=0, hi=4):
             first, count, width, per = span(s)
-            dst = get(3, "ag", ("ag", s, jg), [P, 4 * width], BF16, align_bytes=64)
+            dst = get(f"ag{count}", ("ag", s, jg), [P, 4 * width], BF16)
+            a, b = lo * width // 4, hi * width // 4
             nc.gpsimd.tensor_tensor(
-                out=dst[:].rearrange("p (c t) -> p c t", t=4),
-                in0=T["y", s, jg][:].rearrange("p t c -> p c t"),
-                in1=ag_f[:, jg, :].unsqueeze(1).to_broadcast([P, width, 4]),
+                out=dst[:, 4 * a : 4 * b].rearrange("p (c t) -> p c t", t=4),
+                in0=T["y", s, jg][:, :, a:b].rearrange("p t c -> p c t"),
+                in1=ag_t[:, jg, :].unsqueeze(1).to_broadcast([P, b - a, 4]),
                 op=ALU.mult,
             )
 
         def GS(s, jg):
             first, count, width, per = span(s)
-            planes = get(2, "planes", ("planes", s, jg), [P, 4, width], BF16)
+            planes = get("grouped_H", ("planes", s, jg), [P, 4, width], BF16)
             for t in range(4):
                 nc.scalar.activation(out=planes[:, t, :], in_=T["y", s, jg][:, t, :], func=ACT.Copy, scale=ag_f[:, jg, t : t + 1])
 
         def GI(s, jg):
             first, count, width, per = span(s)
-            dst = get(3, "ag", ("ag", s, jg), [P, 4 * width], BF16, align_bytes=64)
+            dst = get(f"ag{count}", ("ag", s, jg), [P, 4 * width], BF16)
             nc.vector.tensor_copy(out=dst[:].rearrange("p (c i t) -> p c t i", i=4, t=4), in_=T["planes", s, jg][:].rearrange("p t (c i) -> p c t i", i=4))
 
         def AQ(s, jg):
             quantize(f"a{s}{jg}", ("a", s, jg), T["ag", s, jg][:], SPANS[s][1] * P)
 
         def VM(jg, t):
-            bank = get(8 - TR_BANKS, "mx", ("v", jg, t), [P, 512], F32)
+            bank = get("mx", ("v", jg, t), [P, 512], F32)
             for g in range(PASSES):
                 mx(bank[:], ("w", jg, g), slice(t * P, (t + 1) * P), ("w", "e", g), slice(0, 512), g == 0, g == PASSES - 1)
 
         def VS(jg, t):
-            vl = get(2, "vl", ("vl", jg), [P, 4, H], BF16)
+            vl = get("vl", ("vl", jg), [P, 4, H], BF16)
             nc.scalar.activation(out=vl[:, t, :], in_=T["v", jg, t][:], func=ACT.Copy, scale=lg_f[:, jg, t : t + 1])
 
-        def VI(jg, on):
-            dst = get(GROUPED[on], "grouped_" + on, ("grouped", "v", jg), [P, 2048], BF16, align_bytes=64)
+        def VI(jg, on, ring=None):
+            dst = get("grouped_" + (ring or on), ("grouped", "v", jg), [P, 2048], BF16)
             if on == "G":
                 nc.gpsimd.tensor_scalar(
                     out=dst[:].rearrange("p (c t) -> p c t", t=4), in0=T["vl", jg][:].rearrange("p t c -> p c t"), scalar1=1.0, scalar2=0.0, op0=ALU.mult, op1=ALU.add
@@ -292,118 +309,108 @@ def tile_pathway_latent_encoder_f5_kernel(
         def VQ(jg):
             quantize(f"v{jg}", ("v", jg), T["grouped", "v", jg][:], H)
 
-        def span_of(i):
-            return [s for s, (first, count) in enumerate(SPANS) if first <= i < first + count][0]
+        def a_op(i, jg, count):
+            s = [n for n, (first, many) in enumerate(SPANS) if first <= i < first + many][0]
+            return ("a", s, jg), slice((i - SPANS[s][0]) * P, (i - SPANS[s][0] + count) * P)
 
-        def Q(i):
-            s = span_of(i)
-            i2 = i - SPANS[s][0]
-            bank = get(8 - TR_BANKS, "mx", ("q", i), [P, 512], F32)
-            for jg in range(GROUPS):
-                mx(bank[:], ("a", s, jg), slice(i2 * P, (i2 + 1) * P), ("v", jg), slice(0, H), jg == 0, jg == GROUPS - 1)
+        def tiles(o):
+            return slice(OUTS[o][0], OUTS[o][0] + OUTS[o][1])
 
-        def QB(i):
-            s = span_of(i)
-            qb = get(RAW_BUFS, "raw", ("qb", s), [P, SPANS[s][1], H], F32)
-            nc.vector.tensor_tensor(out=qb[:, i - SPANS[s][0], :], in0=T["q", i][:], in1=lb_b[:], op=ALU.add)
+        def ST(key, o):
+            out = {"mu": mu_out, "sd": sd_out, "z": z_out}[key]
+            nc.sync.dma_start(out=rows(out)[:, tiles(o), :], in_=T[key, o][:, :, 0:LATENT])
 
-        def tiles(s):
-            return slice(SPANS[s][0], SPANS[s][0] + SPANS[s][1])
+        def QM(o):
+            first, count = OUTS[o]
+            bank = get("mx", ("qm", o), [P, count, LATENT], F32)
+            for i2 in range(count):
+                for jg in range(GROUPS):
+                    mx(bank[:, i2, :], *a_op(first + i2, jg, 1), ("v", jg), slice(0, LATENT), jg == 0, jg == GROUPS - 1)
 
-        def store(out, key, s):
-            nc.sync.dma_start(out=rows(out)[:, tiles(s), :], in_=T[key, s][:, :, 0:LATENT])
+        def MB(o):
+            first, count = OUTS[o]
+            mu = get("raw", ("mu", o), [P, count, LATENT], F32)
+            nc.vector.tensor_tensor(out=mu[:], in0=T["qm", o][:], in1=lb_b[:, 0:LATENT].unsqueeze(1).to_broadcast([P, count, LATENT]), op=ALU.add)
 
-        def SMU(s):
-            store(mu_out, "qb", s)
+        def QL(o, tag="mx"):
+            first, count = OUTS[o]
+            bank = get(tag, ("ql", o), [P, 2, count * P], F32)
+            for h in range(2):
+                for jg in range(GROUPS):
+                    mx(bank[:, h, :], ("v", jg), slice(LATENT + h * P, LATENT + (h + 1) * P), *a_op(first, jg, count), jg == 0, jg == GROUPS - 1)
 
-        def SSD(s):
-            store(sd_out, "sd", s)
+        def TL(o):
+            first, count = OUTS[o]
+            th = get("uy", ("th", o), [P, 2, count * P], F32)
+            for h in range(2):
+                nc.scalar.activation(out=th[:, h, :], in_=T["ql", o][:, h, :], func=ACT.Tanh, bias=lb_c[:, h, 0:1])
 
-        def SZ(s):
-            store(z_out, "z", s)
+        def LT(o, tag="tr"):
+            first, count = OUTS[o]
+            bank = get(tag, ("lt", o), [P, count, LATENT], F32)
+            for i2 in range(count):
+                for h in range(2):
+                    nc.tensor.transpose(bank[:, i2, h * P : (h + 1) * P], T["th", o][:, h, i2 * P : (i2 + 1) * P], ident[:])
 
-        def TH(s):
-            sd = get(1, f"sd{s}", ("sd", s), [P, SPANS[s][1], LATENT], F32)
-            nc.scalar.activation(out=sd[:], in_=T["qb", s][:, :, LATENT:H], func=ACT.Tanh)
+        def EL(o):
+            sd = get("xw" if o < 4 else "raw", ("sd", o), [P, OUTS[o][1], LATENT], F32)
+            nc.scalar.activation(out=sd[:], in_=T["lt", o][:], func=ACT.Exp, scale=0.5)
 
-        def EX(s):
-            sd = T["sd", s]
-            nc.scalar.activation(out=sd[:], in_=sd[:], func=ACT.Exp, scale=0.5)
-
-        def ZM(s, on):
+        def ZM(o, on="V"):
             eng = nc.vector if on == "V" else nc.gpsimd
-            z = get(1, f"z{s}", ("z", s), [P, SPANS[s][1], LATENT], F32)
-            eng.tensor_tensor(out=z[:], in0=T["sd", s][:], in1=noise_t[:, tiles(s), :], op=ALU.mult)
+            z = get("xg" if o < 4 else "grouped_S", ("z", o), [P, OUTS[o][1], LATENT], F32)
+            eng.tensor_tensor(out=z[:], in0=T["sd", o][:], in1=noise_t[:, tiles(o), :], op=ALU.mult)
 
-        def ZA(s, on):
+        def ZA(o, on="V"):
             eng = nc.vector if on == "V" else nc.gpsimd
-            z = T["z", s]
-            eng.tensor_tensor(out=z[:], in0=z[:], in1=T["qb", s][:, :, 0:LATENT], op=ALU.add)
+            z = T["z", o]
+            eng.tensor_tensor(out=z[:], in0=z[:], in1=T["mu", o][:, :, 0:LATENT], op=ALU.add)
 
-        def touches(name, *a):
-            pr, jg = a[0] if a else None, a[1] if len(a) > 1 else None
-            banks = range(SPANS[pr][1]) if name in ("US", "UC", "UT", "G", "GG", "GS", "TH", "SMU") else ()
-            x_done = [("XQ", SPANS[pr][0] // 2, half) for half in range(2)] if banks else []
-            w_done = [("WQ", jg, g) for g in range(PASSES)]
-            turned = (pr, jg) in TURNED
-            return {
-                "K": lambda: ([("x_raw", pr), ("xw", pr)], [("load_x", pr)]),
-                "XT": lambda: ([("xw", 2 * pr), ("xw", 2 * pr + 1)], [("K", 2 * pr), ("K", 2 * pr + 1)]),
-                "PP": lambda: ([("xt", pr, jg), ("xg", pr, jg // 2)], [("XT", pr, jg), ("load_xs",)]),
-                "XQ": lambda: ([("xg", pr, jg)], [("PP", pr, 2 * jg), ("PP", pr, 2 * jg + 1)]),
-                "D": lambda: ([("raw", pr, jg), ("grouped", pr, jg)], [("load_unit", pr, jg)]),
-                "WQ": lambda: ([("grouped", pr, jg)], [s for s in steps if s[:3] == ("D", pr, jg)]),
-                "CF": lambda: ([], [("load_cf",)]),
-                "LC": lambda: ([], [("load_small",)]),
-                "CC": lambda: ([("cf",)], [("CF",)]),
-                "US": lambda: ([], x_done + w_done),
-                "UC": lambda: ([], x_done + w_done),
-                "C": lambda: ([("us",) + a, ("y", pr, jg)], [("US",) + a, ("CC",)]),
-                "CS": lambda: ([("uc",) + a, ("uy", pr, jg)], [("UC",) + a, ("CC",)]),
-                "UT": lambda: ([("uy", pr, jg)], [("CS", pr, jg, b) for b in banks]),
-                "SI": lambda: ([("ut",) + a, ("y", pr, jg)], [("UT" if turned else "C",) + a, ("load_small",)]),
-                "G": lambda: ([("y", pr, jg)], [("SI", pr, jg, b) for b in banks]),
-                "GG": lambda: ([("y", pr, jg)], [("SI", pr, jg, b) for b in banks] + [("LC",)]),
-                "GS": lambda: ([("y", pr, jg)], [("SI", pr, jg, b) for b in banks]),
-                "GI": lambda: ([("planes", pr, jg)], [("GS", pr, jg)]),
-                "AQ": lambda: ([("ag", pr, jg)], [s for s in steps if s in (("G", pr, jg), ("GI", pr, jg), ("GG", pr, jg))]),
-                "VM": lambda: ([], [("WQ", k, g) for k in (pr, "e") for g in range(PASSES)]),
-                "VS": lambda: ([("v",) + a, ("vl", pr)], [("VM",) + a, ("LC",)]),
-                "VI": lambda: ([("vl", pr)], [("VS", pr, t) for t in range(4)]),
-                "VQ": lambda: ([("grouped", "v", pr)], [s for s in steps if s[:2] == ("VI", pr)]),
-                "Q": lambda: ([], [("AQ", span_of(pr), g) for g in range(GROUPS)] + [("VQ", g) for g in range(GROUPS)]),
-                "QB": lambda: ([("q", pr), ("qb", span_of(pr))], [("Q", pr), ("load_late",)]),
-                "TH": lambda: ([("qb", pr)], [("QB", SPANS[pr][0] + b) for b in banks]),
-                "SMU": lambda: ([("qb", pr)], [("QB", SPANS[pr][0] + b) for b in banks]),
-                "EX": lambda: ([("sd", pr)], [("TH", pr)]),
-                "SSD": lambda: ([("sd", pr)], [("EX", pr)]),
-                "ZM": lambda: ([("sd", pr)], [("EX", pr)]),
-                "ZA": lambda: ([("z", pr), ("qb", pr)], [s for s in steps if s[:2] == ("ZM", pr)]),
-                "SZ": lambda: ([("z", pr)], [s for s in steps if s[:2] == ("ZA", pr)]),
-            }.get(name, lambda: ([], []))()
 
-        calls = dict(GG=GG, GS=GS, GI=GI, load_cf=load_cf, LC=LC, load_x=load_x, load_unit=load_unit, load_xs=load_xs, load_small=load_small, load_late=load_late, K=K, XT=XT, PP=PP, XQ=XQ, D=D, WQ=WQ, CF=CF, CC=CC, US=US, UC=UC, C=C, CS=CS, UT=UT, SI=SI, G=G, AQ=AQ, VM=VM, VS=VS, VI=VI, VQ=VQ, Q=Q, QB=QB, TH=TH, EX=EX, ZM=ZM, ZA=ZA, SMU=SMU, SSD=SSD, SZ=SZ)
-        queues = [
-            [("load_x", 0), ("load_cf",), ("load_unit", 0,0), ("load_x", 1), ("load_xs",), ("load_unit", 0,1), ("load_unit", 0,2), ("load_unit", 0,3), ("load_x", 2), ("load_x", 3), ("load_unit", "e",0), ("load_small",), ("load_unit", "e",3), ("load_unit", "e",1), ("load_x", 4), ("load_x", 5), ("load_unit", "e",2), ("load_x", 6), ("load_unit", 1,0), ("load_unit", 1,2), ("load_x", 7), ("load_unit", 1,3), ("load_unit", 1,1), ("load_late",), ("SMU", 0), ("SMU", 1), ("SSD", 0), ("SSD", 1), ("SMU", 2), ("SMU", 3), ("SZ", 0), ("SSD", 2), ("SMU", 4), ("SSD", 3), ("SZ", 1), ("SSD", 4), ("SZ", 2), ("SZ", 3), ("SZ", 4)],
-            [("D", 0,3,"G"), ("D", "e",3,"G"), ("D", 1,2,"G"), ("D", 1,3,"H"), ("VI", 0,"G"), ("VI", 1,"G"), ("ZM", 0,"G"), ("ZA", 0,"G")],
-            [("CF",), ("XT", 0,0), ("XT", 0,1), ("XT", 0,2), ("XT", 0,3), ("XT", 1,0), ("XT", 1,1), ("XT", 1,2), ("XT", 1,3), ("US", 0,0,0), ("XT", 2,0), ("XT", 2,1), ("US", 0,0,1), ("XT", 2,2), ("XT", 2,3), ("US", 1,0,0), ("US", 1,0,1), ("VM", 0,0), ("VM", 0,1), ("VM", 0,2), ("XT", 3,0), ("XT", 3,1), ("VM", 0,3), ("XT", 3,2), ("XT", 3,3), ("US", 2,0,0), ("US", 2,0,1), ("VM", 1,0), ("VM", 1,1), ("VM", 1,2), ("VM", 1,3), ("US", 0,1,0), ("US", 0,1,1), ("UC", 1,1,0), ("UC", 1,1,1), ("UC", 2,1,0), ("UC", 2,1,1), ("UT", 1,1,0), ("UT", 1,1,1), ("US", 3,0,0), ("US", 3,1,0), ("UT", 2,1,0), ("UT", 2,1,1), ("Q", 0), ("Q", 1), ("US", 4,0,0), ("US", 4,1,0), ("Q", 2), ("Q", 3), ("Q", 4), ("Q", 5), ("Q", 6), ("Q", 7)],
-            [("K", 0), ("CC",), ("K", 1), ("D", 0,2,"S"), ("K", 2), ("K", 3), ("D", "e",0,"S"), ("K", 4), ("K", 5), ("D", "e",1,"S"), ("D", "e",2,"S"), ("K", 6), ("D", 1,0,"S"), ("K", 7), ("D", 1,1,"S"), ("LC",), ("VS", 0,0), ("VS", 0,1), ("VS", 0,2), ("VS", 0,3), ("SI", 0,0,0), ("SI", 0,0,1), ("SI", 1,0,0), ("SI", 1,0,1), ("GS", 0,0), ("VS", 1,0), ("VS", 1,1), ("VS", 1,2), ("VS", 1,3), ("GS", 1,0), ("SI", 2,0,0), ("SI", 2,0,1), ("SI", 0,1,0), ("SI", 0,1,1), ("CS", 1,1,0), ("CS", 1,1,1), ("GS", 2,0), ("CS", 2,1,0), ("CS", 2,1,1), ("SI", 1,1,0), ("SI", 1,1,1), ("GS", 1,1), ("SI", 3,0,0), ("SI", 3,1,0), ("SI", 2,1,0), ("SI", 2,1,1), ("GS", 2,1), ("TH", 0), ("SI", 4,0,0), ("SI", 4,1,0), ("EX", 0), ("TH", 1), ("EX", 1), ("TH", 2), ("EX", 2), ("TH", 3), ("EX", 3), ("TH", 4), ("EX", 4)],
-            [("D", 0,0,"V"), ("WQ", 0,0), ("D", 0,1,"V"), ("PP", 0,0), ("PP", 0,1), ("PP", 0,2), ("PP", 0,3), ("WQ", 0,1), ("XQ", 0,0), ("WQ", 0,2), ("XQ", 0,1), ("WQ", 0,3), ("PP", 1,0), ("PP", 1,1), ("PP", 1,2), ("PP", 1,3), ("XQ", 1,0), ("XQ", 1,1), ("WQ", "e",0), ("WQ", "e",1), ("WQ", "e",2), ("WQ", "e",3), ("C", 0,0,0), ("C", 0,0,1), ("PP", 2,0), ("C", 1,0,0), ("C", 1,0,1), ("PP", 2,1), ("PP", 2,2), ("PP", 2,3), ("XQ", 2,0), ("XQ", 2,1), ("WQ", 1,0), ("WQ", 1,1), ("WQ", 1,3), ("WQ", 1,2), ("PP", 3,0), ("C", 2,0,0), ("C", 2,0,1), ("PP", 3,1), ("GI", 0,0), ("AQ", 0,0), ("VQ", 0), ("PP", 3,2), ("C", 0,1,0), ("C", 0,1,1), ("PP", 3,3), ("GI", 1,0), ("XQ", 3,0), ("XQ", 3,1), ("VQ", 1), ("AQ", 1,0), ("G", 0,1), ("GI", 2,0), ("AQ", 0,1), ("AQ", 2,0), ("C", 3,0,0), ("GI", 1,1), ("C", 3,1,0), ("AQ", 1,1), ("QB", 0), ("QB", 1), ("G", 3,0), ("G", 3,1), ("C", 4,0,0), ("AQ", 3,0), ("C", 4,1,0), ("AQ", 3,1), ("GI", 2,1), ("QB", 2), ("QB", 3), ("AQ", 2,1), ("G", 4,0), ("G", 4,1), ("AQ", 4,0), ("AQ", 4,1), ("QB", 4), ("QB", 5), ("QB", 6), ("QB", 7), ("ZM", 1,"V"), ("ZM", 2,"V"), ("ZA", 1,"V"), ("ZA", 2,"V"), ("ZM", 3,"V"), ("ZM", 4,"V"), ("ZA", 3,"V"), ("ZA", 4,"V")],
-        ]
-        steps = [s for queue in queues for s in queue]
-        done = set()
+        load_x(0); load_x(1); load_xs(); load_x(2); load_x(3); load_w(0, 0); load_w(0, 1); load_x(4); load_w(0, 2); load_x(5); load_w(0, 3); load_cf()
+        load_w("e", 0); load_w("e", 1); load_w("e", 2)
+        K(0); K(1, "V"); K(2); K(3)
+        D(0, 0, "G"); D(0, 1, "S"); D(0, 2, "G", ring="H")
+        load_w("e", 3); load_small()
+        for pr in range(2):
+            for g in range(4): XT(pr, g); PP(pr, g)
+        K(4); K(5); D(0, 3, "S"); D("e", 0, "G", 0, 2, ring="I")
+        CF(0, 8); CC()
+        for g in range(4): XT(2, g)
+        D("e", 1, "S"); D("e", 2, "S")
+        load_w(1, 0); load_w(1, 1); load_w(1, 2)
+        for g in range(4): XQ(0, g); WQ(0, g); UG(0, 0, g, g == 0, g == 3)
+        D("e", 3, "S"); D("e", 0, "V", 2, 4)
+        load_w(1, 3); load_x(6); load_x(7); load_late(); load_lbc()
+        WQ("e", 1); WQ("e", 2); WQ("e", 3); WQ("e", 0)
+        D(1, 0, "G", ring="I"); D(1, 1, "S"); D(1, 2, "G"); LC(); AC(); K(6); K(7); D(1, 3, "S")
+        for t in range(4): C(0, 0, t)
+        for g in range(4): PP(2, g)
+        VM(0, 0); VM(0, 1); VM(0, 2); XT(3, 0); XT(3, 1); VM(0, 3); XT(3, 2); XT(3, 3)
+        for t in range(4): VS(0, t)
+        for g in (1, 2, 3, 0): WQ(1, g); UG(0, 1, g, g == 1, g == 0)
+        XQ(2, 0); XQ(2, 1)
+        VI(0, "G", ring="I")
+        SI(0, 0)
+        PP(3, 0); PP(3, 1)
+        for t in range(4): C(0, 1, t)
+        PP(3, 2); PP(3, 3)
 
-        def users(key):
-            return [s for s in steps if key in touches(*s)[0]]
-
-        def emit(step):
-            queue = [qu for qu in queues if step in qu][0]
-            for s in queue[: queue.index(step) + 1]:
-                if s not in done:
-                    done.add(s)
-                    for need in touches(*s)[1]:
-                        emit(need)
-                    calls[s[0]](*s[1:])
-
-        for step in steps:
-            emit(step)
+        GG(0, 0, 0, 3)
+        for t in range(4): VM(1, t)
+        SI(0, 1)
+        for t in range(4): VS(1, t)
+        GS(0, 1)
+        US(1, 0, 0); US(1, 0, 1)
+        XQ(3, 0); VQ(0); XQ(3, 1); G(0, 0, 3, 4); C(1, 0, 0); AQ(0, 0); C(1, 0, 1); VI(1, "V"); GI(0, 1); VQ(1); AQ(0, 1)
+        UC(1, 1, 0); CS(1, 1, 0); UC(1, 1, 1); CS(1, 1, 1); SI(1, 0)
+        UC(2, 0, 0); CS(2, 0, 0); UT(1, 1); UC(2, 1, 0); SI(1, 1); CS(2, 1, 0)
+        G(1, 0)
+        US(3, 0, 0); UT(2, 0); UT(2, 1); US(3, 1, 0); SI(2, 0); SI(2, 1)
+        G(1, 1); AQ(1, 0); C(3, 0, 0); AQ(1, 1); C(3, 1, 0); SI(3, 0)
+        QL(0); TL(0); SI(3, 1); QM(0); QM(1); QL(1); TL(1); LT(0); QL(2, "tr"); QM(2)
+        G(2, 0); G(2, 1); G(3, 0); AQ(2, 0); AQ(2, 1); G(3, 1); MB(0); ST("mu", 0); AQ(3, 0); AQ(3, 1); MB(1); ST("mu", 1); MB(2); ST("mu", 2)
+        LT(1); QL(3); QL(4, "tr"); QM(3); EL(0); EL(1); TL(2); TL(3); TL(4); QM(4); LT(2); LT(3); LT(4); EL(2); EL(3); EL(4)
+        ST("sd", 0); ST("sd", 1)
+        ZM(0); ZM(1); ZA(0); ST("z", 0); MB(3); ZA(1); ST("mu", 3); ST("sd", 2); ST("z", 1); MB(4); ST("sd", 3); ST("sd", 4); ST("mu", 4)
+        ZM(2); ZM(3); ZA(2); ST("z", 2); ZM(4); ZA(3); ST("z", 3); ZA(4); ST("z", 4)

@@ -25,7 +25,7 @@ LB_COLS = LATENT
 GAIN_RUN = 2
 SPANS = [(0, 4), (4, 2), (6, 1), (7, 1)]
 OUTS = [(0, 2), (2, 2), (4, 2), (6, 1), (7, 1)]
-BUFS = {"x_raw": 5, "raw": 7, "xw": 4, "xg": 4, "grouped_S": 4, "y4": 2, "y2": 2, "y1": 4, "uy": 4, "ag4": 2, "ag2": 2, "ag1": 4}
+BUFS = {"x_raw": 6, "raw": 7, "xw": 4, "xg": 4, "grouped_S": 4, "y4": 2, "y2": 2, "y1": 4, "uy": 4, "ag4": 2, "ag2": 2, "ag1": 4}
 
 
 def tile_pathway_latent_encoder_f5_kernel(
@@ -388,21 +388,21 @@ def tile_pathway_latent_encoder_f5_kernel(
         for g in range(4): PP(2, g)
         VM(0, 0); VM(0, 1); VM(0, 2); XT(3, 0); XT(3, 1); VM(0, 3); XT(3, 2); XT(3, 3)
         for t in range(4): VS(0, t)
-        for g in (1, 2, 3, 0): WQ(1, g); UG(0, 1, g, g == 1, g == 0)
-        XQ(2, 0); XQ(2, 1)
+        for g in (1, 2, 3): WQ(1, g); UG(0, 1, g, g == 1, False)
+        XQ(2, 0); XQ(2, 1); WQ(1, 0); UG(0, 1, 0, False, True)
         VI(0, "G", ring="I")
         SI(0, 0)
         PP(3, 0); PP(3, 1)
         for t in range(4): C(0, 1, t)
         PP(3, 2); PP(3, 3)
 
-        GG(0, 0, 0, 3)
+        GG(0, 0, 0, 2)
         for t in range(4): VM(1, t)
         SI(0, 1)
         for t in range(4): VS(1, t)
         GS(0, 1)
         US(1, 0, 0); US(1, 0, 1)
-        XQ(3, 0); VQ(0); XQ(3, 1); G(0, 0, 3, 4); C(1, 0, 0); AQ(0, 0); C(1, 0, 1); VI(1, "V"); GI(0, 1); VQ(1); AQ(0, 1)
+        XQ(3, 0); VQ(0); XQ(3, 1); G(0, 0, 2, 4); C(1, 0, 0); AQ(0, 0); C(1, 0, 1); VI(1, "V"); GI(0, 1); VQ(1); AQ(0, 1)
         UC(1, 1, 0); CS(1, 1, 0); UC(1, 1, 1); CS(1, 1, 1); SI(1, 0)
         UC(2, 0, 0); CS(2, 0, 0); UT(1, 1); UC(2, 1, 0); SI(1, 1); CS(2, 1, 0)
         G(1, 0)

@@ -22,7 +22,7 @@ PAIRS = TILES // 2
 FLOPS = 2 * CELLS * GENES * PATHWAYS + 2 * GENES * PATHWAYS * H + 2 * CELLS * PATHWAYS * H
 TR_BANKS = 4
 LB_COLS = LATENT
-GAIN_RUN = 2
+GAIN_RUN = 4
 SPANS = [(0, 4), (4, 2), (6, 1), (7, 1)]
 OUTS = [(0, 2), (2, 2), (4, 2), (6, 1), (7, 1)]
 BUFS = {"x_raw": 6, "raw": 7, "xw": 4, "xg": 4, "grouped_S": 4, "y4": 2, "y2": 2, "y1": 4, "uy": 4, "ag4": 2, "ag2": 2, "ag1": 4}
@@ -176,8 +176,8 @@ def tile_pathway_latent_encoder_f5_kernel(
                     o = out.rearrange("p (c j) -> p c j", j=4)
                     i = raw[:, :, lo * P : hi * P].rearrange("p j c -> p c j")
                 else:
-                    o = out.rearrange("p (t m j) -> p t m j", m=P, j=4)
-                    i = raw[:].rearrange("p j (m t) -> p t m j", t=4)[:, lo:hi, :, :]
+                    o = out.rearrange("p (t m j) -> p m t j", m=P, j=4)
+                    i = raw[:].rearrange("p j (m t) -> p m t j", t=4)[:, :, lo:hi, :]
                 nc.gpsimd.tensor_scalar(out=o, in0=i, scalar1=1.0, scalar2=0.0, op0=ALU.mult, op1=ALU.add)
                 return
             if k == "e":

@@ -23,9 +23,9 @@ FLOPS = 2 * CELLS * GENES * PATHWAYS + 2 * GENES * PATHWAYS * H + 2 * CELLS * PA
 TR_BANKS = 4
 LB_COLS = LATENT
 GAIN_RUN = 4
-SPANS = [(0, 4), (4, 2), (6, 1), (7, 1)]
+SPANS = [(0, 4), (4, 2), (6, 2)]
 OUTS = [(0, 2), (2, 2), (4, 2), (6, 1), (7, 1)]
-BUFS = {"x_raw": 6, "raw": 7, "xw": 4, "xg": 4, "grouped_S": 4, "y4": 2, "y2": 2, "y1": 4, "uy": 4, "ag4": 2, "ag2": 2, "ag1": 4}
+BUFS = {"x_raw": 3, "raw": 4, "xw": 4, "xg": 4, "grouped_S": 4, "y4": 2, "y2": 4, "uy": 4, "ag4": 1, "ag2": 3, "vl": 1, "planes": 1}
 
 
 def tile_pathway_latent_encoder_f5_kernel(
@@ -71,16 +71,21 @@ def tile_pathway_latent_encoder_f5_kernel(
         lb_b = sb.tile([P, LB_COLS], BF16, name="lb_b")
         lb_c = sb.tile([P, 2, 2], BF16, name="lb_c")
         cf_b = sb.tile([P, CELLS], BF16, name="cf_b")
-        noise_t = sb.tile([P, TILES, LATENT], BF16, name="noise_t")
 
-        def load_x(i):
-            raw = get("x_raw", ("x_raw", i), [P, GENES], U8)
-            nc.sync.dma_start(out=raw[:], in_=rows(x_bytes)[:, i, :])
+        def load_x(pr, lo=0, hi=PASSES):
+            raw = get("x_raw", ("x_raw", pr, lo), [P, 2, (hi - lo) * 512], U8)
+            nc.sync.dma_start(out=raw[:], in_=rows(x_bytes)[:, 2 * pr : 2 * pr + 2, lo * 512 : hi * 512])
 
-        def load_w(k, g):
-            src = e if k == "e" else w[:, k * 512 : (k + 1) * 512]
-            raw = get("raw", ("raw", k, g), [P, 4, 512], BF16)
-            nc.sync.dma_start(out=raw[:], in_=src[g * 512 : (g + 1) * 512, :].rearrange("(p j) n -> p j n", j=4))
+        def load_w(g):
+            raw = get("raw", ("raw", g), [P, 4, PATHWAYS], BF16)
+            nc.sync.dma_start(out=raw[:], in_=w[g * 512 : (g + 1) * 512, :].rearrange("(p j) n -> p j n", j=4))
+
+        def load_e(g):
+            raw = get("raw", ("raw", "e", g // 2), [P, 2, 4, H], BF16)
+            nc.sync.dma_start(out=raw[:, g % 2, :, :], in_=e[g * 512 : (g + 1) * 512, :].rearrange("(p j) n -> p j n", j=4))
+
+        def raw_of(k, g):
+            return T["raw", "e", g // 2][:, g % 2, :, :] if k == "e" else T["raw", g][:, :, k * 512 : (k + 1) * 512]
 
         def load_xs():
             nc.sync.dma_start(out=xs_t[:], in_=by_slot(x_scale.rearrange("o k -> (o k)")))
@@ -95,7 +100,9 @@ def tile_pathway_latent_encoder_f5_kernel(
 
         def load_late():
             nc.sync.dma_start(out=lb_b[:], in_=latent_bias[0:LB_COLS].partition_broadcast(P))
-            nc.sync.dma_start(out=noise_t[:], in_=rows(noise))
+
+        def load_noise():
+            nc.sync.dma_start(out=get("raw", "noise", [P, TILES, LATENT], BF16)[:], in_=rows(noise))
 
         def load_lbc():
             with nc.allow_non_contiguous_dma(reason="one bias value for each partition"):
@@ -104,10 +111,10 @@ def tile_pathway_latent_encoder_f5_kernel(
         def CF(first, count):
             bank = get("mx", ("cf", first), [P, count * P], BF16)
             for i in range(count):
-                nc.tensor.transpose(bank[:, i * P : (i + 1) * P], cf_c[:, first + i : first + i + 1].to_broadcast([P, P]), ident_bf[:])
-            nc.scalar.copy(out=cf_b[:, first * P : (first + count) * P], in_=bank[:])
+                nc.tensor.matmul(bank[:, i * P : (i + 1) * P], lhsT=cf_c[:, first + i : first + i + 1].to_broadcast([P, P]), rhs=ident_bf[:], start=True, stop=True)
 
         def CC():
+            nc.vector.tensor_copy(out=cf_b[:], in_=T["cf", 0][:])
             nc.scalar.copy(out=cf_f[:], in_=cf_c[:])
 
         def LC():
@@ -116,13 +123,13 @@ def tile_pathway_latent_encoder_f5_kernel(
         def AC():
             nc.scalar.copy(out=ag_f[:], in_=ag_t[:])
 
-        def K(i, on="S"):
+        def K(i, on="S", lo=0, hi=PASSES):
             xw = get("xw", ("xw", i), [P, GENES], BF16)
             copy = nc.scalar.copy if on == "S" else nc.vector.tensor_copy
-            copy(out=xw[:], in_=T["x_raw", i][:].bitcast(F8))
+            copy(out=xw[:, lo * 512 : hi * 512], in_=T["x_raw", i // 2, lo][:, i % 2, :].bitcast(F8))
 
-        def XT(pr, g):
-            bank = get("tr", ("xt", pr, g), [P, 512], F32)
+        def XT(pr, g, tag="tr"):
+            bank = get(tag, ("xt", pr, g), [P, 512], F32)
             for i2 in range(2):
                 words = T["xw", 2 * pr + i2][:].bitcast(F32)
                 for u in range(2):
@@ -169,7 +176,7 @@ def tile_pathway_latent_encoder_f5_kernel(
 
         def D(k, g, eng, lo=0, hi=4, ring=None):
             dst = get("grouped_" + (ring or eng), ("grouped", k, g), [P, 2048], BF16)
-            raw = T["raw", k, g]
+            raw = raw_of(k, g)
             out = dst[:, lo * 512 : hi * 512]
             if eng == "G":
                 if k == "e":
@@ -177,7 +184,7 @@ def tile_pathway_latent_encoder_f5_kernel(
                     i = raw[:, :, lo * P : hi * P].rearrange("p j c -> p c j")
                 else:
                     o = out.rearrange("p (t m j) -> p m t j", m=P, j=4)
-                    i = raw[:].rearrange("p j (m t) -> p m t j", t=4)[:, :, lo:hi, :]
+                    i = raw.rearrange("p j (m t) -> p m t j", t=4)[:, :, lo:hi, :]
                 nc.gpsimd.tensor_scalar(out=o, in0=i, scalar1=1.0, scalar2=0.0, op0=ALU.mult, op1=ALU.add)
                 return
             if k == "e":
@@ -185,7 +192,7 @@ def tile_pathway_latent_encoder_f5_kernel(
                 i = raw[:, :, lo * P : hi * P].rearrange("p j (c i) -> p c j i", i=4)
             else:
                 o = out.rearrange("p (t c i j) -> p t c j i", c=P // 4, i=4, j=4)
-                i = raw[:].rearrange("p j (c i t) -> p t c j i", i=4, t=4)[:, lo:hi, :, :, :]
+                i = raw.rearrange("p j (c i t) -> p t c j i", i=4, t=4)[:, lo:hi, :, :, :]
             if eng == "V":
                 nc.vector.tensor_copy(out=o, in_=i)
             else:
@@ -198,18 +205,18 @@ def tile_pathway_latent_encoder_f5_kernel(
             first, count = SPANS[s]
             return first, count, count * P, 4 // count
 
-        def US(s, jg, b):
+        def US(s, jg, b, tag="mx"):
             first, count, width, per = span(s)
-            bank = get("mx", ("us", s, jg, b), [P, 512], F32)
+            bank = get(tag, ("us", s, jg, b), [P, 512], F32)
             for tt in range(per):
                 t = per * b + tt
                 for g in range(PASSES):
                     mx(bank[:, tt * width : (tt + 1) * width], ("w", jg, g), slice(t * P, (t + 1) * P), *x_op(first, g, count), g == 0, g == PASSES - 1)
 
-        def UG(s, jg, g, start, stop):
+        def UG(s, jg, g, start, stop, tag="mx"):
             first, count, width, per = span(s)
             for t in range(4):
-                bank = get("mx", ("us", s, jg, t), [P, 512], F32)
+                bank = get(tag, ("us", s, jg, t), [P, 512], F32)
                 mx(bank[:], ("w", jg, g), slice(t * P, (t + 1) * P), *x_op(first, g, count), start, stop)
 
         def C(s, jg, b):
@@ -222,31 +229,10 @@ def tile_pathway_latent_encoder_f5_kernel(
                 op=ALU.mult,
             )
 
-        def UC(s, jg, i2):
-            i = SPANS[s][0] + i2
-            bank = get("mx", ("uc", s, jg, i2), [P, 512], F32)
-            for g in range(PASSES):
-                mx(bank[:], *x_op(i, g, 1), ("w", jg, g), slice(0, 512), g == 0, g == PASSES - 1)
-
-        def CS(s, jg, i2):
-            first, count, width, per = span(s)
-            uy = get("uy", ("uy", s, jg, i2), [P, 512], F32)
-            i = first + i2
-            nc.scalar.activation(out=uy[:], in_=T["uc", s, jg, i2][:], func=ACT.Copy, scale=cf_f[:, i : i + 1])
-
-        def UT(s, jg):
-            first, count, width, per = span(s)
-            for b in range(count):
-                bank = get("tr", ("ut", s, jg, b), [P, 512], F32)
-                for tt in range(per):
-                    t = per * b + tt
-                    for i2 in range(count):
-                        nc.tensor.transpose(bank[:, tt * width + i2 * P : tt * width + (i2 + 1) * P], T["uy", s, jg, i2][:, t * P : (t + 1) * P], ident[:])
-
-        def SI(s, jg):
+        def SI(s, jg, lo=0, hi=4):
             first, count, width, per = span(s)
             y = get(f"y{count}", ("y", s, jg), [P, 4, width], F32)
-            for t in range(4):
+            for t in range(lo, hi):
                 b, tt = divmod(t, per)
                 src = T["ut", s, jg, b][:, tt * width : (tt + 1) * width] if ("ut", s, jg, 0) in T else y[:, t, :]
                 nc.scalar.activation(out=y[:, t, :], in_=src, func=ACT.Silu, bias=pb_t[:, jg, t : t + 1])
@@ -262,9 +248,9 @@ def tile_pathway_latent_encoder_f5_kernel(
                 op=ALU.mult,
             )
 
-        def GG(s, jg, lo=0, hi=4):
+        def GG(s, jg, ring="H", lo=0, hi=4):
             first, count, width, per = span(s)
-            dst = get(f"ag{count}", ("ag", s, jg), [P, 4 * width], BF16)
+            dst = get("grouped_" + ring, ("ag", s, jg), [P, 4 * width], BF16)
             a, b = lo * width // 4, hi * width // 4
             nc.gpsimd.tensor_tensor(
                 out=dst[:, 4 * a : 4 * b].rearrange("p (c t) -> p c t", t=4),
@@ -273,9 +259,9 @@ def tile_pathway_latent_encoder_f5_kernel(
                 op=ALU.mult,
             )
 
-        def GS(s, jg):
+        def GS(s, jg, tag="planes"):
             first, count, width, per = span(s)
-            planes = get("grouped_H", ("planes", s, jg), [P, 4, width], BF16)
+            planes = get(tag, ("planes", s, jg), [P, 4, width], BF16)
             for t in range(4):
                 nc.scalar.activation(out=planes[:, t, :], in_=T["y", s, jg][:, t, :], func=ACT.Copy, scale=ag_f[:, jg, t : t + 1])
 
@@ -287,10 +273,15 @@ def tile_pathway_latent_encoder_f5_kernel(
         def AQ(s, jg):
             quantize(f"a{s}{jg}", ("a", s, jg), T["ag", s, jg][:], SPANS[s][1] * P)
 
-        def VM(jg, t):
-            bank = get("mx", ("v", jg, t), [P, 512], F32)
+        def VM(jg, t, tag="mx"):
+            bank = get(tag, ("v", jg, t), [P, 512], F32)
             for g in range(PASSES):
                 mx(bank[:], ("w", jg, g), slice(t * P, (t + 1) * P), ("w", "e", g), slice(0, 512), g == 0, g == PASSES - 1)
+
+        def VP(jg, g, start, stop, tag="mx"):
+            for t in range(4):
+                bank = get(tag, ("v", jg, t), [P, 512], F32)
+                mx(bank[:], ("w", jg, g), slice(t * P, (t + 1) * P), ("w", "e", g), slice(0, 512), start, stop)
 
         def VS(jg, t):
             vl = get("vl", ("vl", jg), [P, 4, H], BF16)
@@ -316,9 +307,12 @@ def tile_pathway_latent_encoder_f5_kernel(
         def tiles(o):
             return slice(OUTS[o][0], OUTS[o][0] + OUTS[o][1])
 
+        def part(key, o):
+            return get("raw", key, [P, TILES, LATENT], F32)[:, tiles(o), :]
+
         def ST(key, o):
             out = {"mu": mu_out, "sd": sd_out, "z": z_out}[key]
-            nc.sync.dma_start(out=rows(out)[:, tiles(o), :], in_=T[key, o][:, :, 0:LATENT])
+            nc.sync.dma_start(out=rows(out)[:, tiles(o), :], in_=part(key, o))
 
         def QM(o):
             first, count = OUTS[o]
@@ -329,8 +323,7 @@ def tile_pathway_latent_encoder_f5_kernel(
 
         def MB(o):
             first, count = OUTS[o]
-            mu = get("raw", ("mu", o), [P, count, LATENT], F32)
-            nc.vector.tensor_tensor(out=mu[:], in0=T["qm", o][:], in1=lb_b[:, 0:LATENT].unsqueeze(1).to_broadcast([P, count, LATENT]), op=ALU.add)
+            nc.vector.tensor_tensor(out=part("mu", o), in0=T["qm", o][:], in1=lb_b[:, 0:LATENT].unsqueeze(1).to_broadcast([P, count, LATENT]), op=ALU.add)
 
         def QL(o, tag="mx"):
             first, count = OUTS[o]
@@ -353,64 +346,61 @@ def tile_pathway_latent_encoder_f5_kernel(
                     nc.tensor.transpose(bank[:, i2, h * P : (h + 1) * P], T["th", o][:, h, i2 * P : (i2 + 1) * P], ident[:])
 
         def EL(o):
-            sd = get("xw" if o < 4 else "raw", ("sd", o), [P, OUTS[o][1], LATENT], F32)
-            nc.scalar.activation(out=sd[:], in_=T["lt", o][:], func=ACT.Exp, scale=0.5)
+            nc.scalar.activation(out=part("sd", o), in_=T["lt", o][:], func=ACT.Exp, scale=0.5)
 
         def ZM(o, on="V"):
             eng = nc.vector if on == "V" else nc.gpsimd
-            z = get("xg" if o < 4 else "grouped_S", ("z", o), [P, OUTS[o][1], LATENT], F32)
-            eng.tensor_tensor(out=z[:], in0=T["sd", o][:], in1=noise_t[:, tiles(o), :], op=ALU.mult)
+            eng.tensor_tensor(out=part("z", o), in0=part("sd", o), in1=T["noise"][:, tiles(o), :], op=ALU.mult)
 
         def ZA(o, on="V"):
             eng = nc.vector if on == "V" else nc.gpsimd
-            z = T["z", o]
-            eng.tensor_tensor(out=z[:], in0=z[:], in1=T["mu", o][:, :, 0:LATENT], op=ALU.add)
+            eng.tensor_tensor(out=part("z", o), in0=part("z", o), in1=part("mu", o), op=ALU.add)
 
 
-        load_x(0); load_x(1); load_xs(); load_x(2); load_x(3); load_w(0, 0); load_w(0, 1); load_x(4); load_w(0, 2); load_x(5); load_w(0, 3); load_cf()
-        load_w("e", 0); load_w("e", 1); load_w("e", 2)
-        K(0); K(1, "V"); K(2); K(3)
-        D(0, 0, "G"); D(0, 1, "S"); D(0, 2, "G", ring="H")
-        load_w("e", 3); load_small()
-        for pr in range(2):
-            for g in range(4): XT(pr, g); PP(pr, g)
-        K(4); K(5); D(0, 3, "S"); D("e", 0, "G", 0, 2, ring="I")
-        CF(0, 8); CC()
-        for g in range(4): XT(2, g)
-        D("e", 1, "S"); D("e", 2, "S")
-        load_w(1, 0); load_w(1, 1); load_w(1, 2)
+        load_cf(); load_x(0, 0, 1); load_x(0, 1, 4); load_xs(); load_x(1)
+        for g in range(4): load_w(g)
+        load_x(2)
+        for g in range(4): load_e(g)
+        load_x(3); load_small(); load_late(); load_lbc()
+        K(0, "S", 0, 1); K(1, "V", 0, 1); CF(0, 8); CC(); K(0, "S", 1, 4); K(1, "V", 1, 4); K(2); K(3)
+        XT(0, 0); PP(0, 0)
+        D(0, 0, "G"); D(1, 0, "S"); D(0, 1, "G", ring="H"); D(1, 1, "S"); D(0, 2, "S")
+        for g in range(1, 4): XT(0, g); PP(0, g)
+        for g in range(4): XT(1, g, "mx"); PP(1, g)
+        D(0, 3, "S")
+        D(1, 2, "S", ring="I")
         for g in range(4): XQ(0, g); WQ(0, g); UG(0, 0, g, g == 0, g == 3)
-        D("e", 3, "S"); D("e", 0, "V", 2, 4)
-        load_w(1, 3); load_x(6); load_x(7); load_late(); load_lbc()
-        WQ("e", 1); WQ("e", 2); WQ("e", 3); WQ("e", 0)
-        D(1, 0, "G", ring="I"); D(1, 1, "S"); D(1, 2, "G"); LC(); AC(); K(6); K(7); D(1, 3, "S")
+        D(1, 3, "S", ring="H"); K(4); K(5)
+        WQ(1, 0); UG(0, 1, 0, True, False, "tr"); WQ(1, 1); UG(0, 1, 1, False, False); WQ(1, 2); WQ(1, 3)
+        D("e", 0, "G", ring="H"); D("e", 1, "G"); D("e", 3, "S"); D("e", 2, "S", ring="I"); LC(); AC()
         for t in range(4): C(0, 0, t)
+        XT(2, 0, "mx"); XT(2, 1, "mx"); UG(0, 1, 2, False, False); XT(2, 2, "mx"); XT(2, 3, "mx"); UG(0, 1, 3, False, True)
         for g in range(4): PP(2, g)
-        VM(0, 0); VM(0, 1); VM(0, 2); XT(3, 0); XT(3, 1); VM(0, 3); XT(3, 2); XT(3, 3)
-        for t in range(4): VS(0, t)
-        for g in (1, 2, 3): WQ(1, g); UG(0, 1, g, g == 1, False)
-        XQ(2, 0); XQ(2, 1); WQ(1, 0); UG(0, 1, 0, False, True)
-        VI(0, "G", ring="I")
-        SI(0, 0)
-        PP(3, 0); PP(3, 1)
+        SI(0, 0); K(6); K(7)
+        for g in (3, 2, 1): WQ("e", g); VP(0, g, g == 3, False)
+        XQ(2, 0); XQ(2, 1); WQ("e", 0); VP(0, 0, False, True)
         for t in range(4): C(0, 1, t)
-        PP(3, 2); PP(3, 3)
+        for g in range(4): XT(3, g)
+        load_noise()
 
-        GG(0, 0, 0, 2)
-        for t in range(4): VM(1, t)
-        SI(0, 1)
-        for t in range(4): VS(1, t)
-        GS(0, 1)
+        GG(0, 0)
+        for t in range(4): VS(0, t)
+        VI(0, "G"); SI(0, 1); GS(0, 1)
         US(1, 0, 0); US(1, 0, 1)
-        XQ(3, 0); VQ(0); XQ(3, 1); G(0, 0, 2, 4); C(1, 0, 0); AQ(0, 0); C(1, 0, 1); VI(1, "V"); GI(0, 1); VQ(1); AQ(0, 1)
-        UC(1, 1, 0); CS(1, 1, 0); UC(1, 1, 1); CS(1, 1, 1); SI(1, 0)
-        UC(2, 0, 0); CS(2, 0, 0); UT(1, 1); UC(2, 1, 0); SI(1, 1); CS(2, 1, 0)
-        G(1, 0)
-        US(3, 0, 0); UT(2, 0); UT(2, 1); US(3, 1, 0); SI(2, 0); SI(2, 1)
-        G(1, 1); AQ(1, 0); C(3, 0, 0); AQ(1, 1); C(3, 1, 0); SI(3, 0)
-        QL(0); TL(0); SI(3, 1); QM(0); QM(1); QL(1); TL(1); LT(0); QL(2, "tr"); QM(2)
-        G(2, 0); G(2, 1); G(3, 0); AQ(2, 0); AQ(2, 1); G(3, 1); MB(0); ST("mu", 0); AQ(3, 0); AQ(3, 1); MB(1); ST("mu", 1); MB(2); ST("mu", 2)
-        LT(1); QL(3); QL(4, "tr"); QM(3); EL(0); EL(1); TL(2); TL(3); TL(4); QM(4); LT(2); LT(3); LT(4); EL(2); EL(3); EL(4)
-        ST("sd", 0); ST("sd", 1)
-        ZM(0); ZM(1); ZA(0); ST("z", 0); MB(3); ZA(1); ST("mu", 3); ST("sd", 2); ST("z", 1); MB(4); ST("sd", 3); ST("sd", 4); ST("mu", 4)
+        for g in range(4): PP(3, g)
+        C(1, 0, 0); C(1, 0, 1)
+        for t in range(4): VM(1, t)
+        SI(1, 0)
+        for t in range(4): VS(1, t)
+        XQ(3, 0); AQ(0, 0); XQ(3, 1); GI(0, 1); VQ(0); G(1, 0); AQ(0, 1)
+        US(1, 1, 0, "tr"); US(1, 1, 1, "tr"); US(2, 0, 0); US(2, 0, 1)
+        VI(1, "S", ring="I"); C(1, 1, 0); AQ(1, 0); C(1, 1, 1); SI(1, 1); VQ(1); GG(1, 1, "I")
+        US(2, 1, 0); US(2, 1, 1)
+        C(2, 0, 0); C(2, 0, 1); SI(2, 0); C(2, 1, 0); SI(2, 1, 0, 2); C(2, 1, 1)
+        QM(0); QL(0, "tr"); QL(1, "tr"); SI(2, 1, 2, 4); TL(0); TL(1); QM(1); LT(0); LT(1)
+        MB(0); AQ(1, 1); G(2, 0); G(2, 1); AQ(2, 0); MB(1); AQ(2, 1); ST("mu", 0); ST("mu", 1)
+        QL(2, "tr"); QM(2); QL(3, "tr"); QL(4); QM(3); QM(4)
+        EL(0); EL(1); TL(2); TL(3); TL(4); LT(2); LT(3); LT(4, "mx"); EL(2); EL(3); EL(4)
+        ST("sd", 0); MB(2); ST("sd", 1); ST("mu", 2)
+        ZM(0); ZM(1); ZA(0); ST("z", 0); ZA(1); MB(3); MB(4); ST("sd", 2); ST("z", 1); ST("sd", 3); ST("sd", 4); ST("mu", 3); ST("mu", 4)
         ZM(2); ZM(3); ZA(2); ST("z", 2); ZM(4); ZA(3); ST("z", 3); ZA(4); ST("z", 4)

@@ -23,6 +23,7 @@ FLOPS = 2 * CELLS * GENES * PATHWAYS + 2 * GENES * PATHWAYS * H + 2 * CELLS * PA
 TR_BANKS = 4
 LB_COLS = LATENT
 GAIN_RUN = 4
+VEC_ROWS = 26
 SPANS = [(0, 4), (4, 2), (6, 2)]
 OUTS = [(0, 2), (2, 2), (4, 2), (6, 1), (7, 1)]
 BUFS = {"x_raw": 3, "raw": 4, "xw": 4, "xg": 4, "grouped_S": 4, "y4": 2, "y2": 4, "uy": 4, "ag4": 1, "ag2": 3, "vl": 1, "planes": 1}
@@ -62,14 +63,12 @@ def tile_pathway_latent_encoder_f5_kernel(
 
         xs_t = sb.tile([P, PASSES, 4], F32, name="xs_t")
         cf_c = sb.tile([P, TILES], BF16, name="cf_c")
-        pb_t = sb.tile([P, GROUPS, 4], BF16, name="pb_t")
-        ag_t = sb.tile([P, GROUPS, 4], BF16, name="ag_t")
-        lg_t = sb.tile([P, GROUPS, 4], BF16, name="lg_t")
+        vec_rows = sb.tile([P, P], BF16, name="vec_rows")
+        nc.gpsimd.memset(vec_rows[:], 0.0)
+        vec_cols = sb.tile([P, VEC_ROWS], F32, name="vec_cols")
+        pb_t, lg_t, ag_t = (vec_cols[:, 8 * n : 8 * n + 8].rearrange("p (g t) -> p g t", t=4) for n in range(3))
         cf_f = sb.tile([P, TILES], F32, name="cf_f")
-        lg_f = sb.tile([P, GROUPS, 4], F32, name="lg_f")
-        ag_f = sb.tile([P, GROUPS, 4], F32, name="ag_f")
         lb_b = sb.tile([P, LB_COLS], BF16, name="lb_b")
-        lb_c = sb.tile([P, 2, 2], BF16, name="lb_c")
         cf_b = sb.tile([P, CELLS], BF16, name="cf_b")
 
         def load_x(pr, lo=0, hi=PASSES):
@@ -94,19 +93,25 @@ def tile_pathway_latent_encoder_f5_kernel(
             nc.sync.dma_start(out=cf_c[:], in_=cell_factor.rearrange("(p i) -> p i", i=TILES))
 
         def load_small():
-            nc.sync.dma_start(out=pb_t[:], in_=by_slot(pathway_bias))
-            nc.sync.dma_start(out=lg_t[:], in_=by_slot(loading_gain))
-            nc.sync.dma_start(out=ag_t[:], in_=by_slot(activity_gain))
+            for n, vec in enumerate((pathway_bias, loading_gain, activity_gain)):
+                for g in range(GROUPS):
+                    r = 8 * n + 4 * g
+                    nc.sync.dma_start(
+                        out=vec_rows[r : r + 4, :].rearrange("t (c i) -> t c i", i=4),
+                        in_=vec[g * 512 : (g + 1) * 512].rearrange("(c t i) -> t c i", t=4, i=4),
+                    )
+            nc.sync.dma_start(out=vec_rows[24:26, :], in_=latent_bias[LATENT:H].rearrange("(h p) -> h p", h=2))
+
+        def VT():
+            bank = get("mx", "vec", [P, P], BF16)
+            nc.tensor.transpose(bank[:], vec_rows[:], ident_bf[:])
+            nc.scalar.copy(out=vec_cols[:], in_=bank[:, 0:VEC_ROWS])
 
         def load_late():
             nc.sync.dma_start(out=lb_b[:], in_=latent_bias[0:LB_COLS].partition_broadcast(P))
 
         def load_noise():
             nc.sync.dma_start(out=get("raw", "noise", [P, TILES, LATENT], BF16)[:], in_=rows(noise))
-
-        def load_lbc():
-            with nc.allow_non_contiguous_dma(reason="one bias value for each partition"):
-                nc.sync.dma_start(out=lb_c[:, :, 0:1], in_=latent_bias[LATENT:H].rearrange("(h p o) -> p h o", h=2, o=1))
 
         def CF(first, count):
             bank = get("mx", ("cf", first), [P, count * P], BF16)
@@ -116,12 +121,6 @@ def tile_pathway_latent_encoder_f5_kernel(
         def CC():
             nc.vector.tensor_copy(out=cf_b[:], in_=T["cf", 0][:])
             nc.scalar.copy(out=cf_f[:], in_=cf_c[:])
-
-        def LC():
-            nc.scalar.copy(out=lg_f[:], in_=lg_t[:])
-
-        def AC():
-            nc.scalar.copy(out=ag_f[:], in_=ag_t[:])
 
         def K(i, on="S", lo=0, hi=PASSES):
             xw = get("xw", ("xw", i), [P, GENES], BF16)
@@ -183,16 +182,16 @@ def tile_pathway_latent_encoder_f5_kernel(
                     o = out.rearrange("p (c j) -> p c j", j=4)
                     i = raw[:, :, lo * P : hi * P].rearrange("p j c -> p c j")
                 else:
-                    o = out.rearrange("p (t m j) -> p m t j", m=P, j=4)
-                    i = raw.rearrange("p j (m t) -> p m t j", t=4)[:, :, lo:hi, :]
+                    o = out.rearrange("p (t c i j) -> p c t i j", t=4, i=4, j=4)
+                    i = raw.rearrange("p j (c t i) -> p c t i j", t=4, i=4)
                 nc.gpsimd.tensor_scalar(out=o, in0=i, scalar1=1.0, scalar2=0.0, op0=ALU.mult, op1=ALU.add)
                 return
             if k == "e":
                 o = out.rearrange("p (c i j) -> p c j i", i=4, j=4)
                 i = raw[:, :, lo * P : hi * P].rearrange("p j (c i) -> p c j i", i=4)
             else:
-                o = out.rearrange("p (t c i j) -> p t c j i", c=P // 4, i=4, j=4)
-                i = raw.rearrange("p j (c i t) -> p t c j i", i=4, t=4)[:, lo:hi, :, :, :]
+                o = out.rearrange("p (t c i j) -> p c t j i", t=4, i=4, j=4)
+                i = raw.rearrange("p j (c t i) -> p c t j i", t=4, i=4)
             if eng == "V":
                 nc.vector.tensor_copy(out=o, in_=i)
             else:
@@ -263,7 +262,7 @@ def tile_pathway_latent_encoder_f5_kernel(
             first, count, width, per = span(s)
             planes = get(tag, ("planes", s, jg), [P, 4, width], BF16)
             for t in range(4):
-                nc.scalar.activation(out=planes[:, t, :], in_=T["y", s, jg][:, t, :], func=ACT.Copy, scale=ag_f[:, jg, t : t + 1])
+                nc.scalar.activation(out=planes[:, t, :], in_=T["y", s, jg][:, t, :], func=ACT.Copy, scale=ag_t[:, jg, t : t + 1])
 
         def GI(s, jg):
             first, count, width, per = span(s)
@@ -285,7 +284,7 @@ def tile_pathway_latent_encoder_f5_kernel(
 
         def VS(jg, t):
             vl = get("vl", ("vl", jg), [P, 4, H], BF16)
-            nc.scalar.activation(out=vl[:, t, :], in_=T["v", jg, t][:], func=ACT.Copy, scale=lg_f[:, jg, t : t + 1])
+            nc.scalar.activation(out=vl[:, t, :], in_=T["v", jg, t][:], func=ACT.Copy, scale=lg_t[:, jg, t : t + 1])
 
         def VI(jg, on, ring=None):
             dst = get("grouped_" + (ring or on), ("grouped", "v", jg), [P, 2048], BF16)
@@ -336,7 +335,7 @@ def tile_pathway_latent_encoder_f5_kernel(
             first, count = OUTS[o]
             th = get("uy", ("th", o), [P, 2, count * P], F32)
             for h in range(2):
-                nc.scalar.activation(out=th[:, h, :], in_=T["ql", o][:, h, :], func=ACT.Tanh, bias=lb_c[:, h, 0:1])
+                nc.scalar.activation(out=th[:, h, :], in_=T["ql", o][:, h, :], func=ACT.Tanh, bias=vec_cols[:, 24 + h : 25 + h])
 
         def LT(o, tag="tr"):
             first, count = OUTS[o]
@@ -361,7 +360,7 @@ def tile_pathway_latent_encoder_f5_kernel(
         for g in range(4): load_w(g)
         load_x(2)
         for g in range(4): load_e(g)
-        load_x(3); load_small(); load_late(); load_lbc()
+        load_small(); load_x(3); load_late()
         K(0, "S", 0, 1); K(1, "V", 0, 1); CF(0, 8); CC(); K(0, "S", 1, 4); K(1, "V", 1, 4); K(2); K(3)
         XT(0, 0); PP(0, 0)
         D(0, 0, "G"); D(1, 0, "S"); D(0, 1, "G", ring="H"); D(1, 1, "S"); D(0, 2, "S")
@@ -372,9 +371,9 @@ def tile_pathway_latent_encoder_f5_kernel(
         for g in range(4): XQ(0, g); WQ(0, g); UG(0, 0, g, g == 0, g == 3)
         D(1, 3, "S", ring="H"); K(4); K(5)
         WQ(1, 0); UG(0, 1, 0, True, False, "tr"); WQ(1, 1); UG(0, 1, 1, False, False); WQ(1, 2); WQ(1, 3)
-        D("e", 0, "G", ring="H"); D("e", 1, "G"); D("e", 3, "S"); D("e", 2, "S", ring="I"); LC(); AC()
+        D("e", 0, "G", ring="H"); D("e", 1, "G"); D("e", 3, "S")
         for t in range(4): C(0, 0, t)
-        XT(2, 0, "mx"); XT(2, 1, "mx"); UG(0, 1, 2, False, False); XT(2, 2, "mx"); XT(2, 3, "mx"); UG(0, 1, 3, False, True)
+        XT(2, 0, "mx"); XT(2, 1, "mx"); UG(0, 1, 2, False, False); XT(2, 2, "mx"); XT(2, 3, "mx"); D("e", 2, "S", ring="I"); VT(); UG(0, 1, 3, False, True)
         for g in range(4): PP(2, g)
         SI(0, 0); K(6); K(7)
         for g in (3, 2, 1): WQ("e", g); VP(0, g, g == 3, False)

@@ -26,7 +26,7 @@ GAIN_RUN = 4
 VEC_ROWS = 26
 SPANS = [(0, 4), (4, 2), (6, 2)]
 OUTS = [(0, 2), (2, 2), (4, 2), (6, 1), (7, 1)]
-BUFS = {"x_raw": 3, "raw": 4, "xw": 4, "xg": 4, "grouped_S": 4, "y4": 2, "y2": 4, "uy": 4, "ag4": 1, "ag2": 3, "vl": 1, "planes": 1}
+BUFS = {"x_raw": 3, "raw": 4, "xw": 4, "xg": 4, "grouped_S": 4, "y4": 2, "y2": 4, "uy": 4, "ag4": 1, "ag2": 3, "vl": 2, "planes": 1}
 
 
 def tile_pathway_latent_encoder_f5_kernel(
@@ -105,6 +105,9 @@ def tile_pathway_latent_encoder_f5_kernel(
         def VT():
             bank = get("mx", "vec", [P, P], BF16)
             nc.tensor.transpose(bank[:], vec_rows[:], ident_bf[:])
+
+        def VC():
+            bank = T["vec"]
             nc.scalar.copy(out=vec_cols[:], in_=bank[:, 0:VEC_ROWS])
 
         def load_late():
@@ -197,6 +200,20 @@ def tile_pathway_latent_encoder_f5_kernel(
             else:
                 nc.scalar.copy(out=o, in_=i)
 
+        def PI(k, g, t):
+            bank = get("tr", ("pi", k, g, t // 2), [P, 2, 512], BF16)
+            nc.tensor.matmul(
+                bank[:, t % 2, :].rearrange("p (c i j) -> p j c i", i=4, j=4),
+                lhsT=ident_bf[:],
+                rhs=raw_of(k, g).rearrange("p j (c t i) -> p t j c i", t=4, i=4)[:, t, :, :, :],
+                start=True,
+                stop=True,
+            )
+
+        def PC(k, g, half, ring="S"):
+            dst = get("grouped_" + ring, ("grouped", k, g), [P, 2048], BF16)
+            nc.scalar.copy(out=dst[:, half * 1024 : (half + 1) * 1024], in_=T["pi", k, g, half][:].rearrange("p t c -> p (t c)"))
+
         def WQ(k, g):
             quantize(f"w{k}{g}", ("w", k, g), T["grouped", k, g][:], 512)
 
@@ -277,8 +294,8 @@ def tile_pathway_latent_encoder_f5_kernel(
             for g in range(PASSES):
                 mx(bank[:], ("w", jg, g), slice(t * P, (t + 1) * P), ("w", "e", g), slice(0, 512), g == 0, g == PASSES - 1)
 
-        def VP(jg, g, start, stop, tag="mx"):
-            for t in range(4):
+        def VP(jg, g, start, stop, tag="mx", lo=0, hi=4):
+            for t in range(lo, hi):
                 bank = get(tag, ("v", jg, t), [P, 512], F32)
                 mx(bank[:], ("w", jg, g), slice(t * P, (t + 1) * P), ("w", "e", g), slice(0, 512), start, stop)
 
@@ -286,15 +303,16 @@ def tile_pathway_latent_encoder_f5_kernel(
             vl = get("vl", ("vl", jg), [P, 4, H], BF16)
             nc.scalar.activation(out=vl[:, t, :], in_=T["v", jg, t][:], func=ACT.Copy, scale=lg_t[:, jg, t : t + 1])
 
-        def VI(jg, on, ring=None):
-            dst = get("grouped_" + (ring or on), ("grouped", "v", jg), [P, 2048], BF16)
+        def VI(jg, on, ring=None, lo=0, hi=H):
+            dst = get("grouped_" + (ring or on), ("grouped", "v", jg), [P, 2048], BF16)[:, 4 * lo : 4 * hi]
+            src = T["vl", jg][:, :, lo:hi]
             if on == "G":
                 nc.gpsimd.tensor_scalar(
-                    out=dst[:].rearrange("p (c t) -> p c t", t=4), in0=T["vl", jg][:].rearrange("p t c -> p c t"), scalar1=1.0, scalar2=0.0, op0=ALU.mult, op1=ALU.add
+                    out=dst.rearrange("p (c t) -> p c t", t=4), in0=src.rearrange("p t c -> p c t"), scalar1=1.0, scalar2=0.0, op0=ALU.mult, op1=ALU.add
                 )
             else:
                 copy = nc.vector.tensor_copy if on == "V" else nc.scalar.copy
-                copy(out=dst[:].rearrange("p (c i t) -> p c t i", i=4, t=4), in_=T["vl", jg][:].rearrange("p t (c i) -> p c t i", i=4))
+                copy(out=dst.rearrange("p (c i t) -> p c t i", i=4, t=4), in_=src.rearrange("p t (c i) -> p c t i", i=4))
 
         def VQ(jg):
             quantize(f"v{jg}", ("v", jg), T["grouped", "v", jg][:], H)
@@ -367,33 +385,32 @@ def tile_pathway_latent_encoder_f5_kernel(
         for g in range(1, 4): XT(0, g); PP(0, g)
         for g in range(4): XT(1, g, "mx"); PP(1, g)
         D(0, 3, "S")
-        D(1, 2, "S", ring="I")
+        for t in range(4): PI(1, 2, t)
+        PC(1, 2, 0, "I"); PC(1, 2, 1, "I")
         for g in range(4): XQ(0, g); WQ(0, g); UG(0, 0, g, g == 0, g == 3)
         D(1, 3, "S", ring="H"); K(4); K(5)
-        WQ(1, 0); UG(0, 1, 0, True, False, "tr"); WQ(1, 1); UG(0, 1, 1, False, False); WQ(1, 2); WQ(1, 3)
+        WQ(1, 0); UG(0, 1, 0, True, False, "tr"); WQ(1, 1); WQ(1, 2); WQ(1, 3)
         D("e", 0, "G", ring="H"); D("e", 1, "G"); D("e", 3, "S")
         for t in range(4): C(0, 0, t)
-        XT(2, 0, "mx"); XT(2, 1, "mx"); UG(0, 1, 2, False, False); XT(2, 2, "mx"); XT(2, 3, "mx"); D("e", 2, "S", ring="I"); VT(); UG(0, 1, 3, False, True)
+        XT(2, 0, "mx"); XT(2, 1, "mx"); UG(0, 1, 1, False, False); XT(2, 2, "mx"); XT(2, 3, "mx"); VT(); UG(0, 1, 2, False, False); UG(0, 1, 3, False, True)
         for g in range(4): PP(2, g)
-        SI(0, 0); K(6); K(7)
-        for g in (3, 2, 1): WQ("e", g); VP(0, g, g == 3, False)
-        XQ(2, 0); XQ(2, 1); WQ("e", 0); VP(0, 0, False, True)
+        K(6); K(7); VC(); D("e", 2, "S", ring="I"); XT(3, 0, "mx"); XT(3, 1, "mx")
+        for g in (3, 1, 2, 0): WQ("e", g); VP(0, g, g == 3, g == 0, "mx", 0, 2)
         for t in range(4): C(0, 1, t)
-        for g in range(4): XT(3, g)
+        VM(0, 2, "tr"); VM(0, 3, "tr"); XT(3, 2); XT(3, 3)
         load_noise()
-
-        GG(0, 0)
+        SI(0, 0); GG(0, 0)
         for t in range(4): VS(0, t)
-        VI(0, "G"); SI(0, 1); GS(0, 1)
-        US(1, 0, 0); US(1, 0, 1)
+        SI(0, 1)
         for g in range(4): PP(3, g)
-        C(1, 0, 0); C(1, 0, 1)
         for t in range(4): VM(1, t)
-        SI(1, 0)
+
+        VI(0, "G", hi=192); VI(0, "S", lo=192)
+        XQ(2, 0); XQ(2, 1); AQ(0, 0); XQ(3, 0); XQ(3, 1); VQ(0)
+        GS(0, 1)
         for t in range(4): VS(1, t)
-        XQ(3, 0); AQ(0, 0); XQ(3, 1); GI(0, 1); VQ(0); G(1, 0); AQ(0, 1)
-        US(1, 1, 0, "tr"); US(1, 1, 1, "tr"); US(2, 0, 0); US(2, 0, 1)
-        VI(1, "S", ring="I"); C(1, 1, 0); AQ(1, 0); C(1, 1, 1); SI(1, 1); VQ(1); GG(1, 1, "I")
+        US(1, 0, 0, "tr"); US(1, 0, 1, "tr"); US(1, 1, 0, "tr"); US(1, 1, 1, "tr"); US(2, 0, 0); US(2, 0, 1)
+        GI(0, 1); C(1, 0, 0); C(1, 0, 1); SI(1, 0); VI(1, "S", ring="I"); AQ(0, 1); C(1, 1, 0); C(1, 1, 1); SI(1, 1); G(1, 0); AQ(1, 0); VQ(1); GG(1, 1, "I")
         US(2, 1, 0); US(2, 1, 1)
         C(2, 0, 0); C(2, 0, 1); SI(2, 0); C(2, 1, 0); SI(2, 1, 0, 2); C(2, 1, 1)
         QM(0); QL(0, "tr"); QL(1, "tr"); SI(2, 1, 2, 4); TL(0); TL(1); QM(1); LT(0); LT(1)

@@ -121,6 +121,11 @@ def tile_pathway_latent_encoder_f5_kernel(
             for i in range(count):
                 nc.tensor.matmul(bank[:, i * P : (i + 1) * P], lhsT=cf_c[:, first + i : first + i + 1].to_broadcast([P, P]), rhs=ident_bf[:], start=True, stop=True)
 
+        def WARM():
+            warm = sb.tile([P, 2], F32, name="warm")
+            nc.vector.memset(warm[:], 0.0)
+            nc.scalar.activation(out=warm[:, 1:2], in_=warm[:, 0:1], func=ACT.Silu)
+
         def CC():
             nc.vector.tensor_copy(out=cf_b[:], in_=T["cf", 0][:])
             nc.scalar.copy(out=cf_f[:], in_=cf_c[:])
@@ -373,6 +378,7 @@ def tile_pathway_latent_encoder_f5_kernel(
             eng = nc.vector if on == "V" else nc.gpsimd
             eng.tensor_tensor(out=part("z", o), in0=part("z", o), in1=part("mu", o), op=ALU.add)
 
+        WARM()
 
         load_cf(); load_x(0, 0, 1); load_x(0, 1, 4); load_xs(); load_x(1)
         for g in range(4): load_w(g)

@@ -13,20 +13,22 @@ ACT = mybir.ActivationFunctionType
 ALU = mybir.AluOpType
 
 CELLS, GENES, PATHWAYS, LATENT = 1024, 2048, 1024, 256
-H = 2 * LATENT
+WIDE = 2 * LATENT
 P = 128
-PASSES = GENES // 512
-GROUPS = PATHWAYS // 512
+SLOTS = 4
+DEPTH = P * SLOTS
+PASSES = GENES // DEPTH
+GROUPS = PATHWAYS // DEPTH
 TILES = CELLS // P
-PAIRS = TILES // 2
-FLOPS = 2 * CELLS * GENES * PATHWAYS + 2 * GENES * PATHWAYS * H + 2 * CELLS * PATHWAYS * H
-TR_BANKS = 4
-LB_COLS = LATENT
-GAIN_RUN = 4
-VEC_ROWS = 26
+FLOPS = 2 * CELLS * GENES * PATHWAYS + 2 * GENES * PATHWAYS * WIDE + 2 * CELLS * PATHWAYS * WIDE
+
 SPANS = [(0, 4), (4, 2), (6, 2)]
-OUTS = [(0, 2), (2, 2), (4, 2), (6, 1), (7, 1)]
-BUFS = {"x_raw": 3, "raw": 4, "xw": 4, "xg": 4, "grouped_S": 4, "y4": 2, "y2": 4, "uy": 4, "ag4": 1, "ag2": 3, "vl": 2, "planes": 1}
+PIECES = [(0, 2), (2, 2), (4, 2), (6, 1), (7, 1)]
+BIAS_ROW = 24
+VECTOR_ROWS = 26
+V0_ON_GPSIMD = 192
+E2_ON_SCALAR = 3
+BUFFERS = {"x_raw": 2, "big": 4, "x_wide": 4, "x_scaled": 4, "ring_s": 4, "y4": 2, "y2": 4, "tanh": 4, "gained2": 3, "v_planes": 2}
 
 
 def tile_pathway_latent_encoder_f5_kernel(
@@ -35,394 +37,464 @@ def tile_pathway_latent_encoder_f5_kernel(
     nc = tc.nc
     with ExitStack() as ctx:
         sb = ctx.enter_context(tc.tile_pool(name="sb", bufs=1))
-        ps_tr = ctx.enter_context(tc.psum_pool(name="ps_tr", bufs=TR_BANKS))
-        ps_mx = ctx.enter_context(tc.psum_pool(name="ps_mx", bufs=8 - TR_BANKS))
+        banks = {ring: ctx.enter_context(tc.psum_pool(name="banks_" + ring, bufs=4)) for ring in "AB"}
         ctx.enter_context(tc.manual_schedule())
-        T = {}
+        held = {}
 
-        def get(tag, key, shape, dt):
-            if key not in T:
-                if tag == "tr":
-                    T[key] = ps_tr.tile(shape, dt, name=tag)
-                elif tag == "mx":
-                    T[key] = ps_mx.tile(shape, dt, name=tag)
-                else:
-                    T[key] = sb.tile(shape, dt, name=tag, bufs=BUFS.get(tag, 1), align_bytes=64)
-            return T[key]
+        def tile(tag, key, shape, dtype):
+            if key not in held:
+                held[key] = sb.tile(shape, dtype, name=tag, bufs=BUFFERS.get(tag, 1), align_bytes=64)
+            return held[key]
 
-        def rows(ap):
+        def bank(ring, key, shape, dtype=F32):
+            if key not in held:
+                held[key] = banks[ring].tile(shape, dtype, name="bank_" + ring)
+            return held[key]
+
+        def by_tile(ap):
             return ap.rearrange("(p i) c -> p i c", i=TILES)
 
-        def by_slot(vec):
-            return vec.rearrange("(g p t) -> p g t", p=P, t=4)
+        def block(n, count=1):
+            return slice(n * P, (n + count) * P)
 
         ident = sb.tile([P, P], F32, name="ident")
         make_identity(nc, ident[:])
         ident_bf = sb.tile([P, P], BF16, name="ident_bf")
         make_identity(nc, ident_bf[:])
+        gene_scale = sb.tile([P, PASSES, SLOTS], F32, name="gene_scale")
+        factor_col = sb.tile([P, TILES], BF16, name="factor_col")
+        vector_rows = sb.tile([P, P], BF16, name="vector_rows")
+        nc.gpsimd.memset(vector_rows[:], 0.0)
+        vector_cols = sb.tile([P, VECTOR_ROWS], F32, name="vector_cols")
+        bias_col, loading_col, gain_col = (vector_cols[:, 8 * n : 8 * n + 8].rearrange("p (g t) -> p g t", t=SLOTS) for n in range(3))
+        mean_bias = sb.tile([P, LATENT], BF16, name="mean_bias")
+        factor_row = sb.tile([P, CELLS], BF16, name="factor_row")
 
-        xs_t = sb.tile([P, PASSES, 4], F32, name="xs_t")
-        cf_c = sb.tile([P, TILES], BF16, name="cf_c")
-        vec_rows = sb.tile([P, P], BF16, name="vec_rows")
-        nc.gpsimd.memset(vec_rows[:], 0.0)
-        vec_cols = sb.tile([P, VEC_ROWS], F32, name="vec_cols")
-        pb_t, lg_t, ag_t = (vec_cols[:, 8 * n : 8 * n + 8].rearrange("p (g t) -> p g t", t=4) for n in range(3))
-        cf_f = sb.tile([P, TILES], F32, name="cf_f")
-        lb_b = sb.tile([P, LB_COLS], BF16, name="lb_b")
-        cf_b = sb.tile([P, CELLS], BF16, name="cf_b")
-
-        def load_x(pr, lo=0, hi=PASSES):
-            raw = get("x_raw", ("x_raw", pr, lo), [P, 2, (hi - lo) * 512], U8)
-            nc.sync.dma_start(out=raw[:], in_=rows(x_bytes)[:, 2 * pr : 2 * pr + 2, lo * 512 : hi * 512])
+        def load_x(pair, lo=0, hi=PASSES):
+            raw = tile("x_raw%d" % lo if pair == 0 else "x_raw", ("x_raw", pair, lo), [P, 2, (hi - lo) * DEPTH], U8)
+            nc.sync.dma_start(out=raw[:], in_=by_tile(x_bytes)[:, 2 * pair : 2 * pair + 2, lo * DEPTH : hi * DEPTH])
 
         def load_w(g):
-            raw = get("raw", ("raw", g), [P, 4, PATHWAYS], BF16)
-            nc.sync.dma_start(out=raw[:], in_=w[g * 512 : (g + 1) * 512, :].rearrange("(p j) n -> p j n", j=4))
+            raw = tile("big", ("w_raw", g), [P, SLOTS, PATHWAYS], BF16)
+            nc.sync.dma_start(out=raw[:], in_=w[g * DEPTH : (g + 1) * DEPTH, :].rearrange("(p j) n -> p j n", j=SLOTS))
 
         def load_e(g):
-            raw = get("raw", ("raw", "e", g // 2), [P, 2, 4, H], BF16)
-            nc.sync.dma_start(out=raw[:, g % 2, :, :], in_=e[g * 512 : (g + 1) * 512, :].rearrange("(p j) n -> p j n", j=4))
+            raw = tile("big", ("e_raw", g // 2), [P, 2, SLOTS, WIDE], BF16)
+            nc.sync.dma_start(out=raw[:, g % 2, :, :], in_=e[g * DEPTH : (g + 1) * DEPTH, :].rearrange("(p j) n -> p j n", j=SLOTS))
 
-        def raw_of(k, g):
-            return T["raw", "e", g // 2][:, g % 2, :, :] if k == "e" else T["raw", g][:, :, k * 512 : (k + 1) * 512]
-
-        def load_xs():
-            nc.sync.dma_start(out=xs_t[:], in_=by_slot(x_scale.rearrange("o k -> (o k)")))
-
-        def load_cf():
-            nc.sync.dma_start(out=cf_c[:], in_=cell_factor.rearrange("(p i) -> p i", i=TILES))
-
-        def load_small():
+        def load_vectors():
             for n, vec in enumerate((pathway_bias, loading_gain, activity_gain)):
-                for g in range(GROUPS):
-                    r = 8 * n + 4 * g
+                for jg in range(GROUPS):
+                    row = 8 * n + SLOTS * jg
                     nc.sync.dma_start(
-                        out=vec_rows[r : r + 4, :].rearrange("t (c i) -> t c i", i=4),
-                        in_=vec[g * 512 : (g + 1) * 512].rearrange("(c t i) -> t c i", t=4, i=4),
+                        out=vector_rows[row : row + SLOTS, :].rearrange("t (c i) -> t c i", i=4),
+                        in_=vec[jg * DEPTH : (jg + 1) * DEPTH].rearrange("(c t i) -> t c i", t=SLOTS, i=4),
                     )
-            nc.sync.dma_start(out=vec_rows[24:26, :], in_=latent_bias[LATENT:H].rearrange("(h p) -> h p", h=2))
+            nc.sync.dma_start(out=vector_rows[BIAS_ROW:VECTOR_ROWS, :], in_=latent_bias[LATENT:WIDE].rearrange("(h p) -> h p", h=2))
+            nc.sync.dma_start(out=mean_bias[:], in_=latent_bias[0:LATENT].partition_broadcast(P))
 
-        def VT():
-            bank = get("mx", "vec", [P, P], BF16)
-            nc.tensor.transpose(bank[:], vec_rows[:], ident_bf[:])
+        def tiles_of(piece):
+            return slice(PIECES[piece][0], PIECES[piece][0] + PIECES[piece][1])
 
-        def VC():
-            bank = T["vec"]
-            nc.scalar.copy(out=vec_cols[:], in_=bank[:, 0:VEC_ROWS])
+        def result(name, piece):
+            return tile("big", name, [P, TILES, LATENT], F32)[:, tiles_of(piece), :]
 
-        def load_late():
-            nc.sync.dma_start(out=lb_b[:], in_=latent_bias[0:LB_COLS].partition_broadcast(P))
+        def store(name, piece):
+            out = {"mu": mu_out, "sd": sd_out, "z": z_out}[name]
+            nc.sync.dma_start(out=by_tile(out)[:, tiles_of(piece), :], in_=result(name, piece))
 
-        def load_noise():
-            nc.sync.dma_start(out=get("raw", "noise", [P, TILES, LATENT], BF16)[:], in_=rows(noise))
-
-        def CF(first, count):
-            bank = get("mx", ("cf", first), [P, count * P], BF16)
-            for i in range(count):
-                nc.tensor.matmul(bank[:, i * P : (i + 1) * P], lhsT=cf_c[:, first + i : first + i + 1].to_broadcast([P, P]), rhs=ident_bf[:], start=True, stop=True)
-
-        def WARM():
-            warm = sb.tile([P, 2], F32, name="warm")
-            nc.vector.memset(warm[:], 0.0)
-            nc.scalar.activation(out=warm[:, 1:2], in_=warm[:, 0:1], func=ACT.Silu)
-
-        def CC():
-            nc.vector.tensor_copy(out=cf_b[:], in_=T["cf", 0][:])
-            nc.scalar.copy(out=cf_f[:], in_=cf_c[:])
-
-        def K(i, on="S", lo=0, hi=PASSES):
-            xw = get("xw", ("xw", i), [P, GENES], BF16)
-            copy = nc.scalar.copy if on == "S" else nc.vector.tensor_copy
-            copy(out=xw[:, lo * 512 : hi * 512], in_=T["x_raw", i // 2, lo][:, i % 2, :].bitcast(F8))
-
-        def XT(pr, g, tag="tr"):
-            bank = get(tag, ("xt", pr, g), [P, 512], F32)
-            for i2 in range(2):
-                words = T["xw", 2 * pr + i2][:].bitcast(F32)
-                for u in range(2):
-                    nc.tensor.transpose(
-                        bank[:, u * 256 + i2 * P : u * 256 + (i2 + 1) * P], words[:, 256 * g + u : 256 * (g + 1) : 2], ident[:]
-                    )
-
-        def x_part(pr, g):
-            return ((0, g), pr) if pr < 2 else ((pr, g // 2), g % 2)
-
-        def x_op(i, g, count):
-            key, half = x_part(i // 2, g)
-            first = half * 256 + i % 2 * P
-            return ("x",) + key, slice(first, first + count * P)
-
-        def PP(pr, g):
-            key, half = x_part(pr, g)
-            xg = get("xg", ("xg",) + key, [P, 2, 1024], BF16)
-            nc.vector.tensor_tensor(
-                out=xg[:, half, :].rearrange("p (m u e) -> p m u e", u=2, e=2),
-                in0=T["xt", pr, g][:].bitcast(BF16).rearrange("p (u m e) -> p m u e", u=2, e=2),
-                in1=xs_t[:, g, :].rearrange("p (u e) -> p u e", e=2).unsqueeze(1).to_broadcast([P, 256, 2, 2]),
-                op=ALU.mult,
-            )
-
-        def quantize(name, key, src, width):
-            c = get(name + "_c", ("codes",) + key, [P, width], U32)
-            s = get(name + "_s", ("scales",) + key, [P, width], U8)
-            nc.vector.quantize_mx(out=c[:].bitcast(FP8X4), scales=s[:], in_=src)
+        def quantize(key, src, width):
+            name = "".join(str(part) for part in key)
+            codes = tile(name + "_codes", ("codes",) + key, [P, width], U32)
+            scales = tile(name + "_scales", ("scales",) + key, [P, width], U8)
+            nc.vector.quantize_mx(out=codes[:].bitcast(FP8X4), scales=scales[:], in_=src)
 
         def mx(out, left, left_cols, right, right_cols, start, stop):
             nc.tensor.matmul_mx(
                 out=out,
-                lhsT=T[("codes",) + left][:, left_cols].bitcast(FP8X4),
-                lhsT_scale=T[("scales",) + left][:, left_cols],
-                rhs=T[("codes",) + right][:, right_cols].bitcast(FP8X4),
-                rhs_scale=T[("scales",) + right][:, right_cols],
+                lhsT=held[("codes",) + left][:, left_cols].bitcast(FP8X4),
+                lhsT_scale=held[("scales",) + left][:, left_cols],
+                rhs=held[("codes",) + right][:, right_cols].bitcast(FP8X4),
+                rhs_scale=held[("scales",) + right][:, right_cols],
                 start=start,
                 stop=stop,
             )
 
-        def XQ(pr, a):
-            quantize(f"x{pr}{a}", ("x", pr, a), T["xg", pr, a][:].rearrange("p g c -> p (g c)"), 512)
+        def widen(i, copy, lo=0, hi=PASSES):
+            wide = tile("x_wide", ("x_wide", i), [P, GENES], BF16)
+            copy(out=wide[:, lo * DEPTH : hi * DEPTH], in_=held["x_raw", i // 2, lo][:, i % 2, :].bitcast(F8))
 
-        def D(k, g, eng, lo=0, hi=4, ring=None):
-            dst = get("grouped_" + (ring or eng), ("grouped", k, g), [P, 2048], BF16)
-            raw = raw_of(k, g)
-            out = dst[:, lo * 512 : hi * 512]
-            if eng == "G":
-                if k == "e":
-                    o = out.rearrange("p (c j) -> p c j", j=4)
-                    i = raw[:, :, lo * P : hi * P].rearrange("p j c -> p c j")
-                else:
-                    o = out.rearrange("p (t c i j) -> p c t i j", t=4, i=4, j=4)
-                    i = raw.rearrange("p j (c t i) -> p c t i j", t=4, i=4)
-                nc.gpsimd.tensor_scalar(out=o, in0=i, scalar1=1.0, scalar2=0.0, op0=ALU.mult, op1=ALU.add)
-                return
-            if k == "e":
-                o = out.rearrange("p (c i j) -> p c j i", i=4, j=4)
-                i = raw[:, :, lo * P : hi * P].rearrange("p j (c i) -> p c j i", i=4)
-            else:
-                o = out.rearrange("p (t c i j) -> p c t j i", t=4, i=4, j=4)
-                i = raw.rearrange("p j (c t i) -> p c t j i", t=4, i=4)
-            if eng == "V":
-                nc.vector.tensor_copy(out=o, in_=i)
-            else:
-                nc.scalar.copy(out=o, in_=i)
+        def turn_x(pair, g, ring):
+            out = bank(ring, ("x_turned", pair, g), [P, 512])
+            for i in range(2):
+                words = held["x_wide", 2 * pair + i][:].bitcast(F32)
+                for u in range(2):
+                    nc.tensor.transpose(out[:, block(2 * u + i)], words[:, 256 * g + u : 256 * (g + 1) : 2], ident[:])
 
-        def PI(k, g, t):
-            bank = get("tr", ("pi", k, g, t // 2), [P, 2, 512], BF16)
-            nc.tensor.matmul(
-                bank[:, t % 2, :].rearrange("p (c i j) -> p j c i", i=4, j=4),
-                lhsT=ident_bf[:],
-                rhs=raw_of(k, g).rearrange("p j (c t i) -> p t j c i", t=4, i=4)[:, t, :, :, :],
-                start=True,
-                stop=True,
+        def x_place(pair, g):
+            return ((0, g), pair) if pair < 2 else ((pair, g // 2), g % 2)
+
+        def scale_x(pair, g):
+            key, half = x_place(pair, g)
+            scaled = tile("x_scaled", ("x_scaled",) + key, [P, 2, 1024], BF16)
+            nc.vector.tensor_tensor(
+                out=scaled[:, half, :].rearrange("p (m u e) -> p m u e", u=2, e=2),
+                in0=held["x_turned", pair, g][:].bitcast(BF16).rearrange("p (u m e) -> p m u e", u=2, e=2),
+                in1=gene_scale[:, g, :].rearrange("p (u e) -> p u e", e=2).unsqueeze(1).to_broadcast([P, 256, 2, 2]),
+                op=ALU.mult,
             )
 
-        def PC(k, g, half, ring="S"):
-            dst = get("grouped_" + ring, ("grouped", k, g), [P, 2048], BF16)
-            nc.scalar.copy(out=dst[:, half * 1024 : (half + 1) * 1024], in_=T["pi", k, g, half][:].rearrange("p t c -> p (t c)"))
+        def quantize_x(*key):
+            quantize(("x",) + key, held[("x_scaled",) + key][:].rearrange("p g c -> p (g c)"), 512)
 
-        def WQ(k, g):
-            quantize(f"w{k}{g}", ("w", k, g), T["grouped", k, g][:], 512)
+        def x_operand(span, g):
+            first, count = SPANS[span]
+            key, half = x_place(first // 2, g)
+            return ("x",) + key, block(2 * half, count)
 
-        def span(s):
-            first, count = SPANS[s]
-            return first, count, count * P, 4 // count
+        def rows_of(k, g):
+            return held["e_raw", g // 2][:, g % 2, :, :] if k == "e" else held["w_raw", g][:, :, k * DEPTH : (k + 1) * DEPTH]
 
-        def US(s, jg, b, tag="mx"):
-            first, count, width, per = span(s)
-            bank = get(tag, ("us", s, jg, b), [P, 512], F32)
-            for tt in range(per):
-                t = per * b + tt
+        def grouped(ring, key):
+            return tile("ring_" + ring, key, [P, SLOTS * DEPTH], BF16)
+
+        def gpsimd_move(out, in_):
+            nc.gpsimd.tensor_scalar(out=out, in0=in_, scalar1=1.0, scalar2=0.0, op0=ALU.mult, op1=ALU.add)
+
+        def interleave_w(jg, g, ring, on_gpsimd=False):
+            out, raw = grouped(ring, ("grouped", jg, g))[:], rows_of(jg, g)
+            walk = "p c t i j" if on_gpsimd else "p c t j i"
+            move = gpsimd_move if on_gpsimd else nc.scalar.copy
+            move(out=out.rearrange("p (t c i j) -> " + walk, t=SLOTS, i=4, j=SLOTS), in_=raw.rearrange("p j (c t i) -> " + walk, t=SLOTS, i=4))
+
+        def interleave_rows(out, rows, move):
+            if move is gpsimd_move:
+                move(out=out.rearrange("p (c j) -> p c j", j=SLOTS), in_=rows.rearrange("p j c -> p c j"))
+            else:
+                move(out=out.rearrange("p (c i j) -> p c j i", i=4, j=SLOTS), in_=rows.rearrange("p j (c i) -> p c j i", i=4))
+
+        def interleave_e(g, ring, move, lo=0, hi=4):
+            interleave_rows(grouped(ring, ("grouped", "e", g))[:, lo * DEPTH : hi * DEPTH], rows_of("e", g)[:, :, lo * P : hi * P], move)
+
+        def interleave_w_on_tensor(jg, g, ring):
+            for t in range(SLOTS):
+                nc.tensor.matmul(
+                    bank("A", ("moved", t // 2), [P, 2, DEPTH], BF16)[:, t % 2, :].rearrange("p (c i j) -> p j c i", i=4, j=SLOTS),
+                    lhsT=ident_bf[:],
+                    rhs=rows_of(jg, g).rearrange("p j (c t i) -> p t j c i", t=SLOTS, i=4)[:, t, :, :, :],
+                    start=True,
+                    stop=True,
+                )
+            for half in range(2):
+                out = grouped(ring, ("grouped", jg, g))[:, half * 1024 : (half + 1) * 1024]
+                nc.scalar.copy(out=out, in_=held["moved", half][:].rearrange("p t c -> p (t c)"))
+
+        def quantize_w(k, g):
+            quantize(("w", k, g), held["grouped", k, g][:], DEPTH)
+
+        def u_pass(jg, g, ring, slots=range(SLOTS)):
+            for t in slots:
+                mx(bank(ring, ("u", 0, jg, t), [P, 512])[:], ("w", jg, g), block(t), *x_operand(0, g), g == 0, g == PASSES - 1)
+
+        def u_bank(span, jg, b, ring):
+            out = bank(ring, ("u", span, jg, b), [P, 512])
+            for t in range(2):
                 for g in range(PASSES):
-                    mx(bank[:, tt * width : (tt + 1) * width], ("w", jg, g), slice(t * P, (t + 1) * P), *x_op(first, g, count), g == 0, g == PASSES - 1)
+                    mx(out[:, block(2 * t, 2)], ("w", jg, g), block(2 * b + t), *x_operand(span, g), g == 0, g == PASSES - 1)
 
-        def UG(s, jg, g, start, stop, tag="mx"):
-            first, count, width, per = span(s)
-            for t in range(4):
-                bank = get(tag, ("us", s, jg, t), [P, 512], F32)
-                mx(bank[:], ("w", jg, g), slice(t * P, (t + 1) * P), *x_op(first, g, count), start, stop)
-
-        def C(s, jg, b):
-            first, count, width, per = span(s)
-            y = get(f"y{count}", ("y", s, jg), [P, 4, width], F32)
+        def factor(span, jg, b):
+            first, count = SPANS[span]
+            per = SLOTS // count
+            y = tile("y%d" % count, ("y", span, jg), [P, SLOTS, count * P], F32)
             nc.vector.tensor_tensor(
                 out=y[:, per * b : per * (b + 1), :],
-                in0=T["us", s, jg, b][:].rearrange("p (t m) -> p t m", t=per),
-                in1=cf_b[:, first * P : first * P + width].unsqueeze(1).to_broadcast([P, per, width]),
+                in0=held["u", span, jg, b][:].rearrange("p (t m) -> p t m", t=per),
+                in1=factor_row[:, block(first, count)].unsqueeze(1).to_broadcast([P, per, count * P]),
                 op=ALU.mult,
             )
 
-        def SI(s, jg, lo=0, hi=4):
-            first, count, width, per = span(s)
-            y = get(f"y{count}", ("y", s, jg), [P, 4, width], F32)
-            for t in range(lo, hi):
-                b, tt = divmod(t, per)
-                src = T["ut", s, jg, b][:, tt * width : (tt + 1) * width] if ("ut", s, jg, 0) in T else y[:, t, :]
-                nc.scalar.activation(out=y[:, t, :], in_=src, func=ACT.Silu, bias=pb_t[:, jg, t : t + 1])
+        def silu(span, jg, slots=range(SLOTS)):
+            y = held["y", span, jg]
+            for t in slots:
+                nc.scalar.activation(out=y[:, t, :], in_=y[:, t, :], func=ACT.Silu, bias=bias_col[:, jg, t : t + 1])
 
-        def G(s, jg, lo=0, hi=4):
-            first, count, width, per = span(s)
-            dst = get(f"ag{count}", ("ag", s, jg), [P, 4 * width], BF16)
-            a, b = lo * width // 4, hi * width // 4
+        def gained(span, jg, tag=None):
+            count = SPANS[span][1]
+            return tile(tag or "gained%d" % count, ("gained", span, jg), [P, SLOTS * count * P], BF16)
+
+        def gain_on_vector(span, jg):
+            width = SPANS[span][1] * P
             nc.vector.tensor_tensor(
-                out=dst[:, 4 * a : 4 * b].rearrange("p (c i t) -> p c t i", i=GAIN_RUN, t=4),
-                in0=T["y", s, jg][:, :, a:b].rearrange("p t (c i) -> p c t i", i=GAIN_RUN),
-                in1=ag_t[:, jg, :].unsqueeze(1).unsqueeze(3).to_broadcast([P, (b - a) // GAIN_RUN, 4, GAIN_RUN]),
+                out=gained(span, jg)[:].rearrange("p (c i t) -> p c t i", i=4, t=SLOTS),
+                in0=held["y", span, jg][:].rearrange("p t (c i) -> p c t i", i=4),
+                in1=gain_col[:, jg, :].unsqueeze(1).unsqueeze(3).to_broadcast([P, width // 4, SLOTS, 4]),
                 op=ALU.mult,
             )
 
-        def GG(s, jg, ring="H", lo=0, hi=4):
-            first, count, width, per = span(s)
-            dst = get("grouped_" + ring, ("ag", s, jg), [P, 4 * width], BF16)
-            a, b = lo * width // 4, hi * width // 4
+        def gain_on_gpsimd(span, jg, ring):
+            width = SPANS[span][1] * P
             nc.gpsimd.tensor_tensor(
-                out=dst[:, 4 * a : 4 * b].rearrange("p (c t) -> p c t", t=4),
-                in0=T["y", s, jg][:, :, a:b].rearrange("p t c -> p c t"),
-                in1=ag_t[:, jg, :].unsqueeze(1).to_broadcast([P, b - a, 4]),
+                out=gained(span, jg, "ring_" + ring)[:].rearrange("p (c t) -> p c t", t=SLOTS),
+                in0=held["y", span, jg][:].rearrange("p t c -> p c t"),
+                in1=gain_col[:, jg, :].unsqueeze(1).to_broadcast([P, width, SLOTS]),
                 op=ALU.mult,
             )
 
-        def GS(s, jg, tag="planes"):
-            first, count, width, per = span(s)
-            planes = get(tag, ("planes", s, jg), [P, 4, width], BF16)
-            for t in range(4):
-                nc.scalar.activation(out=planes[:, t, :], in_=T["y", s, jg][:, t, :], func=ACT.Copy, scale=ag_t[:, jg, t : t + 1])
+        def gain_on_scalar(span, jg):
+            planes = tile("a_planes", "a_planes", [P, SLOTS, SPANS[span][1] * P], BF16)
+            for t in range(SLOTS):
+                nc.scalar.activation(out=planes[:, t, :], in_=held["y", span, jg][:, t, :], func=ACT.Copy, scale=gain_col[:, jg, t : t + 1])
 
-        def GI(s, jg):
-            first, count, width, per = span(s)
-            dst = get(f"ag{count}", ("ag", s, jg), [P, 4 * width], BF16)
-            nc.vector.tensor_copy(out=dst[:].rearrange("p (c i t) -> p c t i", i=4, t=4), in_=T["planes", s, jg][:].rearrange("p t (c i) -> p c t i", i=4))
+        def quantize_a(span, jg):
+            quantize(("a", span, jg), held["gained", span, jg][:], SPANS[span][1] * P)
 
-        def AQ(s, jg):
-            quantize(f"a{s}{jg}", ("a", s, jg), T["ag", s, jg][:], SPANS[s][1] * P)
+        def v_pass(jg, g, t, ring, start, stop):
+            mx(bank(ring, ("v", jg, t), [P, WIDE])[:], ("w", jg, g), block(t), ("w", "e", g), slice(0, WIDE), start, stop)
 
-        def VM(jg, t, tag="mx"):
-            bank = get(tag, ("v", jg, t), [P, 512], F32)
+        def v_bank(jg, t, ring):
             for g in range(PASSES):
-                mx(bank[:], ("w", jg, g), slice(t * P, (t + 1) * P), ("w", "e", g), slice(0, 512), g == 0, g == PASSES - 1)
+                v_pass(jg, g, t, ring, g == 0, g == PASSES - 1)
 
-        def VP(jg, g, start, stop, tag="mx", lo=0, hi=4):
-            for t in range(lo, hi):
-                bank = get(tag, ("v", jg, t), [P, 512], F32)
-                mx(bank[:], ("w", jg, g), slice(t * P, (t + 1) * P), ("w", "e", g), slice(0, 512), start, stop)
+        def load_gain(jg):
+            planes = tile("v_planes", ("v_planes", jg), [P, SLOTS, WIDE], BF16)
+            for t in range(SLOTS):
+                nc.scalar.activation(out=planes[:, t, :], in_=held["v", jg, t][:], func=ACT.Copy, scale=loading_col[:, jg, t : t + 1])
 
-        def VS(jg, t):
-            vl = get("vl", ("vl", jg), [P, 4, H], BF16)
-            nc.scalar.activation(out=vl[:, t, :], in_=T["v", jg, t][:], func=ACT.Copy, scale=lg_t[:, jg, t : t + 1])
+        def interleave_v(jg, ring, move, lo=0, hi=WIDE):
+            interleave_rows(grouped(ring, ("grouped", "v", jg))[:, SLOTS * lo : SLOTS * hi], held["v_planes", jg][:, :, lo:hi], move)
 
-        def VI(jg, on, ring=None, lo=0, hi=H):
-            dst = get("grouped_" + (ring or on), ("grouped", "v", jg), [P, 2048], BF16)[:, 4 * lo : 4 * hi]
-            src = T["vl", jg][:, :, lo:hi]
-            if on == "G":
-                nc.gpsimd.tensor_scalar(
-                    out=dst.rearrange("p (c t) -> p c t", t=4), in0=src.rearrange("p t c -> p c t"), scalar1=1.0, scalar2=0.0, op0=ALU.mult, op1=ALU.add
-                )
-            else:
-                copy = nc.vector.tensor_copy if on == "V" else nc.scalar.copy
-                copy(out=dst.rearrange("p (c i t) -> p c t i", i=4, t=4), in_=src.rearrange("p t (c i) -> p c t i", i=4))
+        def quantize_v(jg):
+            quantize(("v", jg), held["grouped", "v", jg][:], WIDE)
 
-        def VQ(jg):
-            quantize(f"v{jg}", ("v", jg), T["grouped", "v", jg][:], H)
+        def a_operand(i, jg, count):
+            span = max(n for n in range(len(SPANS)) if SPANS[n][0] <= i)
+            return ("a", span, jg), block(i - SPANS[span][0], count)
 
-        def a_op(i, jg, count):
-            s = [n for n, (first, many) in enumerate(SPANS) if first <= i < first + many][0]
-            return ("a", s, jg), slice((i - SPANS[s][0]) * P, (i - SPANS[s][0] + count) * P)
-
-        def tiles(o):
-            return slice(OUTS[o][0], OUTS[o][0] + OUTS[o][1])
-
-        def part(key, o):
-            return get("raw", key, [P, TILES, LATENT], F32)[:, tiles(o), :]
-
-        def ST(key, o):
-            out = {"mu": mu_out, "sd": sd_out, "z": z_out}[key]
-            nc.sync.dma_start(out=rows(out)[:, tiles(o), :], in_=part(key, o))
-
-        def QM(o):
-            first, count = OUTS[o]
-            bank = get("mx", ("qm", o), [P, count, LATENT], F32)
-            for i2 in range(count):
+        def q_mean(piece):
+            first, count = PIECES[piece]
+            out = bank("B", ("q_mean", piece), [P, count, LATENT])
+            for i in range(count):
                 for jg in range(GROUPS):
-                    mx(bank[:, i2, :], *a_op(first + i2, jg, 1), ("v", jg), slice(0, LATENT), jg == 0, jg == GROUPS - 1)
+                    mx(out[:, i, :], *a_operand(first + i, jg, 1), ("v", jg), slice(0, LATENT), jg == 0, jg == GROUPS - 1)
 
-        def MB(o):
-            first, count = OUTS[o]
-            nc.vector.tensor_tensor(out=part("mu", o), in0=T["qm", o][:], in1=lb_b[:, 0:LATENT].unsqueeze(1).to_broadcast([P, count, LATENT]), op=ALU.add)
+        def add_mean_bias(piece):
+            bias = mean_bias[:].unsqueeze(1).to_broadcast([P, PIECES[piece][1], LATENT])
+            nc.vector.tensor_tensor(out=result("mu", piece), in0=held["q_mean", piece][:], in1=bias, op=ALU.add)
 
-        def QL(o, tag="mx"):
-            first, count = OUTS[o]
-            bank = get(tag, ("ql", o), [P, 2, count * P], F32)
+        def q_logvar(piece, ring):
+            first, count = PIECES[piece]
+            out = bank(ring, ("q_logvar", piece), [P, 2, count * P])
             for h in range(2):
                 for jg in range(GROUPS):
-                    mx(bank[:, h, :], ("v", jg), slice(LATENT + h * P, LATENT + (h + 1) * P), *a_op(first, jg, count), jg == 0, jg == GROUPS - 1)
+                    mx(out[:, h, :], ("v", jg), block(2 + h), *a_operand(first, jg, count), jg == 0, jg == GROUPS - 1)
 
-        def TL(o):
-            first, count = OUTS[o]
-            th = get("uy", ("th", o), [P, 2, count * P], F32)
+        def tanh(piece):
+            out = tile("tanh", ("tanh", piece), [P, 2, PIECES[piece][1] * P], F32)
             for h in range(2):
-                nc.scalar.activation(out=th[:, h, :], in_=T["ql", o][:, h, :], func=ACT.Tanh, bias=vec_cols[:, 24 + h : 25 + h])
+                bias = vector_cols[:, BIAS_ROW + h : BIAS_ROW + h + 1]
+                nc.scalar.activation(out=out[:, h, :], in_=held["q_logvar", piece][:, h, :], func=ACT.Tanh, bias=bias)
 
-        def LT(o, tag="tr"):
-            first, count = OUTS[o]
-            bank = get(tag, ("lt", o), [P, count, LATENT], F32)
-            for i2 in range(count):
+        def turn_back(piece, ring):
+            count = PIECES[piece][1]
+            out = bank(ring, ("turned_back", piece), [P, count, LATENT])
+            for i in range(count):
                 for h in range(2):
-                    nc.tensor.transpose(bank[:, i2, h * P : (h + 1) * P], T["th", o][:, h, i2 * P : (i2 + 1) * P], ident[:])
+                    nc.tensor.transpose(out[:, i, block(h)], held["tanh", piece][:, h, block(i)], ident[:])
 
-        def EL(o):
-            nc.scalar.activation(out=part("sd", o), in_=T["lt", o][:], func=ACT.Exp, scale=0.5)
+        def exp(piece):
+            nc.scalar.activation(out=result("sd", piece), in_=held["turned_back", piece][:], func=ACT.Exp, scale=0.5)
 
-        def ZM(o, on="V"):
-            eng = nc.vector if on == "V" else nc.gpsimd
-            eng.tensor_tensor(out=part("z", o), in0=part("sd", o), in1=T["noise"][:, tiles(o), :], op=ALU.mult)
+        def spread(piece):
+            nc.vector.tensor_tensor(out=result("z", piece), in0=result("sd", piece), in1=held["noise"][:, tiles_of(piece), :], op=ALU.mult)
 
-        def ZA(o, on="V"):
-            eng = nc.vector if on == "V" else nc.gpsimd
-            eng.tensor_tensor(out=part("z", o), in0=part("z", o), in1=part("mu", o), op=ALU.add)
+        def shift(piece):
+            nc.vector.tensor_tensor(out=result("z", piece), in0=result("z", piece), in1=result("mu", piece), op=ALU.add)
 
-        WARM()
+        on_scalar, on_vector = nc.scalar.copy, nc.vector.tensor_copy
+        low, high = range(0, 2), range(2, 4)
 
-        load_cf(); load_x(0, 0, 1); load_x(0, 1, 4); load_xs(); load_x(1)
-        for g in range(4): load_w(g)
+        warm = sb.tile([P, 2], F32, name="warm")
+        nc.vector.memset(warm[:], 0.0)
+        nc.scalar.activation(out=warm[:, 1:2], in_=warm[:, 0:1], func=ACT.Silu)
+
+        nc.sync.dma_start(out=factor_col[:], in_=cell_factor.rearrange("(p i) -> p i", i=TILES))
+        load_x(0, 0, 1)
+        load_x(0, 1, 2)
+        nc.sync.dma_start(out=gene_scale[:], in_=x_scale.rearrange("o (g p t) -> p (o g) t", p=P, t=SLOTS))
+        load_x(0, 2, 4)
+        load_x(1)
+        for g in range(PASSES):
+            load_w(g)
         load_x(2)
-        for g in range(4): load_e(g)
-        load_small(); load_x(3); load_late()
-        K(0, "S", 0, 1); K(1, "V", 0, 1); CF(0, 8); CC(); K(0, "S", 1, 4); K(1, "V", 1, 4); K(2); K(3)
-        XT(0, 0); PP(0, 0)
-        D(0, 0, "G"); D(1, 0, "S"); D(0, 1, "G", ring="H"); D(1, 1, "S"); D(0, 2, "S")
-        for g in range(1, 4): XT(0, g); PP(0, g)
-        for g in range(4): XT(1, g, "mx"); PP(1, g)
-        D(0, 3, "S")
-        for t in range(4): PI(1, 2, t)
-        PC(1, 2, 0, "I"); PC(1, 2, 1, "I")
-        for g in range(4): XQ(0, g); WQ(0, g); UG(0, 0, g, g == 0, g == 3)
-        D(1, 3, "S", ring="H"); K(4); K(5)
-        WQ(1, 0); UG(0, 1, 0, True, False, "tr"); WQ(1, 1); WQ(1, 2); WQ(1, 3)
-        D("e", 0, "G", ring="H"); D("e", 1, "G"); D("e", 3, "S")
-        for t in range(4): C(0, 0, t)
-        XT(2, 0, "mx"); XT(2, 1, "mx"); UG(0, 1, 1, False, False); XT(2, 2, "mx"); XT(2, 3, "mx"); VT(); UG(0, 1, 2, False, False); UG(0, 1, 3, False, True)
-        for g in range(4): PP(2, g)
-        K(6); K(7); VC(); D("e", 2, "S", ring="I"); XT(3, 0, "mx"); XT(3, 1, "mx")
-        for g in (3, 1, 2, 0): WQ("e", g); VP(0, g, g == 3, g == 0, "mx", 0, 2)
-        for t in range(4): C(0, 1, t)
-        VM(0, 2, "tr"); VM(0, 3, "tr"); XT(3, 2); XT(3, 3)
-        load_noise()
-        SI(0, 0); GG(0, 0)
-        for t in range(4): VS(0, t)
-        SI(0, 1)
-        for g in range(4): PP(3, g)
-        for t in range(4): VM(1, t)
+        for g in range(PASSES):
+            load_e(g)
+        load_x(3)
+        load_vectors()
 
-        VI(0, "G", hi=192); VI(0, "S", lo=192)
-        XQ(2, 0); XQ(2, 1); AQ(0, 0); XQ(3, 0); XQ(3, 1); VQ(0)
-        GS(0, 1)
-        for t in range(4): VS(1, t)
-        US(1, 0, 0, "tr"); US(1, 0, 1, "tr"); US(1, 1, 0, "tr"); US(1, 1, 1, "tr"); US(2, 0, 0); US(2, 0, 1)
-        GI(0, 1); C(1, 0, 0); C(1, 0, 1); SI(1, 0); VI(1, "S", ring="I"); AQ(0, 1); C(1, 1, 0); C(1, 1, 1); SI(1, 1); G(1, 0); AQ(1, 0); VQ(1); GG(1, 1, "I")
-        US(2, 1, 0); US(2, 1, 1)
-        C(2, 0, 0); C(2, 0, 1); SI(2, 0); C(2, 1, 0); SI(2, 1, 0, 2); C(2, 1, 1)
-        QM(0); QL(0, "tr"); QL(1, "tr"); SI(2, 1, 2, 4); TL(0); TL(1); QM(1); LT(0); LT(1)
-        MB(0); AQ(1, 1); G(2, 0); G(2, 1); AQ(2, 0); MB(1); AQ(2, 1); ST("mu", 0); ST("mu", 1)
-        QL(2, "tr"); QM(2); QL(3, "tr"); QL(4); QM(3); QM(4)
-        EL(0); EL(1); TL(2); TL(3); TL(4); LT(2); LT(3); LT(4, "mx"); EL(2); EL(3); EL(4)
-        ST("sd", 0); MB(2); ST("sd", 1); ST("mu", 2)
-        ZM(0); ZM(1); ZA(0); ST("z", 0); ZA(1); MB(3); MB(4); ST("sd", 2); ST("z", 1); ST("sd", 3); ST("sd", 4); ST("mu", 3); ST("mu", 4)
-        ZM(2); ZM(3); ZA(2); ST("z", 2); ZM(4); ZA(3); ST("z", 3); ZA(4); ST("z", 4)
+        widen(0, on_scalar, 0, 1)
+        widen(1, on_vector, 0, 1)
+        spread_factor = bank("B", "factor", [P, CELLS], BF16)
+        for i in range(TILES):
+            nc.tensor.matmul(spread_factor[:, block(i)], lhsT=factor_col[:, i : i + 1].to_broadcast([P, P]), rhs=ident_bf[:], start=True, stop=True)
+        on_vector(out=factor_row[:], in_=spread_factor[:])
+        widen(0, on_scalar, 1, 2)
+        widen(1, on_vector, 1, 2)
+        for i in range(2):
+            widen(i, on_scalar, 2, 4)
+        for i in (2, 3):
+            widen(i, on_scalar)
+        for pair, ring in enumerate("AB"):
+            for g in range(PASSES):
+                turn_x(pair, g, ring)
+                scale_x(pair, g)
+        for g, ring in enumerate("gh"):
+            interleave_w(0, g, ring, on_gpsimd=True)
+            interleave_w(1, g, "s")
+        for g in (2, 3):
+            interleave_w(0, g, "s")
+        interleave_w_on_tensor(1, 2, "i")
+
+        for g in range(PASSES):
+            quantize_x(0, g)
+            quantize_w(0, g)
+            u_pass(0, g, "B")
+        interleave_w(1, 3, "h")
+        for i in (4, 5):
+            widen(i, on_scalar)
+        for g in range(PASSES):
+            quantize_w(1, g)
+
+        for g, ring in enumerate("hg"):
+            interleave_e(g, ring, gpsimd_move)
+        interleave_e(3, "s", on_scalar)
+        u_pass(1, 0, "A")
+        u_pass(1, 1, "A", low)
+        for t in range(SLOTS):
+            factor(0, 0, t)
+        for g in low:
+            turn_x(2, g, "B")
+        u_pass(1, 1, "A", high)
+        u_pass(1, 2, "A", low)
+        for g in high:
+            turn_x(2, g, "B")
+        vectors = bank("B", "vectors", [P, P], BF16)
+        nc.tensor.transpose(vectors[:], vector_rows[:], ident_bf[:])
+        u_pass(1, 2, "A", high)
+        u_pass(1, 3, "A", low)
+        for g in range(PASSES):
+            scale_x(2, g)
+        for i in (6, 7):
+            widen(i, on_scalar)
+        on_scalar(out=vector_cols[:], in_=vectors[:, 0:VECTOR_ROWS])
+        interleave_e(2, "i", on_scalar, hi=E2_ON_SCALAR)
+        for g in low:
+            turn_x(3, g, "B")
+        u_pass(1, 3, "A", high)
+
+        order = (3, 1, 2, 0)
+        for g in order:
+            quantize_w("e", g)
+            for t in low:
+                v_pass(0, g, t, "B", g == order[0], g == order[-1])
+            if g == order[0]:
+                interleave_e(2, "i", on_vector, lo=E2_ON_SCALAR)
+
+        for t in range(SLOTS):
+            factor(0, 1, t)
+        for t in high:
+            v_bank(0, t, "A")
+        for g in high:
+            turn_x(3, g, "A")
+        nc.sync.dma_start(out=tile("big", "noise", [P, TILES, LATENT], BF16)[:], in_=by_tile(noise))
+        silu(0, 0)
+        gain_on_gpsimd(0, 0, "h")
+        load_gain(0)
+        silu(0, 1)
+        for g in range(PASSES):
+            scale_x(3, g)
+        for t in range(SLOTS):
+            v_bank(1, t, "B")
+        interleave_v(0, "g", gpsimd_move, hi=V0_ON_GPSIMD)
+        interleave_v(0, "g", on_scalar, lo=V0_ON_GPSIMD)
+
+        for half in range(2):
+            quantize_x(2, half)
+        quantize_a(0, 0)
+        for half in range(2):
+            quantize_x(3, half)
+        quantize_v(0)
+        gain_on_scalar(0, 1)
+        load_gain(1)
+        for span, ring in ((1, "A"), (2, "B")):
+            for jg in range(GROUPS):
+                for b in range(2):
+                    u_bank(span, jg, b, ring)
+        interleave_rows(gained(0, 1)[:], held["a_planes"][:], on_vector)
+        for b in range(2):
+            factor(1, 0, b)
+        silu(1, 0)
+        interleave_v(1, "i", on_scalar)
+        quantize_a(0, 1)
+        for b in range(2):
+            factor(1, 1, b)
+        silu(1, 1)
+        gain_on_vector(1, 0)
+        quantize_a(1, 0)
+        quantize_v(1)
+
+        gain_on_gpsimd(1, 1, "i")
+        for jg in range(GROUPS):
+            for b in range(2):
+                factor(2, jg, b)
+            silu(2, jg)
+        q_mean(0)
+        for piece in range(2):
+            q_logvar(piece, "A")
+            tanh(piece)
+        q_mean(1)
+        for piece in range(2):
+            turn_back(piece, "A")
+        add_mean_bias(0)
+        quantize_a(1, 1)
+        for jg in range(GROUPS):
+            gain_on_vector(2, jg)
+        quantize_a(2, 0)
+        add_mean_bias(1)
+        quantize_a(2, 1)
+        for piece in range(2):
+            store("mu", piece)
+
+        q_logvar(2, "A")
+        q_mean(2)
+        q_logvar(3, "A")
+        q_logvar(4, "B")
+        for piece in (3, 4):
+            q_mean(piece)
+        for piece in range(2):
+            exp(piece)
+        for piece in (2, 3, 4):
+            tanh(piece)
+        for piece, ring in ((2, "A"), (3, "A"), (4, "B")):
+            turn_back(piece, ring)
+            exp(piece)
+        store("sd", 0)
+        add_mean_bias(2)
+        store("sd", 1)
+        store("mu", 2)
+        for step in (spread, shift):
+            for piece in range(2):
+                step(piece)
+        for piece in (3, 4):
+            add_mean_bias(piece)
+        store("z", 0)
+        store("sd", 2)
+        store("z", 1)
+        for name in ("sd", "mu"):
+            for piece in (3, 4):
+                store(name, piece)
+        spread(2)
+        for piece in (2, 3, 4):
+            if piece + 1 < len(PIECES):
+                spread(piece + 1)
+            shift(piece)
+            store("z", piece)

@@ -26,7 +26,7 @@ SPANS = [(0, 4), (4, 2), (6, 2)]
 PIECES = [(0, 2), (2, 2), (4, 2), (6, 1), (7, 1)]
 BIAS_ROW = 24
 VECTOR_ROWS = 26
-V0_ON_GPSIMD = 192
+CELLS_ON_GPSIMD = 128
 E2_ON_SCALAR = 3
 BUFFERS = {"x_raw": 2, "big": 4, "x_wide": 4, "x_scaled": 4, "ring_s": 4, "y4": 2, "y2": 4, "tanh": 4, "gained2": 3, "v_planes": 2}
 
@@ -99,9 +99,10 @@ def tile_pathway_latent_encoder_f5_kernel(
         def result(name, piece):
             return tile("big", name, [P, TILES, LATENT], F32)[:, tiles_of(piece), :]
 
-        def store(name, piece):
+        def store(name, *pieces):
             out = {"mu": mu_out, "sd": sd_out, "z": z_out}[name]
-            nc.sync.dma_start(out=by_tile(out)[:, tiles_of(piece), :], in_=result(name, piece))
+            tiles = slice(tiles_of(pieces[0]).start, tiles_of(pieces[-1]).stop)
+            nc.sync.dma_start(out=by_tile(out)[:, tiles, :], in_=held[name][:, tiles, :])
 
         def quantize(key, src, width):
             name = "".join(str(part) for part in key)
@@ -231,19 +232,19 @@ def tile_pathway_latent_encoder_f5_kernel(
                 op=ALU.mult,
             )
 
-        def gain_on_gpsimd(span, jg, ring):
-            width = SPANS[span][1] * P
+        def gain_on_gpsimd(span, jg, tag=None, width=None):
+            width = width or SPANS[span][1] * P
             nc.gpsimd.tensor_tensor(
-                out=gained(span, jg, "ring_" + ring)[:].rearrange("p (c t) -> p c t", t=SLOTS),
-                in0=held["y", span, jg][:].rearrange("p t c -> p c t"),
+                out=gained(span, jg, tag)[:, 0 : SLOTS * width].rearrange("p (c t) -> p c t", t=SLOTS),
+                in0=held["y", span, jg][:, :, 0:width].rearrange("p t c -> p c t"),
                 in1=gain_col[:, jg, :].unsqueeze(1).to_broadcast([P, width, SLOTS]),
                 op=ALU.mult,
             )
 
-        def gain_on_scalar(span, jg):
-            planes = tile("a_planes", "a_planes", [P, SLOTS, SPANS[span][1] * P], BF16)
+        def gain_on_scalar(span, jg, lo):
+            planes = tile("a_planes", "a_planes", [P, SLOTS, SPANS[span][1] * P - lo], BF16)
             for t in range(SLOTS):
-                nc.scalar.activation(out=planes[:, t, :], in_=held["y", span, jg][:, t, :], func=ACT.Copy, scale=gain_col[:, jg, t : t + 1])
+                nc.scalar.activation(out=planes[:, t, :], in_=held["y", span, jg][:, t, lo:], func=ACT.Copy, scale=gain_col[:, jg, t : t + 1])
 
         def quantize_a(span, jg):
             quantize(("a", span, jg), held["gained", span, jg][:], SPANS[span][1] * P)
@@ -255,13 +256,13 @@ def tile_pathway_latent_encoder_f5_kernel(
             for g in range(PASSES):
                 v_pass(jg, g, t, ring, g == 0, g == PASSES - 1)
 
-        def load_gain(jg):
+        def load_gain(jg, slots=range(SLOTS)):
             planes = tile("v_planes", ("v_planes", jg), [P, SLOTS, WIDE], BF16)
-            for t in range(SLOTS):
+            for t in slots:
                 nc.scalar.activation(out=planes[:, t, :], in_=held["v", jg, t][:], func=ACT.Copy, scale=loading_col[:, jg, t : t + 1])
 
-        def interleave_v(jg, ring, move, lo=0, hi=WIDE):
-            interleave_rows(grouped(ring, ("grouped", "v", jg))[:, SLOTS * lo : SLOTS * hi], held["v_planes", jg][:, :, lo:hi], move)
+        def interleave_v(jg, ring):
+            interleave_rows(grouped(ring, ("grouped", "v", jg))[:], held["v_planes", jg][:], nc.scalar.copy)
 
         def quantize_v(jg):
             quantize(("v", jg), held["grouped", "v", jg][:], WIDE)
@@ -407,15 +408,16 @@ def tile_pathway_latent_encoder_f5_kernel(
             turn_x(3, g, "A")
         nc.sync.dma_start(out=tile("big", "noise", [P, TILES, LATENT], BF16)[:], in_=by_tile(noise))
         silu(0, 0)
-        gain_on_gpsimd(0, 0, "h")
-        load_gain(0)
+        gain_on_gpsimd(0, 0, "ring_h")
+        load_gain(0, low)
         silu(0, 1)
+        gain_on_gpsimd(0, 1, width=CELLS_ON_GPSIMD)
+        load_gain(0, high)
         for g in range(PASSES):
             scale_x(3, g)
         for t in range(SLOTS):
             v_bank(1, t, "B")
-        interleave_v(0, "g", gpsimd_move, hi=V0_ON_GPSIMD)
-        interleave_v(0, "g", on_scalar, lo=V0_ON_GPSIMD)
+        interleave_v(0, "g")
 
         for half in range(2):
             quantize_x(2, half)
@@ -423,17 +425,17 @@ def tile_pathway_latent_encoder_f5_kernel(
         for half in range(2):
             quantize_x(3, half)
         quantize_v(0)
-        gain_on_scalar(0, 1)
+        gain_on_scalar(0, 1, CELLS_ON_GPSIMD)
         load_gain(1)
         for span, ring in ((1, "A"), (2, "B")):
             for jg in range(GROUPS):
                 for b in range(2):
                     u_bank(span, jg, b, ring)
-        interleave_rows(gained(0, 1)[:], held["a_planes"][:], on_vector)
+        interleave_rows(gained(0, 1)[:, SLOTS * CELLS_ON_GPSIMD :], held["a_planes"][:], on_vector)
         for b in range(2):
             factor(1, 0, b)
         silu(1, 0)
-        interleave_v(1, "i", on_scalar)
+        interleave_v(1, "i")
         quantize_a(0, 1)
         for b in range(2):
             factor(1, 1, b)
@@ -442,7 +444,7 @@ def tile_pathway_latent_encoder_f5_kernel(
         quantize_a(1, 0)
         quantize_v(1)
 
-        gain_on_gpsimd(1, 1, "i")
+        gain_on_gpsimd(1, 1, "ring_i")
         for jg in range(GROUPS):
             for b in range(2):
                 factor(2, jg, b)
@@ -490,8 +492,7 @@ def tile_pathway_latent_encoder_f5_kernel(
         store("sd", 2)
         store("z", 1)
         for name in ("sd", "mu"):
-            for piece in (3, 4):
-                store(name, piece)
+            store(name, 3, 4)
         spread(2)
         for piece in (2, 3, 4):
             if piece + 1 < len(PIECES):

@@ -24,11 +24,10 @@ FLOPS = 2 * CELLS * GENES * PATHWAYS + 2 * GENES * PATHWAYS * WIDE + 2 * CELLS *
 
 SPANS = [(0, 4), (4, 2), (6, 2)]
 PIECES = [(0, 2), (2, 2), (4, 2), (6, 1), (7, 1)]
-BIAS_ROW = 24
-VECTOR_ROWS = 26
-CELLS_ON_GPSIMD = 128
-E2_ON_SCALAR = 3
-BUFFERS = {"x_raw": 2, "big": 4, "x_wide": 4, "x_scaled": 4, "ring_s": 4, "y4": 2, "y2": 4, "tanh": 4, "gained2": 3, "v_planes": 2}
+VECTOR_ROWS = 8
+E_SPLIT = 384
+CELLS_ON_GPSIMD = 384
+BUFFERS = {"x_raw": 2, "big": 4, "x_wide": 4, "x_scaled": 4, "ring": 4, "y4": 2, "y2": 4, "tanh": 4, "gained2": 2, "v_planes": 2}
 
 
 def tile_pathway_latent_encoder_f5_kernel(
@@ -37,7 +36,7 @@ def tile_pathway_latent_encoder_f5_kernel(
     nc = tc.nc
     with ExitStack() as ctx:
         sb = ctx.enter_context(tc.tile_pool(name="sb", bufs=1))
-        banks = {ring: ctx.enter_context(tc.psum_pool(name="banks_" + ring, bufs=4)) for ring in "AB"}
+        psum = ctx.enter_context(tc.psum_pool(name="banks", bufs=1))
         ctx.enter_context(tc.manual_schedule())
         held = {}
 
@@ -46,9 +45,9 @@ def tile_pathway_latent_encoder_f5_kernel(
                 held[key] = sb.tile(shape, dtype, name=tag, bufs=BUFFERS.get(tag, 1), align_bytes=64)
             return held[key]
 
-        def bank(ring, key, shape, dtype=F32):
+        def bank(number, key, shape, dtype=F32):
             if key not in held:
-                held[key] = banks[ring].tile(shape, dtype, name="bank_" + ring)
+                held[key] = psum.tile(shape, dtype, name="bank%d" % number)
             return held[key]
 
         def by_tile(ap):
@@ -58,21 +57,26 @@ def tile_pathway_latent_encoder_f5_kernel(
             return slice(n * P, (n + count) * P)
 
         ident = sb.tile([P, P], F32, name="ident")
-        make_identity(nc, ident[:])
         ident_bf = sb.tile([P, P], BF16, name="ident_bf")
         make_identity(nc, ident_bf[:])
+        make_identity(nc, ident[:])
         gene_scale = sb.tile([P, PASSES, SLOTS], F32, name="gene_scale")
         factor_col = sb.tile([P, TILES], BF16, name="factor_col")
-        vector_rows = sb.tile([P, P], BF16, name="vector_rows")
+        vector_rows = sb.tile([P, DEPTH], BF16, name="vector_rows")
         nc.gpsimd.memset(vector_rows[:], 0.0)
-        vector_cols = sb.tile([P, VECTOR_ROWS], F32, name="vector_cols")
-        bias_col, loading_col, gain_col = (vector_cols[:, 8 * n : 8 * n + 8].rearrange("p (g t) -> p g t", t=SLOTS) for n in range(3))
+        slot_rows = sb.tile([P, SLOTS, P], BF16, name="slot_rows")
+        vector_cols = sb.tile([P, VECTOR_ROWS, 8], F32, name="vector_cols")
+        bias_col, loading_col, gain_col = (vector_cols[:, 2 * n : 2 * n + 2, 0:SLOTS] for n in range(3))
         mean_bias = sb.tile([P, LATENT], BF16, name="mean_bias")
         factor_row = sb.tile([P, CELLS], BF16, name="factor_row")
 
-        def load_x(pair, lo=0, hi=PASSES):
-            raw = tile("x_raw%d" % lo if pair == 0 else "x_raw", ("x_raw", pair, lo), [P, 2, (hi - lo) * DEPTH], U8)
-            nc.sync.dma_start(out=raw[:], in_=by_tile(x_bytes)[:, 2 * pair : 2 * pair + 2, lo * DEPTH : hi * DEPTH])
+        def load_x(first, count, lo=0, hi=PASSES):
+            tag = "x_raw" if first >= 4 else "x_raw%d%d" % (first, lo)
+            raw = tile(tag, ("x_raw", first, lo), [P, count, (hi - lo) * DEPTH], U8)
+            nc.sync.dma_start(out=raw[:], in_=by_tile(x_bytes)[:, first : first + count, lo * DEPTH : hi * DEPTH])
+            for i in range(count):
+                for g in range(lo, hi):
+                    held["x_bytes", first + i, g] = (raw, i, g - lo)
 
         def load_w(g):
             raw = tile("big", ("w_raw", g), [P, SLOTS, PATHWAYS], BF16)
@@ -84,14 +88,8 @@ def tile_pathway_latent_encoder_f5_kernel(
 
         def load_vectors():
             for n, vec in enumerate((pathway_bias, loading_gain, activity_gain)):
-                for jg in range(GROUPS):
-                    row = 8 * n + SLOTS * jg
-                    nc.sync.dma_start(
-                        out=vector_rows[row : row + SLOTS, :].rearrange("t (c i) -> t c i", i=4),
-                        in_=vec[jg * DEPTH : (jg + 1) * DEPTH].rearrange("(c t i) -> t c i", t=SLOTS, i=4),
-                    )
-            nc.sync.dma_start(out=vector_rows[BIAS_ROW:VECTOR_ROWS, :], in_=latent_bias[LATENT:WIDE].rearrange("(h p) -> h p", h=2))
-            nc.sync.dma_start(out=mean_bias[:], in_=latent_bias[0:LATENT].partition_broadcast(P))
+                nc.sync.dma_start(out=vector_rows[2 * n : 2 * n + 2, :], in_=vec.rearrange("(g c) -> g c", g=GROUPS))
+            nc.sync.dma_start(out=vector_rows[6:8, 0:P], in_=latent_bias[LATENT:WIDE].rearrange("(h p) -> h p", h=2))
 
         def tiles_of(piece):
             return slice(PIECES[piece][0], PIECES[piece][0] + PIECES[piece][1])
@@ -104,11 +102,11 @@ def tile_pathway_latent_encoder_f5_kernel(
             tiles = slice(tiles_of(pieces[0]).start, tiles_of(pieces[-1]).stop)
             nc.sync.dma_start(out=by_tile(out)[:, tiles, :], in_=held[name][:, tiles, :])
 
-        def quantize(key, src, width):
+        def quantize(key, src, width, lo=0, hi=None):
             name = "".join(str(part) for part in key)
             codes = tile(name + "_codes", ("codes",) + key, [P, width], U32)
             scales = tile(name + "_scales", ("scales",) + key, [P, width], U8)
-            nc.vector.quantize_mx(out=codes[:].bitcast(FP8X4), scales=scales[:], in_=src)
+            nc.vector.quantize_mx(out=codes[:, lo:hi].bitcast(FP8X4), scales=scales[:, lo:hi], in_=src)
 
         def mx(out, left, left_cols, right, right_cols, start, stop):
             nc.tensor.matmul_mx(
@@ -123,25 +121,26 @@ def tile_pathway_latent_encoder_f5_kernel(
 
         def widen(i, copy, lo=0, hi=PASSES):
             wide = tile("x_wide", ("x_wide", i), [P, GENES], BF16)
-            copy(out=wide[:, lo * DEPTH : hi * DEPTH], in_=held["x_raw", i // 2, lo][:, i % 2, :].bitcast(F8))
+            raw, row, start = held["x_bytes", i, lo]
+            copy(out=wide[:, lo * DEPTH : hi * DEPTH], in_=raw[:, row, start * DEPTH : (start + hi - lo) * DEPTH].bitcast(F8))
 
-        def turn_x(pair, g, ring):
-            out = bank(ring, ("x_turned", pair, g), [P, 512])
+        def turn_x(pair, g, number):
+            out = bank(number, ("x_turned", pair, g), [P, SLOTS, 2, P], BF16)
             for i in range(2):
-                words = held["x_wide", 2 * pair + i][:].bitcast(F32)
-                for u in range(2):
-                    nc.tensor.transpose(out[:, block(2 * u + i)], words[:, 256 * g + u : 256 * (g + 1) : 2], ident[:])
+                genes = held["x_wide", 2 * pair + i][:, g * DEPTH : (g + 1) * DEPTH].rearrange("p (m t) -> p t m", t=SLOTS)
+                for t in range(SLOTS):
+                    nc.tensor.matmul(out[:, t, i, :], lhsT=genes[:, t, :], rhs=ident_bf[:], start=True, stop=True)
 
         def x_place(pair, g):
             return ((0, g), pair) if pair < 2 else ((pair, g // 2), g % 2)
 
-        def scale_x(pair, g):
+        def scale_x(pair, g, tag="x_scaled"):
             key, half = x_place(pair, g)
-            scaled = tile("x_scaled", ("x_scaled",) + key, [P, 2, 1024], BF16)
+            scaled = tile(tag, ("x_scaled",) + key, [P, 2, 1024], BF16)
             nc.vector.tensor_tensor(
-                out=scaled[:, half, :].rearrange("p (m u e) -> p m u e", u=2, e=2),
-                in0=held["x_turned", pair, g][:].bitcast(BF16).rearrange("p (u m e) -> p m u e", u=2, e=2),
-                in1=gene_scale[:, g, :].rearrange("p (u e) -> p u e", e=2).unsqueeze(1).to_broadcast([P, 256, 2, 2]),
+                out=scaled[:, half, :].rearrange("p (m t) -> p m t", t=SLOTS),
+                in0=held["x_turned", pair, g][:].rearrange("p t i m -> p (i m) t"),
+                in1=gene_scale[:, g, :].unsqueeze(1).to_broadcast([P, 256, SLOTS]),
                 op=ALU.mult,
             )
 
@@ -156,14 +155,11 @@ def tile_pathway_latent_encoder_f5_kernel(
         def rows_of(k, g):
             return held["e_raw", g // 2][:, g % 2, :, :] if k == "e" else held["w_raw", g][:, :, k * DEPTH : (k + 1) * DEPTH]
 
-        def grouped(ring, key):
-            return tile("ring_" + ring, key, [P, SLOTS * DEPTH], BF16)
-
         def gpsimd_move(out, in_):
             nc.gpsimd.tensor_scalar(out=out, in0=in_, scalar1=1.0, scalar2=0.0, op0=ALU.mult, op1=ALU.add)
 
-        def interleave_w(jg, g, ring, on_gpsimd=False):
-            out, raw = grouped(ring, ("grouped", jg, g))[:], rows_of(jg, g)
+        def interleave_w(jg, g, tag, on_gpsimd=False):
+            out, raw = tile(tag, ("grouped", jg, g), [P, SLOTS * DEPTH], BF16)[:], rows_of(jg, g)
             walk = "p c t i j" if on_gpsimd else "p c t j i"
             move = gpsimd_move if on_gpsimd else nc.scalar.copy
             move(out=out.rearrange("p (t c i j) -> " + walk, t=SLOTS, i=4, j=SLOTS), in_=raw.rearrange("p j (c t i) -> " + walk, t=SLOTS, i=4))
@@ -174,34 +170,40 @@ def tile_pathway_latent_encoder_f5_kernel(
             else:
                 move(out=out.rearrange("p (c i j) -> p c j i", i=4, j=SLOTS), in_=rows.rearrange("p j (c i) -> p c j i", i=4))
 
-        def interleave_e(g, ring, move, lo=0, hi=4):
-            interleave_rows(grouped(ring, ("grouped", "e", g))[:, lo * DEPTH : hi * DEPTH], rows_of("e", g)[:, :, lo * P : hi * P], move)
+        def interleave_e(g, tag, move, lo=0, hi=WIDE):
+            out = tile(tag, ("grouped", "e", g, lo), [P, SLOTS * (hi - lo)], BF16)
+            interleave_rows(out[:], rows_of("e", g)[:, :, lo:hi], move)
 
-        def interleave_w_on_tensor(jg, g, ring):
+        def interleave_w_on_tensor(jg, g, tag, numbers):
             for t in range(SLOTS):
                 nc.tensor.matmul(
-                    bank("A", ("moved", t // 2), [P, 2, DEPTH], BF16)[:, t % 2, :].rearrange("p (c i j) -> p j c i", i=4, j=SLOTS),
+                    bank(numbers[t // 2], ("moved", jg, g, t // 2), [P, 2, DEPTH], BF16)[:, t % 2, :].rearrange("p (c i j) -> p j c i", i=4, j=SLOTS),
                     lhsT=ident_bf[:],
                     rhs=rows_of(jg, g).rearrange("p j (c t i) -> p t j c i", t=SLOTS, i=4)[:, t, :, :, :],
                     start=True,
                     stop=True,
                 )
+
+        def empty_moved(jg, g, tag):
             for half in range(2):
-                out = grouped(ring, ("grouped", jg, g))[:, half * 1024 : (half + 1) * 1024]
-                nc.scalar.copy(out=out, in_=held["moved", half][:].rearrange("p t c -> p (t c)"))
+                out = tile(tag, ("grouped", jg, g), [P, SLOTS * DEPTH], BF16)[:, half * 1024 : (half + 1) * 1024]
+                nc.scalar.copy(out=out, in_=held["moved", jg, g, half][:].rearrange("p t c -> p (t c)"))
 
-        def quantize_w(k, g):
-            quantize(("w", k, g), held["grouped", k, g][:], DEPTH)
+        def quantize_w(jg, g):
+            quantize(("w", jg, g), held["grouped", jg, g][:], DEPTH)
 
-        def u_pass(jg, g, ring, slots=range(SLOTS)):
+        def quantize_e(g, lo=0, hi=WIDE):
+            quantize(("e", g), held["grouped", "e", g, lo][:], WIDE, lo, hi)
+
+        def u_pass(jg, g, first_bank, slots=range(SLOTS)):
             for t in slots:
-                mx(bank(ring, ("u", 0, jg, t), [P, 512])[:], ("w", jg, g), block(t), *x_operand(0, g), g == 0, g == PASSES - 1)
+                mx(bank(first_bank + t, ("u", 0, jg, t), [P, 512])[:], ("w", jg, g), block(t), *x_operand(0, g), g == 0, g == PASSES - 1)
 
-        def u_bank(span, jg, b, ring):
-            out = bank(ring, ("u", span, jg, b), [P, 512])
-            for t in range(2):
-                for g in range(PASSES):
-                    mx(out[:, block(2 * t, 2)], ("w", jg, g), block(2 * b + t), *x_operand(span, g), g == 0, g == PASSES - 1)
+        def u_bank(span, jg, b, number, passes=range(PASSES)):
+            out = bank(number, ("u", span, jg, b), [P, 512])
+            for g in passes:
+                for t in range(2):
+                    mx(out[:, block(2 * t, 2)], ("w", jg, g), block(2 * b + t), *x_operand(span, g), (g, t) == (0, 0), (g, t) == (PASSES - 1, 1))
 
         def factor(span, jg, b):
             first, count = SPANS[span]
@@ -219,61 +221,64 @@ def tile_pathway_latent_encoder_f5_kernel(
             for t in slots:
                 nc.scalar.activation(out=y[:, t, :], in_=y[:, t, :], func=ACT.Silu, bias=bias_col[:, jg, t : t + 1])
 
-        def gained(span, jg, tag=None):
-            count = SPANS[span][1]
-            return tile(tag or "gained%d" % count, ("gained", span, jg), [P, SLOTS * count * P], BF16)
-
-        def gain_on_vector(span, jg):
+        def gained(span, jg, tag=None, lo=0, hi=None):
             width = SPANS[span][1] * P
+            return tile(tag or "gained2", ("gained", span, jg, 0), [P, SLOTS * width], BF16)[:, SLOTS * lo : SLOTS * (hi or width)]
+
+        def gain_on_vector(span, jg, tag=None, lo=0, hi=None):
+            hi = hi or SPANS[span][1] * P
             nc.vector.tensor_tensor(
-                out=gained(span, jg)[:].rearrange("p (c i t) -> p c t i", i=4, t=SLOTS),
-                in0=held["y", span, jg][:].rearrange("p t (c i) -> p c t i", i=4),
-                in1=gain_col[:, jg, :].unsqueeze(1).unsqueeze(3).to_broadcast([P, width // 4, SLOTS, 4]),
+                out=gained(span, jg, tag, lo, hi).rearrange("p (c i t) -> p c t i", i=4, t=SLOTS),
+                in0=held["y", span, jg][:, :, lo:hi].rearrange("p t (c i) -> p c t i", i=4),
+                in1=gain_col[:, jg, :].unsqueeze(1).unsqueeze(3).to_broadcast([P, (hi - lo) // 4, SLOTS, 4]),
                 op=ALU.mult,
             )
 
-        def gain_on_gpsimd(span, jg, tag=None, width=None):
-            width = width or SPANS[span][1] * P
+        def gain_on_gpsimd(span, jg, tag, lo=0, hi=None):
+            hi = hi or SPANS[span][1] * P
             nc.gpsimd.tensor_tensor(
-                out=gained(span, jg, tag)[:, 0 : SLOTS * width].rearrange("p (c t) -> p c t", t=SLOTS),
-                in0=held["y", span, jg][:, :, 0:width].rearrange("p t c -> p c t"),
-                in1=gain_col[:, jg, :].unsqueeze(1).to_broadcast([P, width, SLOTS]),
+                out=gained(span, jg, tag, lo, hi).rearrange("p (c t) -> p c t", t=SLOTS),
+                in0=held["y", span, jg][:, :, lo:hi].rearrange("p t c -> p c t"),
+                in1=gain_col[:, jg, :].unsqueeze(1).to_broadcast([P, hi - lo, SLOTS]),
                 op=ALU.mult,
             )
 
         def gain_on_scalar(span, jg, lo):
-            planes = tile("a_planes", "a_planes", [P, SLOTS, SPANS[span][1] * P - lo], BF16)
+            width = SPANS[span][1] * P - lo
+            planes = tile("a_planes", "a_planes", [P, SLOTS, width], BF16)
             for t in range(SLOTS):
                 nc.scalar.activation(out=planes[:, t, :], in_=held["y", span, jg][:, t, lo:], func=ACT.Copy, scale=gain_col[:, jg, t : t + 1])
+            interleave_rows(held["gained", span, jg, 0][:, SLOTS * lo :], planes[:], nc.scalar.copy)
 
-        def quantize_a(span, jg):
-            quantize(("a", span, jg), held["gained", span, jg][:], SPANS[span][1] * P)
+        def quantize_a(span, jg, lo=0, hi=None):
+            quantize(("a", span, jg), held["gained", span, jg, lo][:], SPANS[span][1] * P, lo, hi)
 
-        def v_pass(jg, g, t, ring, start, stop):
-            mx(bank(ring, ("v", jg, t), [P, WIDE])[:], ("w", jg, g), block(t), ("w", "e", g), slice(0, WIDE), start, stop)
+        def v_pass(jg, g, t, number, start, stop):
+            mx(bank(number, ("v", jg, t), [P, WIDE])[:], ("w", jg, g), block(t), ("e", g), slice(0, WIDE), start, stop)
 
-        def v_bank(jg, t, ring):
+        def v_bank(jg, t, number):
             for g in range(PASSES):
-                v_pass(jg, g, t, ring, g == 0, g == PASSES - 1)
+                v_pass(jg, g, t, number, g == 0, g == PASSES - 1)
 
         def load_gain(jg, slots=range(SLOTS)):
             planes = tile("v_planes", ("v_planes", jg), [P, SLOTS, WIDE], BF16)
             for t in slots:
                 nc.scalar.activation(out=planes[:, t, :], in_=held["v", jg, t][:], func=ACT.Copy, scale=loading_col[:, jg, t : t + 1])
 
-        def interleave_v(jg, ring):
-            interleave_rows(grouped(ring, ("grouped", "v", jg))[:], held["v_planes", jg][:], nc.scalar.copy)
+        def interleave_v(jg, tag, lo=0, hi=WIDE):
+            out = tile(tag, ("grouped", "v", jg), [P, SLOTS * WIDE], BF16)[:, SLOTS * lo : SLOTS * hi]
+            interleave_rows(out, held["v_planes", jg][:, :, lo:hi], nc.scalar.copy)
 
-        def quantize_v(jg):
-            quantize(("v", jg), held["grouped", "v", jg][:], WIDE)
+        def quantize_v(jg, lo=0, hi=WIDE):
+            quantize(("v", jg), held["grouped", "v", jg][:, SLOTS * lo : SLOTS * hi], WIDE, lo, hi)
 
         def a_operand(i, jg, count):
             span = max(n for n in range(len(SPANS)) if SPANS[n][0] <= i)
             return ("a", span, jg), block(i - SPANS[span][0], count)
 
-        def q_mean(piece):
+        def q_mean(piece, number):
             first, count = PIECES[piece]
-            out = bank("B", ("q_mean", piece), [P, count, LATENT])
+            out = bank(number, ("q_mean", piece), [P, count, LATENT])
             for i in range(count):
                 for jg in range(GROUPS):
                     mx(out[:, i, :], *a_operand(first + i, jg, 1), ("v", jg), slice(0, LATENT), jg == 0, jg == GROUPS - 1)
@@ -282,9 +287,9 @@ def tile_pathway_latent_encoder_f5_kernel(
             bias = mean_bias[:].unsqueeze(1).to_broadcast([P, PIECES[piece][1], LATENT])
             nc.vector.tensor_tensor(out=result("mu", piece), in0=held["q_mean", piece][:], in1=bias, op=ALU.add)
 
-        def q_logvar(piece, ring):
+        def q_logvar(piece, number):
             first, count = PIECES[piece]
-            out = bank(ring, ("q_logvar", piece), [P, 2, count * P])
+            out = bank(number, ("q_logvar", piece), [P, 2, count * P])
             for h in range(2):
                 for jg in range(GROUPS):
                     mx(out[:, h, :], ("v", jg), block(2 + h), *a_operand(first, jg, count), jg == 0, jg == GROUPS - 1)
@@ -292,12 +297,12 @@ def tile_pathway_latent_encoder_f5_kernel(
         def tanh(piece):
             out = tile("tanh", ("tanh", piece), [P, 2, PIECES[piece][1] * P], F32)
             for h in range(2):
-                bias = vector_cols[:, BIAS_ROW + h : BIAS_ROW + h + 1]
+                bias = vector_cols[:, 6 + h, SLOTS : SLOTS + 1]
                 nc.scalar.activation(out=out[:, h, :], in_=held["q_logvar", piece][:, h, :], func=ACT.Tanh, bias=bias)
 
-        def turn_back(piece, ring):
+        def turn_back(piece, number):
             count = PIECES[piece][1]
-            out = bank(ring, ("turned_back", piece), [P, count, LATENT])
+            out = bank(number, ("turned_back", piece), [P, count, LATENT])
             for i in range(count):
                 for h in range(2):
                     nc.tensor.transpose(out[:, i, block(h)], held["tanh", piece][:, h, block(i)], ident[:])
@@ -319,22 +324,26 @@ def tile_pathway_latent_encoder_f5_kernel(
         nc.scalar.activation(out=warm[:, 1:2], in_=warm[:, 0:1], func=ACT.Silu)
 
         nc.sync.dma_start(out=factor_col[:], in_=cell_factor.rearrange("(p i) -> p i", i=TILES))
-        load_x(0, 0, 1)
-        load_x(0, 1, 2)
+        load_x(0, 2, 0, 1)
+        load_x(0, 2, 1, 2)
+        load_x(0, 2, 2, 4)
         nc.sync.dma_start(out=gene_scale[:], in_=x_scale.rearrange("o (g p t) -> p (o g) t", p=P, t=SLOTS))
-        load_x(0, 2, 4)
-        load_x(1)
+        load_x(2, 1)
+        load_x(3, 1)
+        load_vectors()
         for g in range(PASSES):
             load_w(g)
-        load_x(2)
-        for g in range(PASSES):
+        load_x(4, 2)
+        for g in low:
             load_e(g)
-        load_x(3)
-        load_vectors()
+        load_x(6, 2)
+        for g in high:
+            load_e(g)
+        nc.sync.dma_start(out=mean_bias[:], in_=latent_bias[0:LATENT].partition_broadcast(P))
 
         widen(0, on_scalar, 0, 1)
         widen(1, on_vector, 0, 1)
-        spread_factor = bank("B", "factor", [P, CELLS], BF16)
+        spread_factor = bank(4, "factor", [P, CELLS], BF16)
         for i in range(TILES):
             nc.tensor.matmul(spread_factor[:, block(i)], lhsT=factor_col[:, i : i + 1].to_broadcast([P, P]), rhs=ident_bf[:], start=True, stop=True)
         on_vector(out=factor_row[:], in_=spread_factor[:])
@@ -344,158 +353,177 @@ def tile_pathway_latent_encoder_f5_kernel(
             widen(i, on_scalar, 2, 4)
         for i in (2, 3):
             widen(i, on_scalar)
-        for pair, ring in enumerate("AB"):
+        gpsimd_move(out=slot_rows[:].rearrange("p t (c i) -> p t c i", i=4), in_=vector_rows[:].rearrange("p (c t i) -> p t c i", t=SLOTS, i=4))
+        for pair in range(2):
             for g in range(PASSES):
-                turn_x(pair, g, ring)
+                turn_x(pair, g, 4 * pair + g)
                 scale_x(pair, g)
-        for g, ring in enumerate("gh"):
-            interleave_w(0, g, ring, on_gpsimd=True)
-            interleave_w(1, g, "s")
+        vectors = bank(0, "vectors", [P, SLOTS + 1, VECTOR_ROWS])
+        for t in range(SLOTS + 1):
+            rows = slot_rows[:, t, :] if t < SLOTS else vector_rows[:, 0:P]
+            nc.tensor.matmul(vectors[:, t, :], lhsT=rows, rhs=ident_bf[:, 0:VECTOR_ROWS], start=True, stop=True)
+        interleave_w(0, 0, "j", on_gpsimd=True)
+        interleave_w(1, 0, "ring")
+        interleave_w(0, 1, "k", on_gpsimd=True)
+        interleave_w(1, 1, "ring")
+        on_scalar(out=vector_cols[:, :, 0 : SLOTS + 1], in_=vectors[:].rearrange("p t r -> p r t"))
         for g in (2, 3):
-            interleave_w(0, g, "s")
-        interleave_w_on_tensor(1, 2, "i")
+            interleave_w(0, g, "ring")
+        interleave_w_on_tensor(1, 2, "i", (1, 2))
+        empty_moved(1, 2, "i")
 
         for g in range(PASSES):
             quantize_x(0, g)
             quantize_w(0, g)
-            u_pass(0, g, "B")
-        interleave_w(1, 3, "h")
-        for i in (4, 5):
-            widen(i, on_scalar)
+            u_pass(0, g, 4)
+        interleave_w(1, 3, "k")
+        for lo in (0, 2):
+            for i in (4, 5):
+                widen(i, on_scalar, lo, lo + 2)
         for g in range(PASSES):
             quantize_w(1, g)
-
-        for g, ring in enumerate("hg"):
-            interleave_e(g, ring, gpsimd_move)
-        interleave_e(3, "s", on_scalar)
-        u_pass(1, 0, "A")
-        u_pass(1, 1, "A", low)
-        for t in range(SLOTS):
-            factor(0, 0, t)
-        for g in low:
-            turn_x(2, g, "B")
-        u_pass(1, 1, "A", high)
-        u_pass(1, 2, "A", low)
-        for g in high:
-            turn_x(2, g, "B")
-        vectors = bank("B", "vectors", [P, P], BF16)
-        nc.tensor.transpose(vectors[:], vector_rows[:], ident_bf[:])
-        u_pass(1, 2, "A", high)
-        u_pass(1, 3, "A", low)
-        for g in range(PASSES):
-            scale_x(2, g)
         for i in (6, 7):
             widen(i, on_scalar)
-        on_scalar(out=vector_cols[:], in_=vectors[:, 0:VECTOR_ROWS])
-        interleave_e(2, "i", on_scalar, hi=E2_ON_SCALAR)
+
+        interleave_e(0, "k", gpsimd_move)
+        interleave_e(1, "j", gpsimd_move, hi=E_SPLIT)
         for g in low:
-            turn_x(3, g, "B")
-        u_pass(1, 3, "A", high)
-
-        order = (3, 1, 2, 0)
-        for g in order:
-            quantize_w("e", g)
-            for t in low:
-                v_pass(0, g, t, "B", g == order[0], g == order[-1])
-            if g == order[0]:
-                interleave_e(2, "i", on_vector, lo=E2_ON_SCALAR)
-
+            u_pass(1, g, 0)
         for t in range(SLOTS):
-            factor(0, 1, t)
-        for t in high:
-            v_bank(0, t, "A")
-        for g in high:
-            turn_x(3, g, "A")
-        nc.sync.dma_start(out=tile("big", "noise", [P, TILES, LATENT], BF16)[:], in_=by_tile(noise))
+            factor(0, 0, t)
         silu(0, 0)
-        gain_on_gpsimd(0, 0, "ring_h")
-        load_gain(0, low)
-        silu(0, 1)
-        gain_on_gpsimd(0, 1, width=CELLS_ON_GPSIMD)
-        load_gain(0, high)
-        for g in range(PASSES):
-            scale_x(3, g)
-        for t in range(SLOTS):
-            v_bank(1, t, "B")
-        interleave_v(0, "g")
+        for g in low:
+            turn_x(2, g, 4 + g)
+        u_pass(1, 2, 0)
+        for g in high:
+            turn_x(2, g, 4 + g)
+        u_pass(1, 3, 0)
+        for g in range(3):
+            scale_x(2, g, "ih"[g // 2])
+        quantize_x(2, 0)
+        interleave_e(1, "i", gpsimd_move, lo=E_SPLIT)
+        scale_x(2, 3)
+        for g in high:
+            interleave_e(g, "ring", on_scalar)
+        for b in range(2):
+            u_bank(1, 0, b, 4 + b, low)
+        factor(0, 1, 0)
+        quantize_x(2, 1)
+        for g in low:
+            turn_x(3, g, 6 + g)
+        for b in range(2):
+            u_bank(1, 0, b, 4 + b, high)
 
-        for half in range(2):
-            quantize_x(2, half)
-        quantize_a(0, 0)
-        for half in range(2):
-            quantize_x(3, half)
-        quantize_v(0)
-        gain_on_scalar(0, 1, CELLS_ON_GPSIMD)
-        load_gain(1)
-        for span, ring in ((1, "A"), (2, "B")):
-            for jg in range(GROUPS):
-                for b in range(2):
-                    u_bank(span, jg, b, ring)
-        interleave_rows(gained(0, 1)[:, SLOTS * CELLS_ON_GPSIMD :], held["a_planes"][:], on_vector)
+        gain_on_gpsimd(0, 0, "h", hi=CELLS_ON_GPSIMD)
+        for t in range(1, SLOTS):
+            factor(0, 1, t)
+        silu(0, 1)
+        for b in range(2):
+            u_bank(1, 1, b, b)
+        for g in high:
+            turn_x(3, g, g)
         for b in range(2):
             factor(1, 0, b)
         silu(1, 0)
-        interleave_v(1, "i")
-        quantize_a(0, 1)
-        for b in range(2):
-            factor(1, 1, b)
+        factor(1, 1, 0)
+        nc.sync.dma_start(out=tile("big", "noise", [P, TILES, LATENT], BF16)[:], in_=by_tile(noise))
+        order = (2, 1, 3, 0)
+        for g in order:
+            if g == 1:
+                quantize_e(1, hi=E_SPLIT)
+                quantize_e(1, lo=E_SPLIT)
+            else:
+                quantize_e(g)
+            for t in low:
+                v_pass(0, g, t, 4 + t, g == order[0], g == order[-1])
+
+        gain_on_gpsimd(0, 1, "k")
+        gain_on_scalar(0, 0, CELLS_ON_GPSIMD)
+        factor(1, 1, 1)
         silu(1, 1)
+        for t in high:
+            v_bank(0, t, t - 2)
+        for g in range(PASSES):
+            scale_x(3, g)
+        load_gain(0)
+        for t, number in enumerate((6, 7, 4, 5)):
+            v_bank(1, t, number)
+        interleave_v(0, "ring")
+        for half in range(2):
+            quantize_x(3, half)
+        for b in range(2):
+            u_bank(2, 0, b, 2 + b)
+        load_gain(1)
+        interleave_v(1, "j", lo=LATENT)
+        interleave_v(1, "j", hi=LATENT)
         gain_on_vector(1, 0)
+        quantize_a(0, 0)
+        gain_on_vector(1, 1)
+        quantize_a(0, 1)
+        quantize_v(0)
         quantize_a(1, 0)
-        quantize_v(1)
-
-        gain_on_gpsimd(1, 1, "ring_i")
-        for jg in range(GROUPS):
-            for b in range(2):
-                factor(2, jg, b)
-            silu(2, jg)
-        q_mean(0)
-        for piece in range(2):
-            q_logvar(piece, "A")
-            tanh(piece)
-        q_mean(1)
-        for piece in range(2):
-            turn_back(piece, "A")
-        add_mean_bias(0)
         quantize_a(1, 1)
-        for jg in range(GROUPS):
-            gain_on_vector(2, jg)
-        quantize_a(2, 0)
-        add_mean_bias(1)
-        quantize_a(2, 1)
-        for piece in range(2):
-            store("mu", piece)
+        quantize_v(1, lo=LATENT)
+        u_bank(2, 1, 0, 0)
+        q_logvar(0, 6)
+        u_bank(2, 1, 1, 1)
+        for b in range(2):
+            factor(2, 0, b)
+        silu(2, 0)
+        tanh(0)
+        quantize_v(1, hi=LATENT)
 
-        q_logvar(2, "A")
-        q_mean(2)
-        q_logvar(3, "A")
-        q_logvar(4, "B")
-        for piece in (3, 4):
-            q_mean(piece)
+        gain_on_gpsimd(2, 0, "j")
+        for b in range(2):
+            factor(2, 1, b)
+        silu(2, 1)
         for piece in range(2):
-            exp(piece)
-        for piece in (2, 3, 4):
-            tanh(piece)
-        for piece, ring in ((2, "A"), (3, "A"), (4, "B")):
-            turn_back(piece, ring)
-            exp(piece)
-        store("sd", 0)
-        add_mean_bias(2)
-        store("sd", 1)
-        store("mu", 2)
-        for step in (spread, shift):
-            for piece in range(2):
-                step(piece)
-        for piece in (3, 4):
+            q_mean(piece, 4 + piece)
             add_mean_bias(piece)
+            store("mu", piece)
+        turn_back(0, 2)
+        exp(0)
+        q_mean(2, 3)
+        add_mean_bias(2)
+        store("mu", 2)
+        q_logvar(1, 7)
+        q_logvar(2, 0)
+        gain_on_vector(2, 1)
+        quantize_a(2, 0)
+        spread(0)
+        quantize_a(2, 1)
+        shift(0)
+        store("sd", 0)
         store("z", 0)
-        store("sd", 2)
+        tanh(1)
+        turn_back(1, 1)
+        tanh(2)
+        exp(1)
+        for piece in (3, 4):
+            q_logvar(piece, 1 + piece)
+        turn_back(2, 6)
+        for piece, number in ((3, 2), (4, 3)):
+            q_mean(piece, number)
+        tanh(3)
+        exp(2)
+        tanh(4)
+        for piece, number in ((3, 7), (4, 0)):
+            turn_back(piece, number)
+            exp(piece)
+        spread(1)
+        add_mean_bias(3)
+        shift(1)
+        add_mean_bias(4)
+        store("sd", 1)
         store("z", 1)
-        for name in ("sd", "mu"):
-            store(name, 3, 4)
-        spread(2)
-        for piece in (2, 3, 4):
-            if piece + 1 < len(PIECES):
-                spread(piece + 1)
-            shift(piece)
-            store("z", piece)
+        store("sd", 2)
+        store("mu", 3, 4)
+        for piece in range(2, len(PIECES)):
+            spread(piece)
+            if piece > 2:
+                shift(piece - 1)
+                store("z", piece - 1)
+            if piece == 3:
+                store("sd", 3, 4)
+        shift(4)
+        store("z", 4)

@@ -27,6 +27,8 @@ PIECES = [(0, 2), (2, 2), (4, 2), (6, 1), (7, 1)]
 VECTOR_ROWS = 8
 E_SPLIT = 384
 CELLS_ON_GPSIMD = 384
+V_SPLIT = 384
+PAIR_CELLS_ON_GPSIMD = 160
 BUFFERS = {"x_raw": 2, "big": 4, "x_wide": 4, "x_scaled": 4, "ring": 4, "y4": 2, "y2": 4, "tanh": 4, "gained2": 2, "v_planes": 2}
 
 
@@ -125,11 +127,20 @@ def tile_pathway_latent_encoder_f5_kernel(
             copy(out=wide[:, lo * DEPTH : hi * DEPTH], in_=raw[:, row, start * DEPTH : (start + hi - lo) * DEPTH].bitcast(F8))
 
         def turn_x(pair, g, number):
+            out = bank(number, ("x_turned", pair, g), [P, 512])
+            for i in range(2):
+                words = held["x_wide", 2 * pair + i][:].bitcast(F32)
+                for u in range(2):
+                    nc.tensor.transpose(out[:, block(2 * u + i)], words[:, 256 * g + u : 256 * (g + 1) : 2], ident[:])
+            held["x_view", pair, g] = out[:].bitcast(BF16).rearrange("p (u m e) -> p m u e", u=2, e=2)
+
+        def turn_x_plain(pair, g, number):
             out = bank(number, ("x_turned", pair, g), [P, SLOTS, 2, P], BF16)
             for i in range(2):
                 genes = held["x_wide", 2 * pair + i][:, g * DEPTH : (g + 1) * DEPTH].rearrange("p (m t) -> p t m", t=SLOTS)
                 for t in range(SLOTS):
                     nc.tensor.matmul(out[:, t, i, :], lhsT=genes[:, t, :], rhs=ident_bf[:], start=True, stop=True)
+            held["x_view", pair, g] = out[:].rearrange("p (u e) i m -> p (i m) u e", e=2)
 
         def x_place(pair, g):
             return ((0, g), pair) if pair < 2 else ((pair, g // 2), g % 2)
@@ -138,9 +149,9 @@ def tile_pathway_latent_encoder_f5_kernel(
             key, half = x_place(pair, g)
             scaled = tile(tag, ("x_scaled",) + key, [P, 2, 1024], BF16)
             nc.vector.tensor_tensor(
-                out=scaled[:, half, :].rearrange("p (m t) -> p m t", t=SLOTS),
-                in0=held["x_turned", pair, g][:].rearrange("p t i m -> p (i m) t"),
-                in1=gene_scale[:, g, :].unsqueeze(1).to_broadcast([P, 256, SLOTS]),
+                out=scaled[:, half, :].rearrange("p (m u e) -> p m u e", u=2, e=2),
+                in0=held["x_view", pair, g],
+                in1=gene_scale[:, g, :].rearrange("p (u e) -> p u e", e=2).unsqueeze(1).to_broadcast([P, 256, 2, 2]),
                 op=ALU.mult,
             )
 
@@ -205,6 +216,15 @@ def tile_pathway_latent_encoder_f5_kernel(
                 for t in range(2):
                     mx(out[:, block(2 * t, 2)], ("w", jg, g), block(2 * b + t), *x_operand(span, g), (g, t) == (0, 0), (g, t) == (PASSES - 1, 1))
 
+        def u_slot(span, jg, t, number):
+            out = bank(number, ("u_slot", t), [P, 2 * P])
+            for g in range(PASSES):
+                mx(out[:], ("w", jg, g), block(t), *x_operand(span, g), g == 0, g == PASSES - 1)
+
+        def factor_slot(span, jg, t):
+            first, count = SPANS[span]
+            nc.vector.tensor_tensor(out=held["y", span, jg][:, t, :], in0=held["u_slot", t][:], in1=factor_row[:, block(first, count)], op=ALU.mult)
+
         def factor(span, jg, b):
             first, count = SPANS[span]
             per = SLOTS // count
@@ -225,12 +245,17 @@ def tile_pathway_latent_encoder_f5_kernel(
             width = SPANS[span][1] * P
             return tile(tag or "gained2", ("gained", span, jg, 0), [P, SLOTS * width], BF16)[:, SLOTS * lo : SLOTS * (hi or width)]
 
+        def gains_to_psum(number):
+            out = bank(number, "gains", [P, GROUPS, SLOTS])
+            for t in range(SLOTS):
+                nc.tensor.matmul(out[:, :, t], lhsT=slot_rows[:, t, :], rhs=ident_bf[:, 4:6], start=True, stop=True)
+
         def gain_on_vector(span, jg, tag=None, lo=0, hi=None):
             hi = hi or SPANS[span][1] * P
             nc.vector.tensor_tensor(
                 out=gained(span, jg, tag, lo, hi).rearrange("p (c i t) -> p c t i", i=4, t=SLOTS),
                 in0=held["y", span, jg][:, :, lo:hi].rearrange("p t (c i) -> p c t i", i=4),
-                in1=gain_col[:, jg, :].unsqueeze(1).unsqueeze(3).to_broadcast([P, (hi - lo) // 4, SLOTS, 4]),
+                in1=held["gains"][:, jg, :].unsqueeze(1).unsqueeze(3).to_broadcast([P, (hi - lo) // 4, SLOTS, 4]),
                 op=ALU.mult,
             )
 
@@ -265,12 +290,12 @@ def tile_pathway_latent_encoder_f5_kernel(
             for t in slots:
                 nc.scalar.activation(out=planes[:, t, :], in_=held["v", jg, t][:], func=ACT.Copy, scale=loading_col[:, jg, t : t + 1])
 
-        def interleave_v(jg, tag, lo=0, hi=WIDE):
-            out = tile(tag, ("grouped", "v", jg), [P, SLOTS * WIDE], BF16)[:, SLOTS * lo : SLOTS * hi]
-            interleave_rows(out, held["v_planes", jg][:, :, lo:hi], nc.scalar.copy)
+        def interleave_v(jg, tag, move, lo=0, hi=WIDE):
+            out = tile(tag, ("grouped", "v", jg, lo), [P, SLOTS * (hi - lo)], BF16)
+            interleave_rows(out[:], held["v_planes", jg][:, :, lo:hi], move)
 
         def quantize_v(jg, lo=0, hi=WIDE):
-            quantize(("v", jg), held["grouped", "v", jg][:, SLOTS * lo : SLOTS * hi], WIDE, lo, hi)
+            quantize(("v", jg), held["grouped", "v", jg, lo][:], WIDE, lo, hi)
 
         def a_operand(i, jg, count):
             span = max(n for n in range(len(SPANS)) if SPANS[n][0] <= i)
@@ -313,8 +338,13 @@ def tile_pathway_latent_encoder_f5_kernel(
         def spread(piece):
             nc.vector.tensor_tensor(out=result("z", piece), in0=result("sd", piece), in1=held["noise"][:, tiles_of(piece), :], op=ALU.mult)
 
-        def shift(piece):
-            nc.vector.tensor_tensor(out=result("z", piece), in0=result("z", piece), in1=result("mu", piece), op=ALU.add)
+        def shift(piece, engine=nc.vector):
+            engine.tensor_tensor(out=result("z", piece), in0=result("z", piece), in1=result("mu", piece), op=ALU.add)
+
+        def warm_tensor(key, number, count):
+            out = bank(number, ("warm", key), [P, SLOTS, P])
+            for n in range(count):
+                nc.tensor.matmul(out[:], lhsT=ident_bf[:], rhs=ident_bf[:].unsqueeze(1).to_broadcast([P, SLOTS, P]), start=True, stop=True)
 
         on_scalar, on_vector = nc.scalar.copy, nc.vector.tensor_copy
         low, high = range(0, 2), range(2, 4)
@@ -367,9 +397,9 @@ def tile_pathway_latent_encoder_f5_kernel(
         interleave_w(0, 1, "k", on_gpsimd=True)
         interleave_w(1, 1, "ring")
         on_scalar(out=vector_cols[:, :, 0 : SLOTS + 1], in_=vectors[:].rearrange("p t r -> p r t"))
+        interleave_w_on_tensor(1, 2, "i", (1, 2))
         for g in (2, 3):
             interleave_w(0, g, "ring")
-        interleave_w_on_tensor(1, 2, "i", (1, 2))
         empty_moved(1, 2, "i")
 
         for g in range(PASSES):
@@ -387,16 +417,18 @@ def tile_pathway_latent_encoder_f5_kernel(
 
         interleave_e(0, "k", gpsimd_move)
         interleave_e(1, "j", gpsimd_move, hi=E_SPLIT)
-        for g in low:
-            u_pass(1, g, 0)
+        u_pass(1, 0, 0)
+        u_pass(1, 1, 0, low)
         for t in range(SLOTS):
             factor(0, 0, t)
         silu(0, 0)
         for g in low:
             turn_x(2, g, 4 + g)
-        u_pass(1, 2, 0)
+        u_pass(1, 1, 0, high)
+        u_pass(1, 2, 0, low)
         for g in high:
             turn_x(2, g, 4 + g)
+        u_pass(1, 2, 0, high)
         u_pass(1, 3, 0)
         for g in range(3):
             scale_x(2, g, "ih"[g // 2])
@@ -407,7 +439,6 @@ def tile_pathway_latent_encoder_f5_kernel(
             interleave_e(g, "ring", on_scalar)
         for b in range(2):
             u_bank(1, 0, b, 4 + b, low)
-        factor(0, 1, 0)
         quantize_x(2, 1)
         for g in low:
             turn_x(3, g, 6 + g)
@@ -415,7 +446,7 @@ def tile_pathway_latent_encoder_f5_kernel(
             u_bank(1, 0, b, 4 + b, high)
 
         gain_on_gpsimd(0, 0, "h", hi=CELLS_ON_GPSIMD)
-        for t in range(1, SLOTS):
+        for t in range(SLOTS):
             factor(0, 1, t)
         silu(0, 1)
         for b in range(2):
@@ -444,86 +475,95 @@ def tile_pathway_latent_encoder_f5_kernel(
         for t in high:
             v_bank(0, t, t - 2)
         for g in range(PASSES):
-            scale_x(3, g)
+            scale_x(3, g, "x_scaled" if g < 2 else "i")
         load_gain(0)
-        for t, number in enumerate((6, 7, 4, 5)):
-            v_bank(1, t, number)
-        interleave_v(0, "ring")
+        for t in low:
+            v_bank(1, t, 6 + t)
+        gains_to_psum(1)
+        for t in high:
+            v_bank(1, t, 2 + t)
         for half in range(2):
             quantize_x(3, half)
+        gain_on_gpsimd(1, 0, "i", hi=PAIR_CELLS_ON_GPSIMD)
+        interleave_v(0, "ring", on_scalar)
         for b in range(2):
             u_bank(2, 0, b, 2 + b)
         load_gain(1)
-        interleave_v(1, "j", lo=LATENT)
-        interleave_v(1, "j", hi=LATENT)
-        gain_on_vector(1, 0)
-        quantize_a(0, 0)
+        interleave_v(1, "j", on_scalar, lo=LATENT)
+        interleave_v(1, "ring", on_scalar, P, LATENT)
         gain_on_vector(1, 1)
-        quantize_a(0, 1)
+        gain_on_vector(1, 0, lo=PAIR_CELLS_ON_GPSIMD)
+        for jg in range(GROUPS):
+            quantize_a(0, jg)
         quantize_v(0)
-        quantize_a(1, 0)
-        quantize_a(1, 1)
+        for jg in (1, 0):
+            quantize_a(1, jg)
+        factor(2, 0, 0)
         quantize_v(1, lo=LATENT)
+        interleave_v(1, "j", gpsimd_move, hi=P)
         u_bank(2, 1, 0, 0)
         q_logvar(0, 6)
-        u_bank(2, 1, 1, 1)
-        for b in range(2):
-            factor(2, 0, b)
+        for t, number in ((2, 7), (3, 4)):
+            u_slot(2, 1, t, number)
+        factor(2, 0, 1)
         silu(2, 0)
         tanh(0)
-        quantize_v(1, hi=LATENT)
+        factor(2, 1, 0)
+        quantize_v(1, P, LATENT)
+        quantize_v(1, hi=P)
 
         gain_on_gpsimd(2, 0, "j")
-        for b in range(2):
-            factor(2, 1, b)
+        for t in high:
+            factor_slot(2, 1, t)
         silu(2, 1)
-        for piece in range(2):
-            q_mean(piece, 4 + piece)
-            add_mean_bias(piece)
-            store("mu", piece)
+        q_mean(0, 5)
+        add_mean_bias(0)
+        store("mu", 0)
         turn_back(0, 2)
         exp(0)
-        q_mean(2, 3)
-        add_mean_bias(2)
-        store("mu", 2)
-        q_logvar(1, 7)
-        q_logvar(2, 0)
+        q_mean(1, 3)
+        q_logvar(1, 0)
+        q_mean(2, 7)
+        q_logvar(2, 6)
         gain_on_vector(2, 1)
-        quantize_a(2, 0)
-        spread(0)
-        quantize_a(2, 1)
-        shift(0)
-        store("sd", 0)
-        store("z", 0)
+        for jg in range(GROUPS):
+            quantize_a(2, jg)
+        for piece in (1, 2):
+            add_mean_bias(piece)
+            store("mu", piece)
+        for piece, number in ((3, 1), (4, 4)):
+            q_logvar(piece, number)
         tanh(1)
-        turn_back(1, 1)
+        turn_back(1, 3)
+        for piece, number in ((3, 5), (4, 2)):
+            q_mean(piece, number)
         tanh(2)
         exp(1)
-        for piece in (3, 4):
-            q_logvar(piece, 1 + piece)
-        turn_back(2, 6)
-        for piece, number in ((3, 2), (4, 3)):
-            q_mean(piece, number)
+        turn_back(2, 0)
         tanh(3)
-        exp(2)
         tanh(4)
-        for piece, number in ((3, 7), (4, 0)):
+        exp(2)
+        for piece, number in ((3, 6), (4, 7)):
             turn_back(piece, number)
             exp(piece)
-        spread(1)
+        spread(0)
+        store("sd", 0)
+        shift(0)
+        store("z", 0)
         add_mean_bias(3)
-        shift(1)
+        spread(1)
         add_mean_bias(4)
+        shift(1)
         store("sd", 1)
+        store("mu", 3, 4)
         store("z", 1)
         store("sd", 2)
-        store("mu", 3, 4)
         for piece in range(2, len(PIECES)):
             spread(piece)
             if piece > 2:
                 shift(piece - 1)
                 store("z", piece - 1)
-            if piece == 3:
+            if piece == 2:
                 store("sd", 3, 4)
         shift(4)
         store("z", 4)

@@ -25,11 +25,10 @@ FLOPS = 2 * CELLS * GENES * PATHWAYS + 2 * GENES * PATHWAYS * WIDE + 2 * CELLS *
 SPANS = [(0, 4), (4, 2), (6, 2)]
 PIECES = [(0, 2), (2, 2), (4, 2), (6, 1), (7, 1)]
 VECTOR_ROWS = 8
-E_SPLIT = 384
-CELLS_ON_GPSIMD = 384
-V_SPLIT = 384
-PAIR_CELLS_ON_GPSIMD = 160
-BUFFERS = {"x_raw": 2, "big": 4, "x_wide": 4, "x_scaled": 4, "ring": 4, "y4": 2, "y2": 4, "tanh": 4, "gained2": 2, "v_planes": 2}
+W_SPLIT = 20
+CELLS_ON_GPSIMD = 320
+PAIR_CELLS_ON_GPSIMD = 128
+BUFFERS = {"x_raw": 2, "big": 4, "x_wide": 4, "x_scaled": 4, "ring": 4, "y4": 2, "y2": 2, "tanh": 4, "gained2": 2, "v_planes": 2}
 
 
 def tile_pathway_latent_encoder_f5_kernel(
@@ -169,11 +168,13 @@ def tile_pathway_latent_encoder_f5_kernel(
         def gpsimd_move(out, in_):
             nc.gpsimd.tensor_scalar(out=out, in0=in_, scalar1=1.0, scalar2=0.0, op0=ALU.mult, op1=ALU.add)
 
-        def interleave_w(jg, g, tag, on_gpsimd=False):
+        def interleave_w(jg, g, tag, move, lo=0, hi=32):
             out, raw = tile(tag, ("grouped", jg, g), [P, SLOTS * DEPTH], BF16)[:], rows_of(jg, g)
-            walk = "p c t i j" if on_gpsimd else "p c t j i"
-            move = gpsimd_move if on_gpsimd else nc.scalar.copy
-            move(out=out.rearrange("p (t c i j) -> " + walk, t=SLOTS, i=4, j=SLOTS), in_=raw.rearrange("p j (c t i) -> " + walk, t=SLOTS, i=4))
+            walk = "p c t i j" if move is gpsimd_move else "p c t j i"
+            move(
+                out=out.rearrange("p (t c i j) -> " + walk, t=SLOTS, i=4, j=SLOTS)[:, lo:hi],
+                in_=raw.rearrange("p j (c t i) -> " + walk, t=SLOTS, i=4)[:, lo:hi],
+            )
 
         def interleave_rows(out, rows, move):
             if move is gpsimd_move:
@@ -184,6 +185,12 @@ def tile_pathway_latent_encoder_f5_kernel(
         def interleave_e(g, tag, move, lo=0, hi=WIDE):
             out = tile(tag, ("grouped", "e", g, lo), [P, SLOTS * (hi - lo)], BF16)
             interleave_rows(out[:], rows_of("e", g)[:, :, lo:hi], move)
+
+        def interleave_e_pair(tag):
+            out = tile(tag, ("grouped", "e pair"), [P, 2, SLOTS * WIDE], BF16)
+            gpsimd_move(out=out[:].rearrange("p g (c j) -> p g c j", j=SLOTS), in_=held["e_raw", 0][:].rearrange("p g j c -> p g c j"))
+            for g in range(2):
+                held["grouped", "e", g, 0] = out[:, g, :]
 
         def interleave_w_on_tensor(jg, g, tag, numbers):
             for t in range(SLOTS):
@@ -273,7 +280,9 @@ def tile_pathway_latent_encoder_f5_kernel(
             planes = tile("a_planes", "a_planes", [P, SLOTS, width], BF16)
             for t in range(SLOTS):
                 nc.scalar.activation(out=planes[:, t, :], in_=held["y", span, jg][:, t, lo:], func=ACT.Copy, scale=gain_col[:, jg, t : t + 1])
-            interleave_rows(held["gained", span, jg, 0][:, SLOTS * lo :], planes[:], nc.scalar.copy)
+
+        def interleave_a(span, jg, lo):
+            interleave_rows(held["gained", span, jg, 0][:, SLOTS * lo :], held["a_planes"][:], nc.scalar.copy)
 
         def quantize_a(span, jg, lo=0, hi=None):
             quantize(("a", span, jg), held["gained", span, jg, lo][:], SPANS[span][1] * P, lo, hi)
@@ -392,21 +401,23 @@ def tile_pathway_latent_encoder_f5_kernel(
         for t in range(SLOTS + 1):
             rows = slot_rows[:, t, :] if t < SLOTS else vector_rows[:, 0:P]
             nc.tensor.matmul(vectors[:, t, :], lhsT=rows, rhs=ident_bf[:, 0:VECTOR_ROWS], start=True, stop=True)
-        interleave_w(0, 0, "j", on_gpsimd=True)
-        interleave_w(1, 0, "ring")
-        interleave_w(0, 1, "k", on_gpsimd=True)
-        interleave_w(1, 1, "ring")
+        interleave_w(0, 0, "j", gpsimd_move)
+        interleave_w(1, 0, "ring", on_scalar)
+        interleave_w(0, 1, "h", gpsimd_move, hi=W_SPLIT)
+        interleave_w(1, 1, "ring", on_scalar)
         on_scalar(out=vector_cols[:, :, 0 : SLOTS + 1], in_=vectors[:].rearrange("p t r -> p r t"))
         interleave_w_on_tensor(1, 2, "i", (1, 2))
         for g in (2, 3):
-            interleave_w(0, g, "ring")
+            interleave_w(0, g, "ring", on_scalar)
         empty_moved(1, 2, "i")
 
         for g in range(PASSES):
+            if g == 1:
+                interleave_w(0, 1, "h", on_vector, lo=W_SPLIT)
             quantize_x(0, g)
             quantize_w(0, g)
             u_pass(0, g, 4)
-        interleave_w(1, 3, "k")
+        interleave_w(1, 3, "k", on_scalar)
         for lo in (0, 2):
             for i in (4, 5):
                 widen(i, on_scalar, lo, lo + 2)
@@ -415,8 +426,7 @@ def tile_pathway_latent_encoder_f5_kernel(
         for i in (6, 7):
             widen(i, on_scalar)
 
-        interleave_e(0, "k", gpsimd_move)
-        interleave_e(1, "j", gpsimd_move, hi=E_SPLIT)
+        interleave_e_pair("k")
         u_pass(1, 0, 0)
         u_pass(1, 1, 0, low)
         for t in range(SLOTS):
@@ -430,20 +440,16 @@ def tile_pathway_latent_encoder_f5_kernel(
             turn_x(2, g, 4 + g)
         u_pass(1, 2, 0, high)
         u_pass(1, 3, 0)
-        for g in range(3):
+        for g in range(PASSES):
             scale_x(2, g, "ih"[g // 2])
-        quantize_x(2, 0)
-        interleave_e(1, "i", gpsimd_move, lo=E_SPLIT)
-        scale_x(2, 3)
-        for g in high:
-            interleave_e(g, "ring", on_scalar)
-        for b in range(2):
-            u_bank(1, 0, b, 4 + b, low)
-        quantize_x(2, 1)
+        for half in range(2):
+            quantize_x(2, half)
+        interleave_e(2, "ring", on_scalar)
+        interleave_e(3, "j", on_scalar)
         for g in low:
-            turn_x(3, g, 6 + g)
+            turn_x(3, g, 4 + g)
         for b in range(2):
-            u_bank(1, 0, b, 4 + b, high)
+            u_bank(1, 0, b, 6 + b)
 
         gain_on_gpsimd(0, 0, "h", hi=CELLS_ON_GPSIMD)
         for t in range(SLOTS):
@@ -456,32 +462,29 @@ def tile_pathway_latent_encoder_f5_kernel(
         for b in range(2):
             factor(1, 0, b)
         silu(1, 0)
-        factor(1, 1, 0)
         nc.sync.dma_start(out=tile("big", "noise", [P, TILES, LATENT], BF16)[:], in_=by_tile(noise))
-        order = (2, 1, 3, 0)
+        order = (2, 1, 0, 3)
         for g in order:
-            if g == 1:
-                quantize_e(1, hi=E_SPLIT)
-                quantize_e(1, lo=E_SPLIT)
-            else:
-                quantize_e(g)
+            quantize_e(g)
             for t in low:
-                v_pass(0, g, t, 4 + t, g == order[0], g == order[-1])
+                v_pass(0, g, t, 6 + t, g == order[0], g == order[-1])
 
-        gain_on_gpsimd(0, 1, "k")
+        gain_on_gpsimd(0, 1, "j")
         gain_on_scalar(0, 0, CELLS_ON_GPSIMD)
-        factor(1, 1, 1)
+        for b in range(2):
+            factor(1, 1, b)
         silu(1, 1)
+        interleave_a(0, 0, CELLS_ON_GPSIMD)
         for t in high:
             v_bank(0, t, t - 2)
         for g in range(PASSES):
             scale_x(3, g, "x_scaled" if g < 2 else "i")
         load_gain(0)
         for t in low:
-            v_bank(1, t, 6 + t)
+            v_bank(1, t, 4 + t)
         gains_to_psum(1)
         for t in high:
-            v_bank(1, t, 2 + t)
+            v_bank(1, t, 4 + t)
         for half in range(2):
             quantize_x(3, half)
         gain_on_gpsimd(1, 0, "i", hi=PAIR_CELLS_ON_GPSIMD)
@@ -489,8 +492,8 @@ def tile_pathway_latent_encoder_f5_kernel(
         for b in range(2):
             u_bank(2, 0, b, 2 + b)
         load_gain(1)
-        interleave_v(1, "j", on_scalar, lo=LATENT)
-        interleave_v(1, "ring", on_scalar, P, LATENT)
+        interleave_v(1, "ring", on_scalar, lo=LATENT)
+        interleave_v(1, "k", on_scalar, hi=LATENT)
         gain_on_vector(1, 1)
         gain_on_vector(1, 0, lo=PAIR_CELLS_ON_GPSIMD)
         for jg in range(GROUPS):
@@ -500,42 +503,41 @@ def tile_pathway_latent_encoder_f5_kernel(
             quantize_a(1, jg)
         factor(2, 0, 0)
         quantize_v(1, lo=LATENT)
-        interleave_v(1, "j", gpsimd_move, hi=P)
         u_bank(2, 1, 0, 0)
-        q_logvar(0, 6)
-        for t, number in ((2, 7), (3, 4)):
+        q_logvar(0, 4)
+        for t, number in ((2, 5), (3, 6)):
             u_slot(2, 1, t, number)
         factor(2, 0, 1)
         silu(2, 0)
         tanh(0)
         factor(2, 1, 0)
-        quantize_v(1, P, LATENT)
-        quantize_v(1, hi=P)
+        quantize_v(1, hi=LATENT)
 
-        gain_on_gpsimd(2, 0, "j")
+        gain_on_gpsimd(2, 0, "k")
         for t in high:
             factor_slot(2, 1, t)
         silu(2, 1)
-        q_mean(0, 5)
+        q_mean(0, 7)
         add_mean_bias(0)
         store("mu", 0)
         turn_back(0, 2)
         exp(0)
         q_mean(1, 3)
         q_logvar(1, 0)
-        q_mean(2, 7)
-        q_logvar(2, 6)
+        q_mean(2, 5)
+        q_logvar(2, 4)
         gain_on_vector(2, 1)
-        for jg in range(GROUPS):
+        add_mean_bias(1)
+        store("mu", 1)
+        for jg in (1, 0):
             quantize_a(2, jg)
-        for piece in (1, 2):
-            add_mean_bias(piece)
-            store("mu", piece)
-        for piece, number in ((3, 1), (4, 4)):
+        add_mean_bias(2)
+        store("mu", 2)
+        for piece, number in ((3, 1), (4, 6)):
             q_logvar(piece, number)
         tanh(1)
         turn_back(1, 3)
-        for piece, number in ((3, 5), (4, 2)):
+        for piece, number in ((3, 7), (4, 2)):
             q_mean(piece, number)
         tanh(2)
         exp(1)
@@ -543,7 +545,7 @@ def tile_pathway_latent_encoder_f5_kernel(
         tanh(3)
         tanh(4)
         exp(2)
-        for piece, number in ((3, 6), (4, 7)):
+        for piece, number in ((3, 4), (4, 5)):
             turn_back(piece, number)
             exp(piece)
         spread(0)

@@ -217,11 +217,11 @@ def tile_pathway_latent_encoder_f5_kernel(
             for t in slots:
                 mx(bank(first_bank + t, ("u", 0, jg, t), [P, 512])[:], ("w", jg, g), block(t), *x_operand(0, g), g == 0, g == PASSES - 1)
 
-        def u_bank(span, jg, b, number, passes=range(PASSES)):
+        def u_bank(span, jg, b, number):
             out = bank(number, ("u", span, jg, b), [P, 512])
-            for g in passes:
-                for t in range(2):
-                    mx(out[:, block(2 * t, 2)], ("w", jg, g), block(2 * b + t), *x_operand(span, g), (g, t) == (0, 0), (g, t) == (PASSES - 1, 1))
+            for t in range(2):
+                for g in range(PASSES):
+                    mx(out[:, block(2 * t, 2)], ("w", jg, g), block(2 * b + t), *x_operand(span, g), g == 0, g == PASSES - 1)
 
         def u_slot(span, jg, t, number):
             out = bank(number, ("u_slot", t), [P, 2 * P])
@@ -369,8 +369,9 @@ def tile_pathway_latent_encoder_f5_kernel(
         nc.sync.dma_start(out=gene_scale[:], in_=x_scale.rearrange("o (g p t) -> p (o g) t", p=P, t=SLOTS))
         load_x(2, 1)
         load_x(3, 1)
+        load_w(0)
         load_vectors()
-        for g in range(PASSES):
+        for g in range(1, PASSES):
             load_w(g)
         load_x(4, 2)
         for g in low:
@@ -392,17 +393,17 @@ def tile_pathway_latent_encoder_f5_kernel(
             widen(i, on_scalar, 2, 4)
         for i in (2, 3):
             widen(i, on_scalar)
-        gpsimd_move(out=slot_rows[:].rearrange("p t (c i) -> p t c i", i=4), in_=vector_rows[:].rearrange("p (c t i) -> p t c i", t=SLOTS, i=4))
         for pair in range(2):
             for g in range(PASSES):
                 turn_x(pair, g, 4 * pair + g)
                 scale_x(pair, g)
+        interleave_w(0, 0, "j", gpsimd_move)
+        interleave_w(1, 0, "ring", on_scalar)
+        on_scalar(out=slot_rows[:].rearrange("p t (c i) -> p t c i", i=4), in_=vector_rows[:].rearrange("p (c t i) -> p t c i", t=SLOTS, i=4))
         vectors = bank(0, "vectors", [P, SLOTS + 1, VECTOR_ROWS])
         for t in range(SLOTS + 1):
             rows = slot_rows[:, t, :] if t < SLOTS else vector_rows[:, 0:P]
             nc.tensor.matmul(vectors[:, t, :], lhsT=rows, rhs=ident_bf[:, 0:VECTOR_ROWS], start=True, stop=True)
-        interleave_w(0, 0, "j", gpsimd_move)
-        interleave_w(1, 0, "ring", on_scalar)
         interleave_w(0, 1, "h", gpsimd_move, hi=W_SPLIT)
         interleave_w(1, 1, "ring", on_scalar)
         on_scalar(out=vector_cols[:, :, 0 : SLOTS + 1], in_=vectors[:].rearrange("p t r -> p r t"))

@@ -25,7 +25,7 @@ FLOPS = 2 * CELLS * GENES * PATHWAYS + 2 * GENES * PATHWAYS * WIDE + 2 * CELLS *
 SPANS = [(0, 4), (4, 2), (6, 2)]
 PIECES = [(0, 2), (2, 2), (4, 2), (6, 1), (7, 1)]
 VECTOR_ROWS = 8
-W_SPLIT = 20
+W_SPLIT = 24
 CELLS_ON_GPSIMD = 320
 PAIR_CELLS_ON_GPSIMD = 128
 BUFFERS = {"x_raw": 2, "big": 4, "x_wide": 4, "x_scaled": 4, "ring": 4, "y4": 2, "y2": 2, "tanh": 4, "gained2": 2, "v_planes": 2}
@@ -253,16 +253,17 @@ def tile_pathway_latent_encoder_f5_kernel(
             return tile(tag or "gained2", ("gained", span, jg, 0), [P, SLOTS * width], BF16)[:, SLOTS * lo : SLOTS * (hi or width)]
 
         def gains_to_psum(number):
-            out = bank(number, "gains", [P, GROUPS, SLOTS])
+            out = bank(number, "gains", [P, GROUPS, SLOTS, 4])
             for t in range(SLOTS):
-                nc.tensor.matmul(out[:, :, t], lhsT=slot_rows[:, t, :], rhs=ident_bf[:, 4:6], start=True, stop=True)
+                rows = ident_bf[:, 4:6].unsqueeze(2).to_broadcast([P, GROUPS, 4])
+                nc.tensor.matmul(out[:, :, t, :], lhsT=slot_rows[:, t, :], rhs=rows, start=True, stop=True)
 
         def gain_on_vector(span, jg, tag=None, lo=0, hi=None):
             hi = hi or SPANS[span][1] * P
             nc.vector.tensor_tensor(
                 out=gained(span, jg, tag, lo, hi).rearrange("p (c i t) -> p c t i", i=4, t=SLOTS),
-                in0=held["y", span, jg][:, :, lo:hi].rearrange("p t (c i) -> p c t i", i=4),
-                in1=held["gains"][:, jg, :].unsqueeze(1).unsqueeze(3).to_broadcast([P, (hi - lo) // 4, SLOTS, 4]),
+                in0=held["gains"][:, jg, :, :].unsqueeze(1).to_broadcast([P, (hi - lo) // 4, SLOTS, 4]),
+                in1=held["y", span, jg][:, :, lo:hi].rearrange("p t (c i) -> p c t i", i=4),
                 op=ALU.mult,
             )
 

@@ -282,8 +282,9 @@ def tile_pathway_latent_encoder_f5_kernel(
             for t in range(SLOTS):
                 nc.scalar.activation(out=planes[:, t, :], in_=held["y", span, jg][:, t, lo:], func=ACT.Copy, scale=gain_col[:, jg, t : t + 1])
 
-        def interleave_a(span, jg, lo):
-            interleave_rows(held["gained", span, jg, 0][:, SLOTS * lo :], held["a_planes"][:], nc.scalar.copy)
+        def interleave_a(span, jg, lo, hi):
+            planes = held["a_planes"][:, :, lo - CELLS_ON_GPSIMD : hi - CELLS_ON_GPSIMD]
+            interleave_rows(held["gained", span, jg, 0][:, SLOTS * lo : SLOTS * hi], planes, nc.scalar.copy)
 
         def quantize_a(span, jg, lo=0, hi=None):
             quantize(("a", span, jg), held["gained", span, jg, lo][:], SPANS[span][1] * P, lo, hi)
@@ -476,98 +477,94 @@ def tile_pathway_latent_encoder_f5_kernel(
         for b in range(2):
             factor(1, 1, b)
         silu(1, 1)
-        interleave_a(0, 0, CELLS_ON_GPSIMD)
         for t in high:
             v_bank(0, t, t - 2)
         for g in range(PASSES):
             scale_x(3, g, "x_scaled" if g < 2 else "i")
-        load_gain(0)
-        for t in low:
-            v_bank(1, t, 4 + t)
-        gains_to_psum(1)
-        for t in high:
+        load_gain(0, low)
+        interleave_a(0, 0, CELLS_ON_GPSIMD, 416)
+        load_gain(0, high)
+        interleave_a(0, 0, 416, 512)
+        v_bank(1, 0, 4)
+        gains_to_psum(0)
+        for t in range(1, SLOTS):
             v_bank(1, t, 4 + t)
         for half in range(2):
             quantize_x(3, half)
         gain_on_gpsimd(1, 0, "i", hi=PAIR_CELLS_ON_GPSIMD)
-        interleave_v(0, "ring", on_scalar)
+        interleave_v(0, "ring", on_scalar, lo=P)
         for b in range(2):
             u_bank(2, 0, b, 2 + b)
         load_gain(1)
+        interleave_v(0, "ring", on_scalar, hi=P)
         interleave_v(1, "ring", on_scalar, lo=LATENT)
         interleave_v(1, "k", on_scalar, hi=LATENT)
         gain_on_vector(1, 1)
         gain_on_vector(1, 0, lo=PAIR_CELLS_ON_GPSIMD)
         for jg in range(GROUPS):
             quantize_a(0, jg)
-        quantize_v(0)
+        quantize_v(0, lo=P)
         for jg in (1, 0):
             quantize_a(1, jg)
         factor(2, 0, 0)
-        quantize_v(1, lo=LATENT)
-        u_bank(2, 1, 0, 0)
-        q_logvar(0, 4)
-        for t, number in ((2, 5), (3, 6)):
-            u_slot(2, 1, t, number)
+        quantize_v(0, hi=P)
         factor(2, 0, 1)
+        quantize_v(1, lo=LATENT)
+        u_bank(2, 1, 0, 1)
+        u_slot(2, 1, 2, 5)
+        q_logvar(0, 4)
+        u_slot(2, 1, 3, 6)
         silu(2, 0)
-        tanh(0)
         factor(2, 1, 0)
         quantize_v(1, hi=LATENT)
 
         gain_on_gpsimd(2, 0, "k")
         for t in high:
             factor_slot(2, 1, t)
+        tanh(0)
         silu(2, 1)
         q_mean(0, 7)
         add_mean_bias(0)
         store("mu", 0)
+        q_logvar(1, 1)
         turn_back(0, 2)
+        tanh(1)
         exp(0)
         q_mean(1, 3)
-        q_logvar(1, 0)
+        q_logvar(2, 6)
+        turn_back(1, 4)
         q_mean(2, 5)
-        q_logvar(2, 4)
+        exp(1)
         gain_on_vector(2, 1)
         add_mean_bias(1)
         store("mu", 1)
-        for jg in (1, 0):
+        for jg in (0, 1):
             quantize_a(2, jg)
         add_mean_bias(2)
         store("mu", 2)
-        for piece, number in ((3, 1), (4, 6)):
+        store("sd", 0)
+        for piece, number in ((3, 7), (4, 0)):
             q_logvar(piece, number)
-        tanh(1)
-        turn_back(1, 3)
-        for piece, number in ((3, 7), (4, 2)):
+        for piece, number in ((3, 3), (4, 1)):
             q_mean(piece, number)
-        tanh(2)
-        exp(1)
-        turn_back(2, 0)
-        tanh(3)
-        tanh(4)
-        exp(2)
-        for piece, number in ((3, 4), (4, 5)):
+        for piece in (2, 3, 4):
+            tanh(piece)
+        for piece, number in ((2, 2), (3, 4), (4, 5)):
             turn_back(piece, number)
             exp(piece)
-        spread(0)
-        store("sd", 0)
-        shift(0)
-        store("z", 0)
-        add_mean_bias(3)
-        spread(1)
-        add_mean_bias(4)
-        shift(1)
+        for step in (spread, shift):
+            for piece in range(2):
+                step(piece)
+        for piece in (3, 4):
+            add_mean_bias(piece)
         store("sd", 1)
-        store("mu", 3, 4)
+        store("z", 0)
         store("z", 1)
         store("sd", 2)
-        for piece in range(2, len(PIECES)):
-            spread(piece)
-            if piece > 2:
-                shift(piece - 1)
-                store("z", piece - 1)
-            if piece == 2:
-                store("sd", 3, 4)
-        shift(4)
-        store("z", 4)
+        store("mu", 3, 4)
+        store("sd", 3, 4)
+        for step in (spread, shift):
+            for piece in (2, 3, 4):
+                step(piece)
+        for piece in (2, 3, 4):
+            store("z", piece)

@@ -27,7 +27,6 @@ PIECES = [(0, 2), (2, 2), (4, 2), (6, 1), (7, 1)]
 VECTOR_ROWS = 8
 W_SPLIT = 24
 CELLS_ON_GPSIMD = 320
-PAIR_CELLS_ON_GPSIMD = 128
 BUFFERS = {"x_raw": 2, "big": 4, "x_wide": 4, "x_scaled": 4, "ring": 4, "y4": 2, "y2": 2, "tanh": 4, "gained2": 2, "v_planes": 2}
 
 
@@ -61,7 +60,7 @@ def tile_pathway_latent_encoder_f5_kernel(
         ident_bf = sb.tile([P, P], BF16, name="ident_bf")
         make_identity(nc, ident_bf[:])
         make_identity(nc, ident[:])
-        gene_scale = sb.tile([P, PASSES, SLOTS], F32, name="gene_scale")
+        gene_scale = sb.tile([P, PASSES, 8], F32, name="gene_scale")[:, :, 0:SLOTS]
         factor_col = sb.tile([P, TILES], BF16, name="factor_col")
         vector_rows = sb.tile([P, DEPTH], BF16, name="vector_rows")
         nc.gpsimd.memset(vector_rows[:], 0.0)
@@ -252,18 +251,12 @@ def tile_pathway_latent_encoder_f5_kernel(
             width = SPANS[span][1] * P
             return tile(tag or "gained2", ("gained", span, jg, 0), [P, SLOTS * width], BF16)[:, SLOTS * lo : SLOTS * (hi or width)]
 
-        def gains_to_psum(number):
-            out = bank(number, "gains", [P, GROUPS, SLOTS, 4])
-            for t in range(SLOTS):
-                rows = ident_bf[:, 4:6].unsqueeze(2).to_broadcast([P, GROUPS, 4])
-                nc.tensor.matmul(out[:, :, t, :], lhsT=slot_rows[:, t, :], rhs=rows, start=True, stop=True)
-
         def gain_on_vector(span, jg, tag=None, lo=0, hi=None):
             hi = hi or SPANS[span][1] * P
             nc.vector.tensor_tensor(
                 out=gained(span, jg, tag, lo, hi).rearrange("p (c i t) -> p c t i", i=4, t=SLOTS),
-                in0=held["gains"][:, jg, :, :].unsqueeze(1).to_broadcast([P, (hi - lo) // 4, SLOTS, 4]),
-                in1=held["y", span, jg][:, :, lo:hi].rearrange("p t (c i) -> p c t i", i=4),
+                in0=held["y", span, jg][:, :, lo:hi].rearrange("p t (c i) -> p c t i", i=4),
+                in1=gain_col[:, jg, :].unsqueeze(1).unsqueeze(3).to_broadcast([P, (hi - lo) // 4, SLOTS, 4]),
                 op=ALU.mult,
             )
 
@@ -367,8 +360,8 @@ def tile_pathway_latent_encoder_f5_kernel(
         nc.sync.dma_start(out=factor_col[:], in_=cell_factor.rearrange("(p i) -> p i", i=TILES))
         load_x(0, 2, 0, 1)
         load_x(0, 2, 1, 2)
+        nc.sync.dma_start(out=gene_scale, in_=x_scale.rearrange("o (g p t) -> p (o g) t", p=P, t=SLOTS))
         load_x(0, 2, 2, 4)
-        nc.sync.dma_start(out=gene_scale[:], in_=x_scale.rearrange("o (g p t) -> p (o g) t", p=P, t=SLOTS))
         load_x(2, 1)
         load_x(3, 1)
         load_w(0)
@@ -480,18 +473,15 @@ def tile_pathway_latent_encoder_f5_kernel(
         for t in high:
             v_bank(0, t, t - 2)
         for g in range(PASSES):
-            scale_x(3, g, "x_scaled" if g < 2 else "i")
+            scale_x(3, g, "x_scaled")
         load_gain(0, low)
         interleave_a(0, 0, CELLS_ON_GPSIMD, 416)
         load_gain(0, high)
         interleave_a(0, 0, 416, 512)
-        v_bank(1, 0, 4)
-        gains_to_psum(0)
-        for t in range(1, SLOTS):
+        for t in range(SLOTS):
             v_bank(1, t, 4 + t)
         for half in range(2):
             quantize_x(3, half)
-        gain_on_gpsimd(1, 0, "i", hi=PAIR_CELLS_ON_GPSIMD)
         interleave_v(0, "ring", on_scalar, lo=P)
         for b in range(2):
             u_bank(2, 0, b, 2 + b)
@@ -500,7 +490,7 @@ def tile_pathway_latent_encoder_f5_kernel(
         interleave_v(1, "ring", on_scalar, lo=LATENT)
         interleave_v(1, "k", on_scalar, hi=LATENT)
         gain_on_vector(1, 1)
-        gain_on_vector(1, 0, lo=PAIR_CELLS_ON_GPSIMD)
+        gain_on_vector(1, 0)
         for jg in range(GROUPS):
             quantize_a(0, jg)
         quantize_v(0, lo=P)
@@ -524,32 +514,32 @@ def tile_pathway_latent_encoder_f5_kernel(
         tanh(0)
         silu(2, 1)
         q_mean(0, 7)
-        add_mean_bias(0)
-        store("mu", 0)
         q_logvar(1, 1)
+        q_mean(1, 3)
         turn_back(0, 2)
         tanh(1)
         exp(0)
-        q_mean(1, 3)
         q_logvar(2, 6)
         turn_back(1, 4)
-        q_mean(2, 5)
+        q_mean(2, 0)
         exp(1)
+        for piece in range(2):
+            add_mean_bias(piece)
+            store("mu", piece)
         gain_on_vector(2, 1)
-        add_mean_bias(1)
-        store("mu", 1)
         for jg in (0, 1):
             quantize_a(2, jg)
         add_mean_bias(2)
         store("mu", 2)
+        tanh(2)
         store("sd", 0)
-        for piece, number in ((3, 7), (4, 0)):
+        for piece, number in ((3, 7), (4, 5)):
             q_logvar(piece, number)
         for piece, number in ((3, 3), (4, 1)):
             q_mean(piece, number)
-        for piece in (2, 3, 4):
+        for piece in (3, 4):
             tanh(piece)
-        for piece, number in ((2, 2), (3, 4), (4, 5)):
+        for piece, number in ((2, 2), (3, 4), (4, 6)):
             turn_back(piece, number)
             exp(piece)
         for step in (spread, shift):

@@ -25,8 +25,10 @@ FLOPS = 2 * CELLS * GENES * PATHWAYS + 2 * GENES * PATHWAYS * WIDE + 2 * CELLS *
 SPANS = [(0, 4), (4, 2), (6, 2)]
 PIECES = [(0, 2), (2, 2), (4, 2), (6, 1), (7, 1)]
 VECTOR_ROWS = 8
-W_SPLIT = 24
-CELLS_ON_GPSIMD = 320
+W_SPLIT = 26
+CELLS_ON_GPSIMD = 336
+PAIR_CELLS_ON_VECTOR = 192
+CODE_WORDS = {"wa": 8 * 512 + 2 * 512 + 4 * 256, "xev": 8 * 512 + 4 * 512 + 2 * 512}
 BUFFERS = {"x_raw": 2, "big": 4, "x_wide": 4, "x_scaled": 4, "ring": 4, "y4": 2, "y2": 2, "tanh": 4, "gained2": 2, "v_planes": 2}
 
 
@@ -36,6 +38,7 @@ def tile_pathway_latent_encoder_f5_kernel(
     nc = tc.nc
     with ExitStack() as ctx:
         sb = ctx.enter_context(tc.tile_pool(name="sb", bufs=1))
+        operands = ctx.enter_context(tc.tile_pool(name="operands", bufs=1))
         psum = ctx.enter_context(tc.psum_pool(name="banks", bufs=1))
         ctx.enter_context(tc.manual_schedule())
         held = {}
@@ -102,10 +105,21 @@ def tile_pathway_latent_encoder_f5_kernel(
             tiles = slice(tiles_of(pieces[0]).start, tiles_of(pieces[-1]).stop)
             nc.sync.dma_start(out=by_tile(out)[:, tiles, :], in_=held[name][:, tiles, :])
 
+        cursor, start = {}, 0
+        for part, size in (("codes", 4), ("scales", 1)):
+            for kind in ("wa", "xev"):
+                cursor[part, kind] = start
+                start += size * CODE_WORDS[kind] + 64
+
         def quantize(key, src, width, lo=0, hi=None):
             name = "".join(str(part) for part in key)
-            codes = tile(name + "_codes", ("codes",) + key, [P, width], U32)
-            scales = tile(name + "_scales", ("scales",) + key, [P, width], U8)
+            if ("codes",) + key not in held:
+                kind = "wa" if key[0] in "wa" else "xev"
+                for part, dtype, size in (("codes", U32, 4), ("scales", U8, 1)):
+                    at = cursor[part, kind]
+                    held[(part,) + key] = operands.tile([P, width], dtype, name=name + part, offset=at, align_bytes=256 if at == 0 else 64)
+                    cursor[part, kind] += size * width
+            codes, scales = held[("codes",) + key], held[("scales",) + key]
             nc.vector.quantize_mx(out=codes[:, lo:hi].bitcast(FP8X4), scales=scales[:, lo:hi], in_=src)
 
         def mx(out, left, left_cols, right, right_cols, start, stop):
@@ -130,31 +144,24 @@ def tile_pathway_latent_encoder_f5_kernel(
                 words = held["x_wide", 2 * pair + i][:].bitcast(F32)
                 for u in range(2):
                     nc.tensor.transpose(out[:, block(2 * u + i)], words[:, 256 * g + u : 256 * (g + 1) : 2], ident[:])
-            held["x_view", pair, g] = out[:].bitcast(BF16).rearrange("p (u m e) -> p m u e", u=2, e=2)
-
-        def turn_x_plain(pair, g, number):
-            out = bank(number, ("x_turned", pair, g), [P, SLOTS, 2, P], BF16)
-            for i in range(2):
-                genes = held["x_wide", 2 * pair + i][:, g * DEPTH : (g + 1) * DEPTH].rearrange("p (m t) -> p t m", t=SLOTS)
-                for t in range(SLOTS):
-                    nc.tensor.matmul(out[:, t, i, :], lhsT=genes[:, t, :], rhs=ident_bf[:], start=True, stop=True)
-            held["x_view", pair, g] = out[:].rearrange("p (u e) i m -> p (i m) u e", e=2)
 
         def x_place(pair, g):
-            return ((0, g), pair) if pair < 2 else ((pair, g // 2), g % 2)
+            if pair < 2:
+                return (0, g), pair
+            return ((2, g // 2), g % 2) if pair == 2 else ((3, 0), g)
 
         def scale_x(pair, g, tag="x_scaled"):
             key, half = x_place(pair, g)
-            scaled = tile(tag, ("x_scaled",) + key, [P, 2, 1024], BF16)
+            scaled = tile(tag, ("x_scaled",) + key, [P, 4 if pair == 3 else 2, 1024], BF16)
             nc.vector.tensor_tensor(
                 out=scaled[:, half, :].rearrange("p (m u e) -> p m u e", u=2, e=2),
-                in0=held["x_view", pair, g],
+                in0=held["x_turned", pair, g][:].bitcast(BF16).rearrange("p (u m e) -> p m u e", u=2, e=2),
                 in1=gene_scale[:, g, :].rearrange("p (u e) -> p u e", e=2).unsqueeze(1).to_broadcast([P, 256, 2, 2]),
                 op=ALU.mult,
             )
 
         def quantize_x(*key):
-            quantize(("x",) + key, held[("x_scaled",) + key][:].rearrange("p g c -> p (g c)"), 512)
+            quantize(("x",) + key, held[("x_scaled",) + key][:].rearrange("p g c -> p (g c)"), 1024 if key[0] == 3 else 512)
 
         def x_operand(span, g):
             first, count = SPANS[span]
@@ -175,23 +182,17 @@ def tile_pathway_latent_encoder_f5_kernel(
                 in_=raw.rearrange("p j (c t i) -> " + walk, t=SLOTS, i=4)[:, lo:hi],
             )
 
-        def interleave_rows(out, rows, move):
-            if move is gpsimd_move:
-                move(out=out.rearrange("p (c j) -> p c j", j=SLOTS), in_=rows.rearrange("p j c -> p c j"))
-            else:
-                move(out=out.rearrange("p (c i j) -> p c j i", i=4, j=SLOTS), in_=rows.rearrange("p j (c i) -> p c j i", i=4))
+        def interleave_rows(out, rows):
+            nc.scalar.copy(out=out.rearrange("p (c i j) -> p c j i", i=4, j=SLOTS), in_=rows.rearrange("p j (c i) -> p c j i", i=4))
 
-        def interleave_e(g, tag, move, lo=0, hi=WIDE):
-            out = tile(tag, ("grouped", "e", g, lo), [P, SLOTS * (hi - lo)], BF16)
-            interleave_rows(out[:], rows_of("e", g)[:, :, lo:hi], move)
+        def interleave_e(g, tag):
+            interleave_rows(tile(tag, ("grouped", "e", g), [P, SLOTS * WIDE], BF16)[:], rows_of("e", g))
 
         def interleave_e_pair(tag):
             out = tile(tag, ("grouped", "e pair"), [P, 2, SLOTS * WIDE], BF16)
             gpsimd_move(out=out[:].rearrange("p g (c j) -> p g c j", j=SLOTS), in_=held["e_raw", 0][:].rearrange("p g j c -> p g c j"))
-            for g in range(2):
-                held["grouped", "e", g, 0] = out[:, g, :]
 
-        def interleave_w_on_tensor(jg, g, tag, numbers):
+        def interleave_w_on_tensor(jg, g, numbers):
             for t in range(SLOTS):
                 nc.tensor.matmul(
                     bank(numbers[t // 2], ("moved", jg, g, t // 2), [P, 2, DEPTH], BF16)[:, t % 2, :].rearrange("p (c i j) -> p j c i", i=4, j=SLOTS),
@@ -209,8 +210,11 @@ def tile_pathway_latent_encoder_f5_kernel(
         def quantize_w(jg, g):
             quantize(("w", jg, g), held["grouped", jg, g][:], DEPTH)
 
-        def quantize_e(g, lo=0, hi=WIDE):
-            quantize(("e", g), held["grouped", "e", g, lo][:], WIDE, lo, hi)
+        def quantize_e(g):
+            quantize(("e", g), held["grouped", "e", g][:], WIDE)
+
+        def quantize_e_pair():
+            quantize(("e", 0), held["grouped", "e pair"][:].rearrange("p g c -> p (g c)"), 2 * WIDE)
 
         def u_pass(jg, g, first_bank, slots=range(SLOTS)):
             for t in slots:
@@ -247,43 +251,39 @@ def tile_pathway_latent_encoder_f5_kernel(
             for t in slots:
                 nc.scalar.activation(out=y[:, t, :], in_=y[:, t, :], func=ACT.Silu, bias=bias_col[:, jg, t : t + 1])
 
-        def gained(span, jg, tag=None, lo=0, hi=None):
-            width = SPANS[span][1] * P
-            return tile(tag or "gained2", ("gained", span, jg, 0), [P, SLOTS * width], BF16)[:, SLOTS * lo : SLOTS * (hi or width)]
+        def gained(span, jg, lo, hi, tag="gained2"):
+            return tile(tag, ("gained", span, jg), [P, SLOTS * SPANS[span][1] * P], BF16)[:, SLOTS * lo : SLOTS * hi]
 
-        def gain_on_vector(span, jg, tag=None, lo=0, hi=None):
-            hi = hi or SPANS[span][1] * P
+        def gain_on_vector(span, jg, cells=2 * P):
             nc.vector.tensor_tensor(
-                out=gained(span, jg, tag, lo, hi).rearrange("p (c i t) -> p c t i", i=4, t=SLOTS),
-                in0=held["y", span, jg][:, :, lo:hi].rearrange("p t (c i) -> p c t i", i=4),
-                in1=gain_col[:, jg, :].unsqueeze(1).unsqueeze(3).to_broadcast([P, (hi - lo) // 4, SLOTS, 4]),
+                out=gained(span, jg, 0, cells).rearrange("p (c i t) -> p c t i", i=4, t=SLOTS),
+                in0=held["y", span, jg][:, :, 0:cells].rearrange("p t (c i) -> p c t i", i=4),
+                in1=gain_col[:, jg, :].unsqueeze(1).unsqueeze(3).to_broadcast([P, cells // 4, SLOTS, 4]),
                 op=ALU.mult,
             )
 
-        def gain_on_gpsimd(span, jg, tag, lo=0, hi=None):
-            hi = hi or SPANS[span][1] * P
+        def gain_on_gpsimd(span, jg, tag, cells):
             nc.gpsimd.tensor_tensor(
-                out=gained(span, jg, tag, lo, hi).rearrange("p (c t) -> p c t", t=SLOTS),
-                in0=held["y", span, jg][:, :, lo:hi].rearrange("p t c -> p c t"),
-                in1=gain_col[:, jg, :].unsqueeze(1).to_broadcast([P, hi - lo, SLOTS]),
+                out=gained(span, jg, 0, cells, tag).rearrange("p (c t) -> p c t", t=SLOTS),
+                in0=held["y", span, jg][:, :, 0:cells].rearrange("p t c -> p c t"),
+                in1=gain_col[:, jg, :].unsqueeze(1).to_broadcast([P, cells, SLOTS]),
                 op=ALU.mult,
             )
 
         def gain_on_scalar(span, jg, lo):
-            width = SPANS[span][1] * P - lo
-            planes = tile("a_planes", "a_planes", [P, SLOTS, width], BF16)
+            planes = tile("a_planes", ("a_planes", span), [P, SLOTS, SPANS[span][1] * P - lo], BF16)
             for t in range(SLOTS):
                 nc.scalar.activation(out=planes[:, t, :], in_=held["y", span, jg][:, t, lo:], func=ACT.Copy, scale=gain_col[:, jg, t : t + 1])
 
-        def interleave_a(span, jg, lo, hi):
-            planes = held["a_planes"][:, :, lo - CELLS_ON_GPSIMD : hi - CELLS_ON_GPSIMD]
-            interleave_rows(held["gained", span, jg, 0][:, SLOTS * lo : SLOTS * hi], planes, nc.scalar.copy)
+        def interleave_a(span, jg, lo):
+            interleave_rows(gained(span, jg, lo, SPANS[span][1] * P), held["a_planes", span][:])
 
-        def quantize_a(span, jg, lo=0, hi=None):
-            quantize(("a", span, jg), held["gained", span, jg, lo][:], SPANS[span][1] * P, lo, hi)
+        def quantize_a(span, jg):
+            quantize(("a", span, jg), held["gained", span, jg][:], SPANS[span][1] * P)
 
         def v_pass(jg, g, t, number, start, stop):
-            mx(bank(number, ("v", jg, t), [P, WIDE])[:], ("w", jg, g), block(t), ("e", g), slice(0, WIDE), start, stop)
+            e_codes, e_cols = (("e", 0), block(4 * g, 4)) if g < 2 else (("e", g), block(0, 4))
+            mx(bank(number, ("v", jg, t), [P, WIDE])[:], ("w", jg, g), block(t), e_codes, e_cols, start, stop)
 
         def v_bank(jg, t, number):
             for g in range(PASSES):
@@ -294,9 +294,9 @@ def tile_pathway_latent_encoder_f5_kernel(
             for t in slots:
                 nc.scalar.activation(out=planes[:, t, :], in_=held["v", jg, t][:], func=ACT.Copy, scale=loading_col[:, jg, t : t + 1])
 
-        def interleave_v(jg, tag, move, lo=0, hi=WIDE):
+        def interleave_v(jg, tag, lo=0, hi=WIDE):
             out = tile(tag, ("grouped", "v", jg, lo), [P, SLOTS * (hi - lo)], BF16)
-            interleave_rows(out[:], held["v_planes", jg][:, :, lo:hi], move)
+            interleave_rows(out[:], held["v_planes", jg][:, :, lo:hi])
 
         def quantize_v(jg, lo=0, hi=WIDE):
             quantize(("v", jg), held["grouped", "v", jg, lo][:], WIDE, lo, hi)
@@ -342,13 +342,8 @@ def tile_pathway_latent_encoder_f5_kernel(
         def spread(piece):
             nc.vector.tensor_tensor(out=result("z", piece), in0=result("sd", piece), in1=held["noise"][:, tiles_of(piece), :], op=ALU.mult)
 
-        def shift(piece, engine=nc.vector):
-            engine.tensor_tensor(out=result("z", piece), in0=result("z", piece), in1=result("mu", piece), op=ALU.add)
-
-        def warm_tensor(key, number, count):
-            out = bank(number, ("warm", key), [P, SLOTS, P])
-            for n in range(count):
-                nc.tensor.matmul(out[:], lhsT=ident_bf[:], rhs=ident_bf[:].unsqueeze(1).to_broadcast([P, SLOTS, P]), start=True, stop=True)
+        def shift(piece):
+            nc.vector.tensor_tensor(out=result("z", piece), in0=result("z", piece), in1=result("mu", piece), op=ALU.add)
 
         on_scalar, on_vector = nc.scalar.copy, nc.vector.tensor_copy
         low, high = range(0, 2), range(2, 4)
@@ -392,28 +387,28 @@ def tile_pathway_latent_encoder_f5_kernel(
             for g in range(PASSES):
                 turn_x(pair, g, 4 * pair + g)
                 scale_x(pair, g)
-        interleave_w(0, 0, "j", gpsimd_move)
+        interleave_w(0, 0, "gate_c", gpsimd_move)
         interleave_w(1, 0, "ring", on_scalar)
         on_scalar(out=slot_rows[:].rearrange("p t (c i) -> p t c i", i=4), in_=vector_rows[:].rearrange("p (c t i) -> p t c i", t=SLOTS, i=4))
         vectors = bank(0, "vectors", [P, SLOTS + 1, VECTOR_ROWS])
         for t in range(SLOTS + 1):
             rows = slot_rows[:, t, :] if t < SLOTS else vector_rows[:, 0:P]
             nc.tensor.matmul(vectors[:, t, :], lhsT=rows, rhs=ident_bf[:, 0:VECTOR_ROWS], start=True, stop=True)
-        interleave_w(0, 1, "h", gpsimd_move, hi=W_SPLIT)
+        interleave_w(0, 1, "gate_a", gpsimd_move, hi=W_SPLIT)
         interleave_w(1, 1, "ring", on_scalar)
         on_scalar(out=vector_cols[:, :, 0 : SLOTS + 1], in_=vectors[:].rearrange("p t r -> p r t"))
-        interleave_w_on_tensor(1, 2, "i", (1, 2))
+        interleave_w_on_tensor(1, 2, (1, 2))
         for g in (2, 3):
             interleave_w(0, g, "ring", on_scalar)
-        empty_moved(1, 2, "i")
+        empty_moved(1, 2, "gate_b")
 
         for g in range(PASSES):
             if g == 1:
-                interleave_w(0, 1, "h", on_vector, lo=W_SPLIT)
+                interleave_w(0, 1, "gate_a", on_vector, lo=W_SPLIT)
             quantize_x(0, g)
             quantize_w(0, g)
             u_pass(0, g, 4)
-        interleave_w(1, 3, "k", on_scalar)
+        interleave_w(1, 3, "gate_d", on_scalar)
         for lo in (0, 2):
             for i in (4, 5):
                 widen(i, on_scalar, lo, lo + 2)
@@ -422,7 +417,7 @@ def tile_pathway_latent_encoder_f5_kernel(
         for i in (6, 7):
             widen(i, on_scalar)
 
-        interleave_e_pair("k")
+        interleave_e_pair("gate_d")
         u_pass(1, 0, 0)
         u_pass(1, 1, 0, low)
         for t in range(SLOTS):
@@ -437,17 +432,17 @@ def tile_pathway_latent_encoder_f5_kernel(
         u_pass(1, 2, 0, high)
         u_pass(1, 3, 0)
         for g in range(PASSES):
-            scale_x(2, g, "ih"[g // 2])
+            scale_x(2, g, ("gate_b", "gate_a")[g // 2])
         for half in range(2):
             quantize_x(2, half)
-        interleave_e(2, "ring", on_scalar)
-        interleave_e(3, "j", on_scalar)
+        interleave_e(2, "ring")
+        interleave_e(3, "gate_c")
         for g in low:
             turn_x(3, g, 4 + g)
         for b in range(2):
             u_bank(1, 0, b, 6 + b)
 
-        gain_on_gpsimd(0, 0, "h", hi=CELLS_ON_GPSIMD)
+        gain_on_gpsimd(0, 0, "gate_a", CELLS_ON_GPSIMD)
         for t in range(SLOTS):
             factor(0, 1, t)
         silu(0, 1)
@@ -459,13 +454,15 @@ def tile_pathway_latent_encoder_f5_kernel(
             factor(1, 0, b)
         silu(1, 0)
         nc.sync.dma_start(out=tile("big", "noise", [P, TILES, LATENT], BF16)[:], in_=by_tile(noise))
-        order = (2, 1, 0, 3)
+        order = (2, 0, 1, 3)
+        quantize_e(2)
+        quantize_e_pair()
+        quantize_e(3)
         for g in order:
-            quantize_e(g)
             for t in low:
                 v_pass(0, g, t, 6 + t, g == order[0], g == order[-1])
 
-        gain_on_gpsimd(0, 1, "j")
+        gain_on_gpsimd(0, 1, "gate_c", 4 * P)
         gain_on_scalar(0, 0, CELLS_ON_GPSIMD)
         for b in range(2):
             factor(1, 1, b)
@@ -473,33 +470,32 @@ def tile_pathway_latent_encoder_f5_kernel(
         for t in high:
             v_bank(0, t, t - 2)
         for g in range(PASSES):
-            scale_x(3, g, "x_scaled")
+            scale_x(3, g, "gate_d")
         load_gain(0, low)
-        interleave_a(0, 0, CELLS_ON_GPSIMD, 416)
-        load_gain(0, high)
-        interleave_a(0, 0, 416, 512)
+        interleave_a(0, 0, CELLS_ON_GPSIMD)
+        load_gain(0, range(2, 3))
+        gain_on_scalar(1, 0, PAIR_CELLS_ON_VECTOR)
+        load_gain(0, range(3, 4))
+        interleave_a(1, 0, PAIR_CELLS_ON_VECTOR)
         for t in range(SLOTS):
             v_bank(1, t, 4 + t)
-        for half in range(2):
-            quantize_x(3, half)
-        interleave_v(0, "ring", on_scalar, lo=P)
+        gain_on_vector(1, 1)
+        quantize_x(3, 0)
+        interleave_v(0, "ring")
         for b in range(2):
             u_bank(2, 0, b, 2 + b)
         load_gain(1)
-        interleave_v(0, "ring", on_scalar, hi=P)
-        interleave_v(1, "ring", on_scalar, lo=LATENT)
-        interleave_v(1, "k", on_scalar, hi=LATENT)
-        gain_on_vector(1, 1)
-        gain_on_vector(1, 0)
+        interleave_v(1, "ring", lo=LATENT)
+        interleave_v(1, "gate_d", hi=LATENT)
+        gain_on_vector(1, 0, PAIR_CELLS_ON_VECTOR)
         for jg in range(GROUPS):
             quantize_a(0, jg)
-        quantize_v(0, lo=P)
-        for jg in (1, 0):
-            quantize_a(1, jg)
+        quantize_v(0)
         factor(2, 0, 0)
-        quantize_v(0, hi=P)
         factor(2, 0, 1)
         quantize_v(1, lo=LATENT)
+        for jg in (1, 0):
+            quantize_a(1, jg)
         u_bank(2, 1, 0, 1)
         u_slot(2, 1, 2, 5)
         q_logvar(0, 4)
@@ -508,7 +504,7 @@ def tile_pathway_latent_encoder_f5_kernel(
         factor(2, 1, 0)
         quantize_v(1, hi=LATENT)
 
-        gain_on_gpsimd(2, 0, "k")
+        gain_on_gpsimd(2, 0, "gate_d", 2 * P)
         for t in high:
             factor_slot(2, 1, t)
         tanh(0)

from contextlib import ExitStack

import concourse.mybir as mybir
from concourse.masks import make_identity

F32 = mybir.dt.float32
BF16 = mybir.dt.bfloat16
U32 = mybir.dt.uint32
U8 = mybir.dt.uint8
F8 = mybir.dt.float8_e4m3fn
FP8X4 = mybir.dt.float8_e4m3fn_x4
ACT = mybir.ActivationFunctionType
ALU = mybir.AluOpType

CELLS, GENES, PATHWAYS, LATENT = 1024, 2048, 1024, 256
WIDE = 2 * LATENT
P = 128
SLOTS = 4
DEPTH = P * SLOTS
PASSES = GENES // DEPTH
GROUPS = PATHWAYS // DEPTH
TILES = CELLS // P
FLOPS = 2 * CELLS * GENES * PATHWAYS + 2 * GENES * PATHWAYS * WIDE + 2 * CELLS * PATHWAYS * WIDE

SPANS = [(0, 4), (4, 2), (6, 2)]
PIECES = [(0, 2), (2, 2), (4, 2), (6, 1), (7, 1)]
VECTOR_ROWS = 8
W_SPLIT = 26
CELLS_ON_GPSIMD = 336
PAIR_CELLS_ON_VECTOR = 192
CODE_WORDS = {"wa": 8 * 512 + 2 * 512 + 4 * 256, "xev": 8 * 512 + 4 * 512 + 2 * 512}
BUFFERS = {"x_raw": 2, "big": 4, "x_wide": 4, "x_scaled": 4, "ring": 4, "y4": 2, "y2": 2, "tanh": 4, "gained2": 2, "v_planes": 2}


def tile_pathway_latent_encoder_f5_kernel(
    tc, x_bytes, x_scale, w, e, cell_factor, pathway_bias, activity_gain, loading_gain, latent_bias, noise, mu_out, sd_out, z_out
):
    nc = tc.nc
    with ExitStack() as ctx:
        sb = ctx.enter_context(tc.tile_pool(name="sb", bufs=1))
        operands = ctx.enter_context(tc.tile_pool(name="operands", bufs=1))
        psum = ctx.enter_context(tc.psum_pool(name="banks", bufs=1))
        ctx.enter_context(tc.manual_schedule())
        held = {}

        def tile(tag, key, shape, dtype):
            if key not in held:
                held[key] = sb.tile(shape, dtype, name=tag, bufs=BUFFERS.get(tag, 1), align_bytes=64)
            return held[key]

        def bank(number, key, shape, dtype=F32):
            if key not in held:
                held[key] = psum.tile(shape, dtype, name="bank%d" % number)
            return held[key]

        def by_tile(ap):
            return ap.rearrange("(p i) c -> p i c", i=TILES)

        def block(n, count=1):
            return slice(n * P, (n + count) * P)

        ident = sb.tile([P, P], F32, name="ident")
        ident_bf = sb.tile([P, P], BF16, name="ident_bf")
        make_identity(nc, ident_bf[:])
        make_identity(nc, ident[:])
        gene_scale = sb.tile([P, PASSES, 8], F32, name="gene_scale")[:, :, 0:SLOTS]
        factor_col = sb.tile([P, TILES], BF16, name="factor_col")
        vector_rows = sb.tile([P, DEPTH], BF16, name="vector_rows")
        nc.gpsimd.memset(vector_rows[:], 0.0)
        slot_rows = sb.tile([P, SLOTS, P], BF16, name="slot_rows")
        vector_cols = sb.tile([P, VECTOR_ROWS, 8], F32, name="vector_cols")
        bias_col, loading_col, gain_col = (vector_cols[:, 2 * n : 2 * n + 2, 0:SLOTS] for n in range(3))
        mean_bias = sb.tile([P, LATENT], BF16, name="mean_bias")
        factor_row = sb.tile([P, CELLS], BF16, name="factor_row")

        def load_x(first, count, lo=0, hi=PASSES):
            tag = "x_raw" if first >= 4 else "x_raw%d%d" % (first, lo)
            raw = tile(tag, ("x_raw", first, lo), [P, count, (hi - lo) * DEPTH], U8)
            nc.sync.dma_start(out=raw[:], in_=by_tile(x_bytes)[:, first : first + count, lo * DEPTH : hi * DEPTH])
            for i in range(count):
                for g in range(lo, hi):
                    held["x_bytes", first + i, g] = (raw, i, g - lo)

        def load_w(g):
            raw = tile("big", ("w_raw", g), [P, SLOTS, PATHWAYS], BF16)
            nc.sync.dma_start(out=raw[:], in_=w[g * DEPTH : (g + 1) * DEPTH, :].rearrange("(p j) n -> p j n", j=SLOTS))

        def load_e(g):
            raw = tile("big", ("e_raw", g // 2), [P, 2, SLOTS, WIDE], BF16)
            nc.sync.dma_start(out=raw[:, g % 2, :, :], in_=e[g * DEPTH : (g + 1) * DEPTH, :].rearrange("(p j) n -> p j n", j=SLOTS))

        def load_vectors():
            for n, vec in enumerate((pathway_bias, loading_gain, activity_gain)):
                nc.sync.dma_start(out=vector_rows[2 * n : 2 * n + 2, :], in_=vec.rearrange("(g c) -> g c", g=GROUPS))
            nc.sync.dma_start(out=vector_rows[6:8, 0:P], in_=latent_bias[LATENT:WIDE].rearrange("(h p) -> h p", h=2))

        def tiles_of(piece):
            return slice(PIECES[piece][0], PIECES[piece][0] + PIECES[piece][1])

        def result(name, piece):
            return tile("big", name, [P, TILES, LATENT], F32)[:, tiles_of(piece), :]

        def store(name, *pieces):
            out = {"mu": mu_out, "sd": sd_out, "z": z_out}[name]
            tiles = slice(tiles_of(pieces[0]).start, tiles_of(pieces[-1]).stop)
            nc.sync.dma_start(out=by_tile(out)[:, tiles, :], in_=held[name][:, tiles, :])

        cursor, start = {}, 0
        for part, size in (("codes", 4), ("scales", 1)):
            for kind in ("wa", "xev"):
                cursor[part, kind] = start
                start += size * CODE_WORDS[kind] + 64

        def quantize(key, src, width, lo=0, hi=None):
            name = "".join(str(part) for part in key)
            if ("codes",) + key not in held:
                kind = "wa" if key[0] in "wa" else "xev"
                for part, dtype, size in (("codes", U32, 4), ("scales", U8, 1)):
                    at = cursor[part, kind]
                    held[(part,) + key] = operands.tile([P, width], dtype, name=name + part, offset=at, align_bytes=256 if at == 0 else 64)
                    cursor[part, kind] += size * width
            codes, scales = held[("codes",) + key], held[("scales",) + key]
            nc.vector.quantize_mx(out=codes[:, lo:hi].bitcast(FP8X4), scales=scales[:, lo:hi], in_=src)

        def mx(out, left, left_cols, right, right_cols, start, stop):
            nc.tensor.matmul_mx(
                out=out,
                lhsT=held[("codes",) + left][:, left_cols].bitcast(FP8X4),
                lhsT_scale=held[("scales",) + left][:, left_cols],
                rhs=held[("codes",) + right][:, right_cols].bitcast(FP8X4),
                rhs_scale=held[("scales",) + right][:, right_cols],
                start=start,
                stop=stop,
            )

        def widen(i, copy, lo=0, hi=PASSES):
            wide = tile("x_wide", ("x_wide", i), [P, GENES], BF16)
            raw, row, start = held["x_bytes", i, lo]
            copy(out=wide[:, lo * DEPTH : hi * DEPTH], in_=raw[:, row, start * DEPTH : (start + hi - lo) * DEPTH].bitcast(F8))

        def turn_x(pair, g, number):
            out = bank(number, ("x_turned", pair, g), [P, 512])
            for i in range(2):
                words = held["x_wide", 2 * pair + i][:].bitcast(F32)
                for u in range(2):
                    nc.tensor.transpose(out[:, block(2 * u + i)], words[:, 256 * g + u : 256 * (g + 1) : 2], ident[:])

        def x_place(pair, g):
            if pair < 2:
                return (0, g), pair
            return ((2, g // 2), g % 2) if pair == 2 else ((3, 0), g)

        def scale_x(pair, g, tag="x_scaled"):
            key, half = x_place(pair, g)
            scaled = tile(tag, ("x_scaled",) + key, [P, 4 if pair == 3 else 2, 1024], BF16)
            nc.vector.tensor_tensor(
                out=scaled[:, half, :].rearrange("p (m u e) -> p m u e", u=2, e=2),
                in0=held["x_turned", pair, g][:].bitcast(BF16).rearrange("p (u m e) -> p m u e", u=2, e=2),
                in1=gene_scale[:, g, :].rearrange("p (u e) -> p u e", e=2).unsqueeze(1).to_broadcast([P, 256, 2, 2]),
                op=ALU.mult,
            )

        def quantize_x(*key):
            quantize(("x",) + key, held[("x_scaled",) + key][:].rearrange("p g c -> p (g c)"), 1024 if key[0] == 3 else 512)

        def x_operand(span, g):
            first, count = SPANS[span]
            key, half = x_place(first // 2, g)
            return ("x",) + key, block(2 * half, count)

        def rows_of(k, g):
            return held["e_raw", g // 2][:, g % 2, :, :] if k == "e" else held["w_raw", g][:, :, k * DEPTH : (k + 1) * DEPTH]

        def gpsimd_move(out, in_):
            nc.gpsimd.tensor_scalar(out=out, in0=in_, scalar1=1.0, scalar2=0.0, op0=ALU.mult, op1=ALU.add)

        def interleave_w(jg, g, tag, move, lo=0, hi=32):
            out, raw = tile(tag, ("grouped", jg, g), [P, SLOTS * DEPTH], BF16)[:], rows_of(jg, g)
            walk = "p c t i j" if move is gpsimd_move else "p c t j i"
            move(
                out=out.rearrange("p (t c i j) -> " + walk, t=SLOTS, i=4, j=SLOTS)[:, lo:hi],
                in_=raw.rearrange("p j (c t i) -> " + walk, t=SLOTS, i=4)[:, lo:hi],
            )

        def interleave_rows(out, rows):
            nc.scalar.copy(out=out.rearrange("p (c i j) -> p c j i", i=4, j=SLOTS), in_=rows.rearrange("p j (c i) -> p c j i", i=4))

        def interleave_e(g, tag):
            interleave_rows(tile(tag, ("grouped", "e", g), [P, SLOTS * WIDE], BF16)[:], rows_of("e", g))

        def interleave_e_pair(tag):
            out = tile(tag, ("grouped", "e pair"), [P, 2, SLOTS * WIDE], BF16)
            gpsimd_move(out=out[:].rearrange("p g (c j) -> p g c j", j=SLOTS), in_=held["e_raw", 0][:].rearrange("p g j c -> p g c j"))

        def interleave_w_on_tensor(jg, g, numbers):
            for t in range(SLOTS):
                nc.tensor.matmul(
                    bank(numbers[t // 2], ("moved", jg, g, t // 2), [P, 2, DEPTH], BF16)[:, t % 2, :].rearrange("p (c i j) -> p j c i", i=4, j=SLOTS),
                    lhsT=ident_bf[:],
                    rhs=rows_of(jg, g).rearrange("p j (c t i) -> p t j c i", t=SLOTS, i=4)[:, t, :, :, :],
                    start=True,
                    stop=True,
                )

        def empty_moved(jg, g, tag):
            for half in range(2):
                out = tile(tag, ("grouped", jg, g), [P, SLOTS * DEPTH], BF16)[:, half * 1024 : (half + 1) * 1024]
                nc.scalar.copy(out=out, in_=held["moved", jg, g, half][:].rearrange("p t c -> p (t c)"))

        def quantize_w(jg, g):
            quantize(("w", jg, g), held["grouped", jg, g][:], DEPTH)

        def quantize_e(g):
            quantize(("e", g), held["grouped", "e", g][:], WIDE)

        def quantize_e_pair():
            quantize(("e", 0), held["grouped", "e pair"][:].rearrange("p g c -> p (g c)"), 2 * WIDE)

        def u_pass(jg, g, first_bank, slots=range(SLOTS)):
            for t in slots:
                mx(bank(first_bank + t, ("u", 0, jg, t), [P, 512])[:], ("w", jg, g), block(t), *x_operand(0, g), g == 0, g == PASSES - 1)

        def u_bank(span, jg, b, number):
            out = bank(number, ("u", span, jg, b), [P, 512])
            for t in range(2):
                for g in range(PASSES):
                    mx(out[:, block(2 * t, 2)], ("w", jg, g), block(2 * b + t), *x_operand(span, g), g == 0, g == PASSES - 1)

        def u_slot(span, jg, t, number):
            out = bank(number, ("u_slot", t), [P, 2 * P])
            for g in range(PASSES):
                mx(out[:], ("w", jg, g), block(t), *x_operand(span, g), g == 0, g == PASSES - 1)

        def factor_slot(span, jg, t):
            first, count = SPANS[span]
            nc.vector.tensor_tensor(out=held["y", span, jg][:, t, :], in0=held["u_slot", t][:], in1=factor_row[:, block(first, count)], op=ALU.mult)

        def factor(span, jg, b):
            first, count = SPANS[span]
            per = SLOTS // count
            y = tile("y%d" % count, ("y", span, jg), [P, SLOTS, count * P], F32)
            nc.vector.tensor_tensor(
                out=y[:, per * b : per * (b + 1), :],
                in0=held["u", span, jg, b][:].rearrange("p (t m) -> p t m", t=per),
                in1=factor_row[:, block(first, count)].unsqueeze(1).to_broadcast([P, per, count * P]),
                op=ALU.mult,
            )

        def silu(span, jg, slots=range(SLOTS)):
            y = held["y", span, jg]
            for t in slots:
                nc.scalar.activation(out=y[:, t, :], in_=y[:, t, :], func=ACT.Silu, bias=bias_col[:, jg, t : t + 1])

        def gained(span, jg, lo, hi, tag="gained2"):
            return tile(tag, ("gained", span, jg), [P, SLOTS * SPANS[span][1] * P], BF16)[:, SLOTS * lo : SLOTS * hi]

        def gain_on_vector(span, jg, cells=2 * P):
            nc.vector.tensor_tensor(
                out=gained(span, jg, 0, cells).rearrange("p (c i t) -> p c t i", i=4, t=SLOTS),
                in0=held["y", span, jg][:, :, 0:cells].rearrange("p t (c i) -> p c t i", i=4),
                in1=gain_col[:, jg, :].unsqueeze(1).unsqueeze(3).to_broadcast([P, cells // 4, SLOTS, 4]),
                op=ALU.mult,
            )

        def gain_on_gpsimd(span, jg, tag, cells):
            nc.gpsimd.tensor_tensor(
                out=gained(span, jg, 0, cells, tag).rearrange("p (c t) -> p c t", t=SLOTS),
                in0=held["y", span, jg][:, :, 0:cells].rearrange("p t c -> p c t"),
                in1=gain_col[:, jg, :].unsqueeze(1).to_broadcast([P, cells, SLOTS]),
                op=ALU.mult,
            )

        def gain_on_scalar(span, jg, lo):
            planes = tile("a_planes", ("a_planes", span), [P, SLOTS, SPANS[span][1] * P - lo], BF16)
            for t in range(SLOTS):
                nc.scalar.activation(out=planes[:, t, :], in_=held["y", span, jg][:, t, lo:], func=ACT.Copy, scale=gain_col[:, jg, t : t + 1])

        def interleave_a(span, jg, lo):
            interleave_rows(gained(span, jg, lo, SPANS[span][1] * P), held["a_planes", span][:])

        def quantize_a(span, jg):
            quantize(("a", span, jg), held["gained", span, jg][:], SPANS[span][1] * P)

        def v_pass(jg, g, t, number, start, stop):
            e_codes, e_cols = (("e", 0), block(4 * g, 4)) if g < 2 else (("e", g), block(0, 4))
            mx(bank(number, ("v", jg, t), [P, WIDE])[:], ("w", jg, g), block(t), e_codes, e_cols, start, stop)

        def v_bank(jg, t, number):
            for g in range(PASSES):
                v_pass(jg, g, t, number, g == 0, g == PASSES - 1)

        def load_gain(jg, slots=range(SLOTS)):
            planes = tile("v_planes", ("v_planes", jg), [P, SLOTS, WIDE], BF16)
            for t in slots:
                nc.scalar.activation(out=planes[:, t, :], in_=held["v", jg, t][:], func=ACT.Copy, scale=loading_col[:, jg, t : t + 1])

        def interleave_v(jg, tag, lo=0, hi=WIDE):
            out = tile(tag, ("grouped", "v", jg, lo), [P, SLOTS * (hi - lo)], BF16)
            interleave_rows(out[:], held["v_planes", jg][:, :, lo:hi])

        def quantize_v(jg, lo=0, hi=WIDE):
            quantize(("v", jg), held["grouped", "v", jg, lo][:], WIDE, lo, hi)

        def a_operand(i, jg, count):
            span = max(n for n in range(len(SPANS)) if SPANS[n][0] <= i)
            return ("a", span, jg), block(i - SPANS[span][0], count)

        def q_mean(piece, number):
            first, count = PIECES[piece]
            out = bank(number, ("q_mean", piece), [P, count, LATENT])
            for i in range(count):
                for jg in range(GROUPS):
                    mx(out[:, i, :], *a_operand(first + i, jg, 1), ("v", jg), slice(0, LATENT), jg == 0, jg == GROUPS - 1)

        def add_mean_bias(piece):
            bias = mean_bias[:].unsqueeze(1).to_broadcast([P, PIECES[piece][1], LATENT])
            nc.vector.tensor_tensor(out=result("mu", piece), in0=held["q_mean", piece][:], in1=bias, op=ALU.add)

        def q_logvar(piece, number):
            first, count = PIECES[piece]
            out = bank(number, ("q_logvar", piece), [P, 2, count * P])
            for h in range(2):
                for jg in range(GROUPS):
                    mx(out[:, h, :], ("v", jg), block(2 + h), *a_operand(first, jg, count), jg == 0, jg == GROUPS - 1)

        def tanh(piece):
            out = tile("tanh", ("tanh", piece), [P, 2, PIECES[piece][1] * P], F32)
            for h in range(2):
                bias = vector_cols[:, 6 + h, SLOTS : SLOTS + 1]
                nc.scalar.activation(out=out[:, h, :], in_=held["q_logvar", piece][:, h, :], func=ACT.Tanh, bias=bias)

        def turn_back(piece, number):
            count = PIECES[piece][1]
            out = bank(number, ("turned_back", piece), [P, count, LATENT])
            for i in range(count):
                for h in range(2):
                    nc.tensor.transpose(out[:, i, block(h)], held["tanh", piece][:, h, block(i)], ident[:])

        def exp(piece):
            nc.scalar.activation(out=result("sd", piece), in_=held["turned_back", piece][:], func=ACT.Exp, scale=0.5)

        def spread(piece):
            nc.vector.tensor_tensor(out=result("z", piece), in0=result("sd", piece), in1=held["noise"][:, tiles_of(piece), :], op=ALU.mult)

        def shift(piece):
            nc.vector.tensor_tensor(out=result("z", piece), in0=result("z", piece), in1=result("mu", piece), op=ALU.add)

        on_scalar, on_vector = nc.scalar.copy, nc.vector.tensor_copy
        low, high = range(0, 2), range(2, 4)

        warm = sb.tile([P, 2], F32, name="warm")
        nc.vector.memset(warm[:], 0.0)
        nc.scalar.activation(out=warm[:, 1:2], in_=warm[:, 0:1], func=ACT.Silu)

        nc.sync.dma_start(out=factor_col[:], in_=cell_factor.rearrange("(p i) -> p i", i=TILES))
        load_x(0, 2, 0, 1)
        load_x(0, 2, 1, 2)
        nc.sync.dma_start(out=gene_scale, in_=x_scale.rearrange("o (g p t) -> p (o g) t", p=P, t=SLOTS))
        load_x(0, 2, 2, 4)
        load_x(2, 1)
        load_x(3, 1)
        load_w(0)
        load_vectors()
        for g in range(1, PASSES):
            load_w(g)
        load_x(4, 2)
        for g in low:
            load_e(g)
        load_x(6, 2)
        for g in high:
            load_e(g)
        nc.sync.dma_start(out=mean_bias[:], in_=latent_bias[0:LATENT].partition_broadcast(P))

        widen(0, on_scalar, 0, 1)
        widen(1, on_vector, 0, 1)
        spread_factor = bank(4, "factor", [P, CELLS], BF16)
        for i in range(TILES):
            nc.tensor.matmul(spread_factor[:, block(i)], lhsT=factor_col[:, i : i + 1].to_broadcast([P, P]), rhs=ident_bf[:], start=True, stop=True)
        on_vector(out=factor_row[:], in_=spread_factor[:])
        widen(0, on_scalar, 1, 2)
        widen(1, on_vector, 1, 2)
        for i in range(2):
            widen(i, on_scalar, 2, 4)
        for i in (2, 3):
            widen(i, on_scalar)
        for pair in range(2):
            for g in range(PASSES):
                turn_x(pair, g, 4 * pair + g)
                scale_x(pair, g)
        interleave_w(0, 0, "gate_c", gpsimd_move)
        interleave_w(1, 0, "ring", on_scalar)
        on_scalar(out=slot_rows[:].rearrange("p t (c i) -> p t c i", i=4), in_=vector_rows[:].rearrange("p (c t i) -> p t c i", t=SLOTS, i=4))
        vectors = bank(0, "vectors", [P, SLOTS + 1, VECTOR_ROWS])
        for t in range(SLOTS + 1):
            rows = slot_rows[:, t, :] if t < SLOTS else vector_rows[:, 0:P]
            nc.tensor.matmul(vectors[:, t, :], lhsT=rows, rhs=ident_bf[:, 0:VECTOR_ROWS], start=True, stop=True)
        interleave_w(0, 1, "gate_a", gpsimd_move, hi=W_SPLIT)
        interleave_w(1, 1, "ring", on_scalar)
        on_scalar(out=vector_cols[:, :, 0 : SLOTS + 1], in_=vectors[:].rearrange("p t r -> p r t"))
        interleave_w_on_tensor(1, 2, (1, 2))
        for g in (2, 3):
            interleave_w(0, g, "ring", on_scalar)
        empty_moved(1, 2, "gate_b")

        for g in range(PASSES):
            if g == 1:
                interleave_w(0, 1, "gate_a", on_vector, lo=W_SPLIT)
            quantize_x(0, g)
            quantize_w(0, g)
            u_pass(0, g, 4)
        interleave_w(1, 3, "gate_d", on_scalar)
        for lo in (0, 2):
            for i in (4, 5):
                widen(i, on_scalar, lo, lo + 2)
        for g in range(PASSES):
            quantize_w(1, g)
        for i in (6, 7):
            widen(i, on_scalar)

        interleave_e_pair("gate_d")
        u_pass(1, 0, 0)
        u_pass(1, 1, 0, low)
        for t in range(SLOTS):
            factor(0, 0, t)
        silu(0, 0)
        for g in low:
            turn_x(2, g, 4 + g)
        u_pass(1, 1, 0, high)
        u_pass(1, 2, 0, low)
        for g in high:
            turn_x(2, g, 4 + g)
        u_pass(1, 2, 0, high)
        u_pass(1, 3, 0)
        for g in range(PASSES):
            scale_x(2, g, ("gate_b", "gate_a")[g // 2])
        for half in range(2):
            quantize_x(2, half)
        interleave_e(2, "ring")
        interleave_e(3, "gate_c")
        for g in low:
            turn_x(3, g, 4 + g)
        for b in range(2):
            u_bank(1, 0, b, 6 + b)

        gain_on_gpsimd(0, 0, "gate_a", CELLS_ON_GPSIMD)
        for t in range(SLOTS):
            factor(0, 1, t)
        silu(0, 1)
        for b in range(2):
            u_bank(1, 1, b, b)
        for g in high:
            turn_x(3, g, g)
        for b in range(2):
            factor(1, 0, b)
        silu(1, 0)
        nc.sync.dma_start(out=tile("big", "noise", [P, TILES, LATENT], BF16)[:], in_=by_tile(noise))
        order = (2, 0, 1, 3)
        quantize_e(2)
        quantize_e_pair()
        quantize_e(3)
        for g in order:
            for t in low:
                v_pass(0, g, t, 6 + t, g == order[0], g == order[-1])

        gain_on_gpsimd(0, 1, "gate_c", 4 * P)
        gain_on_scalar(0, 0, CELLS_ON_GPSIMD)
        for b in range(2):
            factor(1, 1, b)
        silu(1, 1)
        for t in high:
            v_bank(0, t, t - 2)
        for g in range(PASSES):
            scale_x(3, g, "gate_d")
        load_gain(0, low)
        interleave_a(0, 0, CELLS_ON_GPSIMD)
        load_gain(0, range(2, 3))
        gain_on_scalar(1, 0, PAIR_CELLS_ON_VECTOR)
        load_gain(0, range(3, 4))
        interleave_a(1, 0, PAIR_CELLS_ON_VECTOR)
        for t in range(SLOTS):
            v_bank(1, t, 4 + t)
        gain_on_vector(1, 1)
        quantize_x(3, 0)
        interleave_v(0, "ring")
        for b in range(2):
            u_bank(2, 0, b, 2 + b)
        load_gain(1)
        interleave_v(1, "ring", lo=LATENT)
        interleave_v(1, "gate_d", hi=LATENT)
        gain_on_vector(1, 0, PAIR_CELLS_ON_VECTOR)
        for jg in range(GROUPS):
            quantize_a(0, jg)
        quantize_v(0)
        factor(2, 0, 0)
        factor(2, 0, 1)
        quantize_v(1, lo=LATENT)
        for jg in (1, 0):
            quantize_a(1, jg)
        u_bank(2, 1, 0, 1)
        u_slot(2, 1, 2, 5)
        q_logvar(0, 4)
        u_slot(2, 1, 3, 6)
        silu(2, 0)
        factor(2, 1, 0)
        quantize_v(1, hi=LATENT)

        gain_on_gpsimd(2, 0, "gate_d", 2 * P)
        for t in high:
            factor_slot(2, 1, t)
        tanh(0)
        silu(2, 1)
        q_mean(0, 7)
        q_logvar(1, 1)
        q_mean(1, 3)
        turn_back(0, 2)
        tanh(1)
        exp(0)
        q_logvar(2, 6)
        turn_back(1, 4)
        q_mean(2, 0)
        exp(1)
        for piece in range(2):
            add_mean_bias(piece)
            store("mu", piece)
        gain_on_vector(2, 1)
        for jg in (0, 1):
            quantize_a(2, jg)
        add_mean_bias(2)
        store("mu", 2)
        tanh(2)
        store("sd", 0)
        for piece, number in ((3, 7), (4, 5)):
            q_logvar(piece, number)
        for piece, number in ((3, 3), (4, 1)):
            q_mean(piece, number)
        for piece in (3, 4):
            tanh(piece)
        for piece, number in ((2, 2), (3, 4), (4, 6)):
            turn_back(piece, number)
            exp(piece)
        for step in (spread, shift):
            for piece in range(2):
                step(piece)
        for piece in (3, 4):
            add_mean_bias(piece)
        store("sd", 1)
        store("z", 0)
        store("z", 1)
        store("sd", 2)
        store("mu", 3, 4)
        store("sd", 3, 4)
        for step in (spread, shift):
            for piece in (2, 3, 4):
                step(piece)
        for piece in (2, 3, 4):
            store("z", piece)
